import numpy as np
import ml_dtypes


def mxq(x, axis, fmt="e4m3"):
    dtype, down = {"e4m3": (ml_dtypes.float8_e4m3fn, 7), "e5m2": (ml_dtypes.float8_e5m2, 14)}[fmt]
    v = np.moveaxis(np.asarray(x, np.float32).astype(ml_dtypes.bfloat16).astype(np.float64), axis, -1)
    blocks = v.reshape(v.shape[:-1] + (-1, 32))
    amax = np.abs(blocks).max(-1, keepdims=True)
    byte = np.maximum(np.where(amax > 0, np.frexp(amax)[1] - 1 + 127, 0) - down, 1)
    scale = np.exp2(byte - 127.0)
    codes = (blocks / scale).astype(np.float32).astype(dtype).astype(np.float64)
    return np.moveaxis((codes * scale).reshape(v.shape), -1, axis)


WIDE = False


def mx_kscale(k):
    if not WIDE:
        return np.ones(k)
    levels = np.array([10, -10, 5, -5, 0])
    if k % 512:
        return np.exp2(np.random.permutation(np.resize(levels, k // 32))).repeat(32)
    a = np.empty((k // 512, 16))
    for p in range(k // 512):
        a[p, :8] = np.random.permutation(np.resize(levels, 8))
        for g in range(8):
            far = levels[np.abs(levels - a[p, g]) >= 10]
            a[p, g + 8] = far[np.random.randint(len(far))]
    return np.exp2(a.ravel()).repeat(32)


BF16 = ml_dtypes.bfloat16


def bf(x):
    return np.asarray(x, np.float32).astype(BF16)


def f64(x):
    return np.asarray(x).astype(np.float64)


E2M1 = np.array([0.0, 0.5, 1.0, 1.5, 2.0, 3.0, 4.0, 6.0, -0.0, -0.5, -1.0, -1.5, -2.0, -3.0, -4.0, -6.0])


def pack_weight(w, fmt):
    k, n = w.shape
    w = f64(bf(w)).reshape(k // 32, 32, n)
    amax = np.abs(w).max(1)
    if fmt == "e4m3":
        byte = np.frexp(amax)[1] - 1 + 127 - 7
    else:
        mant, ex = np.frexp(amax / 6.0)
        byte = np.where(mant > 0.5, ex, ex - 1) + 127
    byte = np.clip(np.where(amax > 0, byte, 1), 1, 254)
    scaled = (w * np.exp2(127.0 - byte)[:, None, :]).reshape(k, n).astype(np.float32)
    by_word = np.ascontiguousarray(scaled.reshape(k // 512, 128, 4, n).transpose(0, 1, 3, 2))
    if fmt == "e4m3":
        words = by_word.astype(ml_dtypes.float8_e4m3fn).view(np.uint8)
    else:
        c = by_word.astype(ml_dtypes.float4_e2m1fn).view(np.uint8) & 0xF
        words = c[..., 0::2] | (c[..., 1::2] << 4)
    return np.ascontiguousarray(words), np.ascontiguousarray(byte.astype(np.uint8).reshape(k // 512, 16, n))


def unpack_weight(words, scales, fmt):
    g, p, n, _ = words.shape
    if fmt == "e4m3":
        vals = np.ascontiguousarray(words).view(ml_dtypes.float8_e4m3fn).astype(np.float64)
    else:
        nib = np.empty((g, p, n, 4), np.uint8)
        nib[..., 0::2] = words & 0xF
        nib[..., 1::2] = words >> 4
        vals = E2M1[nib]
    vals = vals * np.repeat(np.exp2(scales.astype(np.float64) - 127.0), 8, axis=1)[..., None]
    return vals.transpose(0, 1, 3, 2).reshape(g * 512, n)
def pack4(w):
    words, scales = pack_weight(w, "e2m1")
    return words.reshape(words.shape[0], 128, -1), scales


def unpack4(words, scales):
    return unpack_weight(words.reshape(words.shape[0], 128, -1, 2), scales, "e2m1")


T, H, C, R, D = 2048, 512, 1536, 512, 2560


def draw0():
    s = mx_kscale(H)
    r = mx_kscale(C)
    t = mx_kscale(T)
    b_rest = np.random.standard_normal((C, R)) / np.sqrt(H + C) / r[:, None]
    b_rest_words, b_rest_scales = pack4(b_rest)
    x = np.random.standard_normal((T, D)) / np.sqrt(T) / t[:, None]
    x_words, x_scales = pack4(x)
    return {"dy_hot": bf(2 * np.random.standard_normal((T, H)) * s),
            "b_hot": bf(np.random.standard_normal((H, R)) / np.sqrt(H + C) / s[:, None]),
            "dy_rest": bf(np.random.standard_normal((T, C)) * r),
            "b_rest_words": b_rest_words,
            "b_rest_scales": b_rest_scales,
            "lam": bf(1 + 0.1 * np.random.standard_normal(R)),
            "token_w": bf(np.random.uniform(0.5, 1.5, T) * t),
            "x_words": x_words,
            "x_scales": x_scales}


def core(dy_hot, b_hot, dy_rest, b_rest_words, b_rest_scales, lam, token_w, x_words, x_scales):
    hot = mxq(f64(dy_hot), 1, "e4m3") @ mxq(f64(b_hot), 0, "e4m3")
    rest = mxq(f64(dy_rest), 1, "e4m3") @ unpack4(b_rest_words, b_rest_scales)
    g = (hot + rest) * f64(lam) * f64(token_w)[:, None]
    x = unpack4(x_words, x_scales)
    da = x.T @ mxq(g, 0, "e4m3")
    return da


def e4m3fn_bytes(y):
    return np.clip(np.asarray(y, np.float64), -448.0, 448.0).astype(np.float32).astype(ml_dtypes.float8_e4m3fn).view(np.uint8)


def e4m3fn_values(b):
    return np.asarray(b, np.uint8).view(ml_dtypes.float8_e4m3fn).astype(np.float64)


def setup_inputs():
    d = draw0()
    x0 = np.asarray(d['dy_rest']).astype(np.float64)
    s = (np.max(np.abs(x0), axis=(0,), keepdims=True) / 448.0).astype(np.float32)
    out = {}
    for k, v in d.items():
        if k == 'dy_rest':
            out['dy_rest_bytes'] = e4m3fn_bytes(x0 / s.astype(np.float64))
            out['dy_rest_scale'] = s
        else:
            out[k] = v
    return out


def reference(dy_hot, b_hot, dy_rest_bytes, dy_rest_scale, b_rest_words, b_rest_scales, lam, token_w, x_words, x_scales):
    return core(dy_hot, b_hot, e4m3fn_values(dy_rest_bytes) * dy_rest_scale.astype(np.float64), b_rest_words, b_rest_scales, lam, token_w, x_words, x_scales)

@@ -1,0 +1,284 @@
+from contextlib import ExitStack
+
+import concourse.mybir as mybir
+from concourse.masks import make_identity
+
+T, H, C, R, D = 2048, 512, 1536, 512, 2560
+FLOPS = 2 * T * (H + C) * R + 2 * D * T * R
+
+F32 = mybir.dt.float32
+BF16 = mybir.dt.bfloat16
+I32 = mybir.dt.int32
+U32 = mybir.dt.uint32
+U8 = mybir.dt.uint8
+FP8 = mybir.dt.float8_e4m3fn
+FP8X4 = mybir.dt.float8_e4m3fn_x4
+FP4X4 = mybir.dt.float4_e2m1fn_x4
+MULT = mybir.AluOpType.mult
+ADD = mybir.AluOpType.add
+COPY = mybir.ActivationFunctionType.Copy
+
+P = 128
+PACK = 4
+K_PASS = P * PACK
+GROUPS = T // K_PASS
+PHASES = PACK
+TILES = GROUPS * PHASES
+REST = C // K_PASS
+OUT_TILES = D // P
+OPEN = 4
+SHORT = 12
+GPSIMD_WIDTH = 64
+
+
+def tile_lora_down_gradient_s3_kernel(
+    tc, dy_hot, b_hot, dy_rest_bytes, dy_rest_scale, b_rest_words, b_rest_scales, lam, token_w, x_words, x_scales, out
+):
+    nc = tc.nc
+
+    with ExitStack() as ctx:
+        keep = ctx.enter_context(tc.tile_pool(name="keep", bufs=1))
+        work = ctx.enter_context(tc.tile_pool(name="work", bufs=3))
+        psum = ctx.enter_context(tc.psum_pool(name="psum", bufs=2))
+        ctx.enter_context(tc.manual_schedule())
+
+        ident = keep.tile([P, P], F32, name="ident")
+        token_weight_bf = keep.tile([P, GROUPS, PHASES], BF16, name="token_weight_bf", align_bytes=64)
+        token_weight = keep.tile([P, GROUPS, PHASES], F32, name="token_weight", align_bytes=64)
+        lam_bf = keep.tile([P, PACK], BF16, name="lam_bf", align_bytes=64)
+        lam_col = keep.tile([P, PACK], F32, name="lam_col", align_bytes=64)
+        lam_all = keep.tile([P, R], F32, name="lam_all", align_bytes=64)
+        channel_scale = keep.tile([P, REST, PACK], F32, name="channel_scale", align_bytes=64)
+        b_raw = keep.tile([P, PACK, R], BF16, name="b_raw", align_bytes=64)
+        b_grouped = keep.tile([P, R, PACK], BF16, name="b_grouped", align_bytes=64)
+        b_hot_codes = keep.tile([P, R], U32, name="b_hot_codes", align_bytes=64)
+        b_hot_scales = keep.tile([P, R], U8, name="b_hot_scales", align_bytes=64)
+        b_words_sb = keep.tile([P, REST, 2 * R], U8, name="b_words_sb", align_bytes=64)
+        b_scales_sb = keep.tile([P, REST, R], U8, name="b_scales_sb", align_bytes=64)
+        x_words_sb = keep.tile([P, GROUPS, 2 * D], U8, name="x_words_sb", align_bytes=64)
+        x_scales_sb = keep.tile([P, GROUPS, D], U8, name="x_scales_sb", align_bytes=64)
+        g_codes = keep.tile([P, GROUPS, R], U32, name="g_codes", align_bytes=64)
+        g_scales = keep.tile([P, GROUPS, R], U8, name="g_scales", align_bytes=64)
+        rest_bytes = [keep.tile([P, PHASES, C], U8, name="rest_bytes_%d" % g, align_bytes=64) for g in range(GROUPS)]
+        hot = [keep.tile([P, PHASES, H], BF16, name="hot_%d" % g, align_bytes=64) for g in range(GROUPS)]
+        result = [keep.tile([P, R], F32, name="result_%d" % d, align_bytes=64) for d in range(OUT_TILES)]
+
+        nc.vector.memset(b_scales_sb[:].rearrange("p g n -> p (g n)").bitcast(I32), 0)
+        nc.vector.memset(x_scales_sb[:].rearrange("p g n -> p (g n)").bitcast(I32), 0)
+        make_identity(nc, ident[:])
+
+        bytes_hbm = dy_rest_bytes.rearrange("(g m t) k -> g m t k", m=P, t=PHASES)
+        hot_hbm = dy_hot.rearrange("(g m t) k -> g m t k", m=P, t=PHASES)
+
+        def load_bytes(g, t0, t1):
+            nc.sync.dma_start(out=rest_bytes[g][:, t0:t1, :], in_=bytes_hbm[g][:, t0:t1, :])
+
+        def load_hot(g, t0, t1):
+            nc.sync.dma_start(out=hot[g][:, t0:t1, :], in_=hot_hbm[g][:, t0:t1, :])
+
+        def load_scale_rows(tile, hbm):
+            for q in range(4):
+                nc.sync.dma_start(
+                    out=tile[32 * q : 32 * q + 4, :, :].bitcast(I32),
+                    in_=hbm[:, 4 * q : 4 * q + 4, :].rearrange("g q n -> q g n").bitcast(I32),
+                )
+
+        load_bytes(0, 0, 1)
+        nc.scalar.dma_start(out=channel_scale[:], in_=dy_rest_scale.rearrange("o (c p t) -> p (o c) t", p=P, t=PACK))
+        load_hot(0, 0, 2)
+        load_bytes(0, 1, 2)
+        nc.scalar.dma_start(out=lam_bf[:], in_=lam.rearrange("(p i) -> p i", i=PACK))
+        load_bytes(0, 2, 4)
+        nc.scalar.dma_start(out=token_weight_bf[:], in_=token_w.rearrange("(g m t) -> m g t", m=P, t=PHASES))
+        nc.sync.dma_start(out=b_raw[:], in_=b_hot.rearrange("(p t) n -> p t n", t=PACK))
+        load_hot(0, 2, 4)
+        nc.sync.dma_start(out=b_words_sb[:].bitcast(I32), in_=b_rest_words.rearrange("g p b -> p g b").bitcast(I32))
+        load_scale_rows(b_scales_sb, b_rest_scales)
+        for g in range(1, GROUPS):
+            load_bytes(g, 0, 2)
+            load_hot(g, 0, 4)
+            load_bytes(g, 2, 4)
+        load_scale_rows(x_scales_sb, x_scales)
+        for g in range(GROUPS):
+            nc.sync.dma_start(out=x_words_sb[:, g, :].bitcast(I32), in_=x_words[g].bitcast(I32))
+
+        def spread_lam():
+            nc.scalar.copy(out=lam_col[:], in_=lam_bf[:])
+            nc.scalar.copy(out=token_weight[:], in_=token_weight_bf[:])
+            bank = psum.tile([P, PACK, P], F32, name="lam_bank", tag="out_bank")
+            for i in range(PACK):
+                nc.tensor.transpose(bank[:, i, :], lam_col[:, i : i + 1].to_broadcast([P, P]), ident[:])
+            nc.scalar.copy(out=lam_all[:].rearrange("p (n i) -> p n i", i=PACK), in_=bank[:].rearrange("p i n -> p n i"))
+
+        def interleave_b_hot():
+            nc.gpsimd.tensor_scalar(
+                out=b_grouped[:],
+                in0=b_raw[:].rearrange("p t n -> p n t"),
+                scalar1=1.0,
+                scalar2=0.0,
+                op0=MULT,
+                op1=ADD,
+            )
+
+        def quantise_b_hot():
+            nc.vector.quantize_mx(
+                out=b_hot_codes[:].bitcast(FP8X4),
+                scales=b_hot_scales[:],
+                in_=b_grouped[:].rearrange("p n t -> p (n t)"),
+            )
+
+        widened = {}
+        banks = {}
+        grouped = {}
+        dy_codes = {}
+        dy_code_scales = {}
+        sums = {}
+        weighted = {}
+
+        def widen(s):
+            g, t = divmod(s, PHASES)
+            widened[s] = work.tile([P, C], BF16, name="widened", align_bytes=64, bufs=4)
+            nc.scalar.copy(out=widened[s][:], in_=rest_bytes[g][:, t, :].bitcast(FP8))
+
+        def turn(s):
+            g, t = divmod(s, PHASES)
+            rest_words = widened[s][:].bitcast(F32)
+            hot_words = hot[g][:, t, :].bitcast(F32)
+            banks[s] = [psum.tile([P, 2, 2, P], F32, name="turned", tag="turned", bufs=4) for h in range(2)]
+            for c in range(REST + 1):
+                words = hot_words if c == REST else rest_words[:, 256 * c : 256 * (c + 1)]
+                for u in range(2):
+                    nc.tensor.transpose(banks[s][c // 2][:, c % 2, u, :], words[:, u:256:2], ident[:])
+            grouped[s] = work.tile([P, REST + 1, P, PACK], BF16, name="grouped", align_bytes=64, bufs=5)
+            nc.scalar.copy(
+                out=grouped[s][:, REST, :, :].bitcast(F32),
+                in_=banks[s][1][:, 1, :, :].rearrange("p u n -> p n u"),
+            )
+
+        def product(s):
+            for c in range(REST):
+                nc.vector.tensor_tensor(
+                    out=grouped[s][:, c, :, :].rearrange("p n (u e) -> p n u e", u=2),
+                    in0=banks[s][c // 2][:, c % 2, :, :].bitcast(BF16).rearrange("p u (n e) -> p n u e", e=2),
+                    in1=channel_scale[:, c, :].unsqueeze(1).to_broadcast([P, P, PACK]).rearrange("p n (u e) -> p n u e", u=2),
+                    op=MULT,
+                )
+
+        def quantise_dy(s):
+            dy_codes[s] = work.tile([P, REST + 1, P], U32, name="dy_codes", align_bytes=64)
+            dy_code_scales[s] = work.tile([P, REST + 1, P], U8, name="dy_code_scales", align_bytes=64)
+            nc.vector.quantize_mx(
+                out=dy_codes[s][:].rearrange("p c n -> p (c n)").bitcast(FP8X4),
+                scales=dy_code_scales[s][:].rearrange("p c n -> p (c n)"),
+                in_=grouped[s][:].rearrange("p c n t -> p (c n t)"),
+            )
+
+        def stage1(s):
+            g, t = divmod(s, PHASES)
+            bank = psum.tile([P, R], F32, name="acc", tag="acc")
+            for c in range(REST + 1):
+                is_hot = c == REST
+                nc.tensor.matmul_mx(
+                    out=bank[:],
+                    lhsT=dy_codes[s][:, c, :].bitcast(FP8X4),
+                    lhsT_scale=dy_code_scales[s][:, c, :],
+                    rhs=b_hot_codes[:].bitcast(FP8X4) if is_hot else b_words_sb[:, c, :].bitcast(FP4X4),
+                    rhs_scale=b_hot_scales[:] if is_hot else b_scales_sb[:, c, :],
+                    start=(c == 0),
+                    stop=is_hot,
+                )
+            if t == 0:
+                sums[g] = work.tile([P, PHASES, R], F32, name="sums", align_bytes=64, bufs=2)
+            nc.scalar.activation(out=sums[g][:, t, :], in_=bank[:], func=COPY, scale=token_weight[:, g, t : t + 1])
+
+        def weigh(g, engine, width):
+            weighted[g] = work.tile([P, R, PHASES], BF16, name="weighted", align_bytes=64, bufs=2)
+            for r0 in range(0, R, width):
+                cols = slice(r0, r0 + width)
+                engine.tensor_tensor(
+                    out=weighted[g][:, cols, :],
+                    in0=sums[g][:, :, cols].rearrange("p t r -> p r t"),
+                    in1=lam_all[:, cols].unsqueeze(2).to_broadcast([P, width, PHASES]),
+                    op=MULT,
+                )
+
+        def quantise_g(g, width):
+            for r0 in range(0, R, width):
+                cols = slice(r0, r0 + width)
+                nc.vector.quantize_mx(
+                    out=g_codes[:, g, cols].bitcast(FP8X4),
+                    scales=g_scales[:, g, cols],
+                    in_=weighted[g][:, cols, :].rearrange("p r t -> p (r t)"),
+                )
+
+        def stage2(bank, d, groups, first, last):
+            for g in groups:
+                nc.tensor.matmul_mx(
+                    out=bank[:],
+                    lhsT=x_words_sb[:, g, 2 * P * d : 2 * P * (d + 1)].bitcast(FP4X4),
+                    lhsT_scale=x_scales_sb[:, g, P * d : P * (d + 1)],
+                    rhs=g_codes[:, g, :].bitcast(FP8X4),
+                    rhs_scale=g_scales[:, g, :],
+                    start=(g == first),
+                    stop=(g == last),
+                )
+
+        def early_groups(d):
+            return 1 if d < OPEN + SHORT else 2
+
+        def early_part(d):
+            bank = psum.tile([P, R], F32, name="early", tag="out_bank")
+            stage2(bank, d, range(early_groups(d)), 0, early_groups(d) - 1)
+            nc.scalar.copy(out=result[d][:], in_=bank[:])
+
+        def store(d):
+            nc.sync.dma_start(out=out[P * d : P * (d + 1), :], in_=result[d][:])
+
+        widen(0)
+        widen(1)
+        first_early, last_step = 8, TILES + 1
+        done = OPEN
+        for n in range(TILES + 2):
+            if n % 2 == 0 and n < TILES:
+                for s in (n, n + 1):
+                    turn(s)
+                    if s + 2 < TILES:
+                        widen(s + 2)
+            if n == 0:
+                spread_lam()
+            if n < TILES:
+                product(n)
+            if n == 0:
+                interleave_b_hot()
+            if 1 <= n <= TILES:
+                quantise_dy(n - 1)
+            if n == 2:
+                quantise_b_hot()
+            if n >= 2:
+                stage1(n - 2)
+            if n % PHASES == 1 and 5 <= n < TILES:
+                weigh(n // PHASES - 1, nc.gpsimd, GPSIMD_WIDTH)
+            if n % PHASES == 0 and 8 <= n <= TILES:
+                quantise_g(n // PHASES - 2, R)
+            while done - OPEN < (n + 1 - first_early) * (OUT_TILES - OPEN) // (last_step + 1 - first_early):
+                early_part(done)
+                done += 1
+
+        weigh(GROUPS - 1, nc.vector, P)
+        quantise_g(GROUPS - 1, P)
+
+        waiting = []
+        for d in range(OPEN):
+            bank = psum.tile([P, R], F32, name="waiting_bank", tag="turned", bufs=4)
+            stage2(bank, d, range(GROUPS - 1), 0, GROUPS - 1)
+            waiting.append(bank)
+        for i in range(OUT_TILES - OPEN):
+            if i < OPEN:
+                stage2(waiting[i], i, (GROUPS - 1,), 0, GROUPS - 1)
+                nc.scalar.copy(out=result[i][:], in_=waiting[i][:])
+                store(i)
+            d = OPEN + i
+            bank = psum.tile([P, R], F32, name="late", tag=("acc", "out_bank")[i % 2])
+            stage2(bank, d, range(early_groups(d), GROUPS), early_groups(d), GROUPS - 1)
+            nc.vector.tensor_tensor(out=result[d][:], in0=bank[:], in1=result[d][:], op=ADD)
+            store(d)

@@ -25,10 +25,11 @@ GROUPS = T // K_PASS
 PHASES = PACK
 TILES = GROUPS * PHASES
 REST = C // K_PASS
+PASSES = REST + 1
+PAIRS = TILES // 2
 OUT_TILES = D // P
-OPEN = 4
-SHORT = 12
-GPSIMD_WIDTH = 64
+HELD = 4
+HALF = R // 2
 
 
 def tile_lora_down_gradient_s3_kernel(
@@ -39,42 +40,50 @@ def tile_lora_down_gradient_s3_kernel(
     with ExitStack() as ctx:
         keep = ctx.enter_context(tc.tile_pool(name="keep", bufs=1))
         work = ctx.enter_context(tc.tile_pool(name="work", bufs=3))
-        psum = ctx.enter_context(tc.psum_pool(name="psum", bufs=2))
+        psum = ctx.enter_context(tc.psum_pool(name="psum", bufs=4))
         ctx.enter_context(tc.manual_schedule())
 
         ident = keep.tile([P, P], F32, name="ident")
-        token_weight_bf = keep.tile([P, GROUPS, PHASES], BF16, name="token_weight_bf", align_bytes=64)
-        token_weight = keep.tile([P, GROUPS, PHASES], F32, name="token_weight", align_bytes=64)
-        lam_bf = keep.tile([P, PACK], BF16, name="lam_bf", align_bytes=64)
-        lam_col = keep.tile([P, PACK], F32, name="lam_col", align_bytes=64)
-        lam_all = keep.tile([P, R], F32, name="lam_all", align_bytes=64)
-        channel_scale = keep.tile([P, REST, PACK], F32, name="channel_scale", align_bytes=64)
+        token_weight_bf = keep.tile([P, TILES], BF16, name="token_weight_bf", align_bytes=64)
+        token_weight = keep.tile([P, TILES], F32, name="token_weight", align_bytes=64)
+        lam_all = keep.tile([P, R], BF16, name="lam_all", align_bytes=64)
+        channel_scale = keep.tile([P, PASSES, PACK], F32, name="channel_scale", align_bytes=64)
         b_raw = keep.tile([P, PACK, R], BF16, name="b_raw", align_bytes=64)
-        b_grouped = keep.tile([P, R, PACK], BF16, name="b_grouped", align_bytes=64)
+        b_grouped = keep.tile([P, R * PACK], BF16, name="b_grouped", align_bytes=64)
         b_hot_codes = keep.tile([P, R], U32, name="b_hot_codes", align_bytes=64)
         b_hot_scales = keep.tile([P, R], U8, name="b_hot_scales", align_bytes=64)
         b_words_sb = keep.tile([P, REST, 2 * R], U8, name="b_words_sb", align_bytes=64)
         b_scales_sb = keep.tile([P, REST, R], U8, name="b_scales_sb", align_bytes=64)
-        x_words_sb = keep.tile([P, GROUPS, 2 * D], U8, name="x_words_sb", align_bytes=64)
+        x_words_sb = [keep.tile([P, 2 * D], U8, name="x_words_%d" % g, align_bytes=64) for g in range(GROUPS)]
         x_scales_sb = keep.tile([P, GROUPS, D], U8, name="x_scales_sb", align_bytes=64)
-        g_codes = keep.tile([P, GROUPS, R], U32, name="g_codes", align_bytes=64)
-        g_scales = keep.tile([P, GROUPS, R], U8, name="g_scales", align_bytes=64)
-        rest_bytes = [keep.tile([P, PHASES, C], U8, name="rest_bytes_%d" % g, align_bytes=64) for g in range(GROUPS)]
-        hot = [keep.tile([P, PHASES, H], BF16, name="hot_%d" % g, align_bytes=64) for g in range(GROUPS)]
+        g_codes = [keep.tile([P, R], U32, name="g_codes_%d" % g, align_bytes=64) for g in range(GROUPS)]
+        g_scales = [keep.tile([P, R], U8, name="g_scales_%d" % g, align_bytes=64) for g in range(GROUPS)]
+        last_planes = keep.tile([P, PHASES, R], BF16, name="last_planes", align_bytes=64)
+        last_grouped = keep.tile([P, R * PHASES], BF16, name="last_grouped", align_bytes=64)
         result = [keep.tile([P, R], F32, name="result_%d" % d, align_bytes=64) for d in range(OUT_TILES)]
 
         nc.vector.memset(b_scales_sb[:].rearrange("p g n -> p (g n)").bitcast(I32), 0)
         nc.vector.memset(x_scales_sb[:].rearrange("p g n -> p (g n)").bitcast(I32), 0)
         make_identity(nc, ident[:])
 
-        bytes_hbm = dy_rest_bytes.rearrange("(g m t) k -> g m t k", m=P, t=PHASES)
-        hot_hbm = dy_hot.rearrange("(g m t) k -> g m t k", m=P, t=PHASES)
+        bytes_hbm = dy_rest_bytes.rearrange("(g m t) k -> g m (t k)", m=P, t=PHASES)
+        hot_hbm = dy_hot.rearrange("(g m t) k -> g m (t k)", m=P, t=PHASES)
+        rest_bytes = {}
+        hot = {}
 
-        def load_bytes(g, t0, t1):
-            nc.sync.dma_start(out=rest_bytes[g][:, t0:t1, :], in_=bytes_hbm[g][:, t0:t1, :])
+        def load_bytes(s, count):
+            g, t = divmod(s, PHASES)
+            tile = keep.tile([P, count * C], U8, name="rest_bytes_%d" % s, align_bytes=64)
+            nc.sync.dma_start(out=tile[:], in_=bytes_hbm[g][:, t * C : (t + count) * C])
+            for i in range(count):
+                rest_bytes[s + i] = tile[:, i * C : (i + 1) * C]
 
-        def load_hot(g, t0, t1):
-            nc.sync.dma_start(out=hot[g][:, t0:t1, :], in_=hot_hbm[g][:, t0:t1, :])
+        def load_hot(s, count):
+            g, t = divmod(s, PHASES)
+            tile = keep.tile([P, count * H], BF16, name="hot_%d" % s, align_bytes=64)
+            nc.sync.dma_start(out=tile[:], in_=hot_hbm[g][:, t * H : (t + count) * H])
+            for i in range(count):
+                hot[s + i] = tile[:, i * H : (i + 1) * H]
 
         def load_scale_rows(tile, hbm):
             for q in range(4):
@@ -83,202 +92,218 @@ def tile_lora_down_gradient_s3_kernel(
                     in_=hbm[:, 4 * q : 4 * q + 4, :].rearrange("g q n -> q g n").bitcast(I32),
                 )
 
-        load_bytes(0, 0, 1)
-        nc.scalar.dma_start(out=channel_scale[:], in_=dy_rest_scale.rearrange("o (c p t) -> p (o c) t", p=P, t=PACK))
-        load_hot(0, 0, 2)
-        load_bytes(0, 1, 2)
-        nc.scalar.dma_start(out=lam_bf[:], in_=lam.rearrange("(p i) -> p i", i=PACK))
-        load_bytes(0, 2, 4)
-        nc.scalar.dma_start(out=token_weight_bf[:], in_=token_w.rearrange("(g m t) -> m g t", m=P, t=PHASES))
+        load_bytes(0, 1)
+        load_bytes(1, 1)
+        nc.sync.dma_start(
+            out=channel_scale[:, 0:REST, :], in_=dy_rest_scale.rearrange("o (c p t) -> p (o c) t", p=P, t=PACK)
+        )
+        load_hot(0, 2)
         nc.sync.dma_start(out=b_raw[:], in_=b_hot.rearrange("(p t) n -> p t n", t=PACK))
-        load_hot(0, 2, 4)
+        load_bytes(2, 2)
+        load_hot(2, 2)
         nc.sync.dma_start(out=b_words_sb[:].bitcast(I32), in_=b_rest_words.rearrange("g p b -> p g b").bitcast(I32))
         load_scale_rows(b_scales_sb, b_rest_scales)
-        for g in range(1, GROUPS):
-            load_bytes(g, 0, 2)
-            load_hot(g, 0, 4)
-            load_bytes(g, 2, 4)
+        nc.sync.dma_start(
+            out=token_weight_bf[:].rearrange("m (g t) -> m g t", t=PHASES),
+            in_=token_w.rearrange("(g m t) -> m g t", m=P, t=PHASES),
+        )
+        load_bytes(4, 2)
+        load_hot(4, 4)
+        load_bytes(6, 2)
+        nc.sync.dma_start(out=lam_all[:], in_=lam.partition_broadcast(P))
+        for g in range(2, GROUPS):
+            load_bytes(PHASES * g, 2)
+            load_hot(PHASES * g, 4)
+            load_bytes(PHASES * g + 2, 2)
         load_scale_rows(x_scales_sb, x_scales)
         for g in range(GROUPS):
-            nc.sync.dma_start(out=x_words_sb[:, g, :].bitcast(I32), in_=x_words[g].bitcast(I32))
+            nc.sync.dma_start(out=x_words_sb[g][:].bitcast(I32), in_=x_words[g].bitcast(I32))
 
-        def spread_lam():
-            nc.scalar.copy(out=lam_col[:], in_=lam_bf[:])
-            nc.scalar.copy(out=token_weight[:], in_=token_weight_bf[:])
-            bank = psum.tile([P, PACK, P], F32, name="lam_bank", tag="out_bank")
-            for i in range(PACK):
-                nc.tensor.transpose(bank[:, i, :], lam_col[:, i : i + 1].to_broadcast([P, P]), ident[:])
-            nc.scalar.copy(out=lam_all[:].rearrange("p (n i) -> p n i", i=PACK), in_=bank[:].rearrange("p i n -> p n i"))
-
-        def interleave_b_hot():
-            nc.gpsimd.tensor_scalar(
-                out=b_grouped[:],
-                in0=b_raw[:].rearrange("p t n -> p n t"),
-                scalar1=1.0,
-                scalar2=0.0,
-                op0=MULT,
-                op1=ADD,
-            )
-
-        def quantise_b_hot():
-            nc.vector.quantize_mx(
-                out=b_hot_codes[:].bitcast(FP8X4),
-                scales=b_hot_scales[:],
-                in_=b_grouped[:].rearrange("p n t -> p (n t)"),
-            )
+        nc.vector.tensor_copy(out=channel_scale[:, REST, :], in_=channel_scale[:, 0, :])
 
         widened = {}
         banks = {}
         grouped = {}
         dy_codes = {}
         dy_code_scales = {}
+        acc = {}
         sums = {}
-        weighted = {}
 
-        def widen(s):
-            g, t = divmod(s, PHASES)
+        def widen(s, pieces):
             widened[s] = work.tile([P, C], BF16, name="widened", align_bytes=64, bufs=4)
-            nc.scalar.copy(out=widened[s][:], in_=rest_bytes[g][:, t, :].bitcast(FP8))
+            width = C // pieces
+            for k0 in range(0, C, width):
+                nc.scalar.copy(out=widened[s][:, k0 : k0 + width], in_=rest_bytes[s][:, k0 : k0 + width].bitcast(FP8))
 
-        def turn(s):
-            g, t = divmod(s, PHASES)
-            rest_words = widened[s][:].bitcast(F32)
-            hot_words = hot[g][:, t, :].bitcast(F32)
-            banks[s] = [psum.tile([P, 2, 2, P], F32, name="turned", tag="turned", bufs=4) for h in range(2)]
-            for c in range(REST + 1):
-                words = hot_words if c == REST else rest_words[:, 256 * c : 256 * (c + 1)]
+        def turn_bank(j, words):
+            bank = psum.tile([P, 2, 2, P], F32, name="turned", tag="turned_%d" % j, bufs=1)
+            for c in range(2):
                 for u in range(2):
-                    nc.tensor.transpose(banks[s][c // 2][:, c % 2, u, :], words[:, u:256:2], ident[:])
-            grouped[s] = work.tile([P, REST + 1, P, PACK], BF16, name="grouped", align_bytes=64, bufs=5)
-            nc.scalar.copy(
-                out=grouped[s][:, REST, :, :].bitcast(F32),
-                in_=banks[s][1][:, 1, :, :].rearrange("p u n -> p n u"),
+                    nc.tensor.transpose(bank[:, u, c, :], words[c][:, u : 2 * P : 2], ident[:])
+            return bank
+
+        def turn_hot(m):
+            bank = turn_bank(REST, [hot[2 * m + i].bitcast(F32) for i in range(2)])
+            slots = grouped[m][:].bitcast(F32).rearrange("p (c n u) -> p c n u", n=P, u=2)
+            nc.scalar.copy(out=slots[:, 0 : 2 * PASSES : 2 * PASSES - 1, :, :], in_=bank[:].rearrange("p u c n -> p c n u"))
+
+        def turn(m):
+            grouped[m] = work.tile([P, 2 * PASSES * K_PASS], BF16, name="grouped", align_bytes=64)
+            if m > 0:
+                turn_hot(m)
+            words = [widened[2 * m + i][:, K_PASS * c : K_PASS * (c + 1)].bitcast(F32) for i in range(2) for c in range(REST)]
+            banks[m] = [turn_bank(j, words[2 * j : 2 * j + 2]) for j in range(REST)]
+            if m == 0:
+                turn_hot(m)
+
+        def product(m, j):
+            c0 = 2 * j % REST
+            nc.vector.tensor_tensor(
+                out=grouped[m][:, K_PASS * (2 * j + 1) : K_PASS * (2 * j + 3)].rearrange("p (c n u e) -> p c n u e", c=2, u=2, e=2),
+                in0=banks[m][j][:].rearrange("p u c n -> p (u c n)").bitcast(BF16).rearrange("p (u c n e) -> p c n u e", u=2, c=2, e=2),
+                in1=channel_scale[:, c0 : c0 + 2, :].unsqueeze(2).to_broadcast([P, 2, P, PACK]).rearrange("p c n (u e) -> p c n u e", u=2),
+                op=MULT,
             )
 
-        def product(s):
-            for c in range(REST):
-                nc.vector.tensor_tensor(
-                    out=grouped[s][:, c, :, :].rearrange("p n (u e) -> p n u e", u=2),
-                    in0=banks[s][c // 2][:, c % 2, :, :].bitcast(BF16).rearrange("p u (n e) -> p n u e", e=2),
-                    in1=channel_scale[:, c, :].unsqueeze(1).to_broadcast([P, P, PACK]).rearrange("p n (u e) -> p n u e", u=2),
-                    op=MULT,
-                )
-
         def quantise_dy(s):
-            dy_codes[s] = work.tile([P, REST + 1, P], U32, name="dy_codes", align_bytes=64)
-            dy_code_scales[s] = work.tile([P, REST + 1, P], U8, name="dy_code_scales", align_bytes=64)
+            m, i = divmod(s, 2)
+            dy_codes[s] = work.tile([P, PASSES * P], U32, name="dy_codes", align_bytes=64, bufs=4)
+            dy_code_scales[s] = work.tile([P, PASSES * P], U8, name="dy_code_scales", align_bytes=64, bufs=4)
             nc.vector.quantize_mx(
-                out=dy_codes[s][:].rearrange("p c n -> p (c n)").bitcast(FP8X4),
-                scales=dy_code_scales[s][:].rearrange("p c n -> p (c n)"),
-                in_=grouped[s][:].rearrange("p c n t -> p (c n t)"),
+                out=dy_codes[s][:].bitcast(FP8X4),
+                scales=dy_code_scales[s][:],
+                in_=grouped[m][:, PASSES * K_PASS * i : PASSES * K_PASS * (i + 1)],
             )
 
         def stage1(s):
-            g, t = divmod(s, PHASES)
-            bank = psum.tile([P, R], F32, name="acc", tag="acc")
-            for c in range(REST + 1):
+            acc[s] = psum.tile([P, R], F32, name="acc", tag="sum_bank")
+            first_rest = 1 - s % 2
+            for c in range(PASSES):
                 is_hot = c == REST
+                slot = (first_rest + c) % PASSES
                 nc.tensor.matmul_mx(
-                    out=bank[:],
-                    lhsT=dy_codes[s][:, c, :].bitcast(FP8X4),
-                    lhsT_scale=dy_code_scales[s][:, c, :],
+                    out=acc[s][:],
+                    lhsT=dy_codes[s][:, P * slot : P * (slot + 1)].bitcast(FP8X4),
+                    lhsT_scale=dy_code_scales[s][:, P * slot : P * (slot + 1)],
                     rhs=b_hot_codes[:].bitcast(FP8X4) if is_hot else b_words_sb[:, c, :].bitcast(FP4X4),
                     rhs_scale=b_hot_scales[:] if is_hot else b_scales_sb[:, c, :],
                     start=(c == 0),
                     stop=is_hot,
                 )
+
+        def weigh_tokens(s):
+            g, t = divmod(s, PHASES)
             if t == 0:
                 sums[g] = work.tile([P, PHASES, R], F32, name="sums", align_bytes=64, bufs=2)
-            nc.scalar.activation(out=sums[g][:, t, :], in_=bank[:], func=COPY, scale=token_weight[:, g, t : t + 1])
+            nc.scalar.activation(out=sums[g][:, t, :], in_=acc[s][:], func=COPY, scale=token_weight[:, s : s + 1])
 
-        def weigh(g, engine, width):
-            weighted[g] = work.tile([P, R, PHASES], BF16, name="weighted", align_bytes=64, bufs=2)
-            for r0 in range(0, R, width):
-                cols = slice(r0, r0 + width)
-                engine.tensor_tensor(
-                    out=weighted[g][:, cols, :],
-                    in0=sums[g][:, :, cols].rearrange("p t r -> p r t"),
-                    in1=lam_all[:, cols].unsqueeze(2).to_broadcast([P, width, PHASES]),
-                    op=MULT,
-                )
+        def weigh_ranks(g, h, dst):
+            cols = slice(HALF * h, HALF * (h + 1))
+            nc.gpsimd.tensor_tensor(
+                out=dst.rearrange("p (c i t) -> p c t i", i=4, t=PHASES),
+                in0=sums[g][:, :, cols].rearrange("p t (c i) -> p c t i", i=4),
+                in1=lam_all[:, cols].rearrange("p (c i) -> p c i", i=4).unsqueeze(2).to_broadcast([P, HALF // 4, PHASES, 4]),
+                op=MULT,
+            )
 
-        def quantise_g(g, width):
-            for r0 in range(0, R, width):
-                cols = slice(r0, r0 + width)
-                nc.vector.quantize_mx(
-                    out=g_codes[:, g, cols].bitcast(FP8X4),
-                    scales=g_scales[:, g, cols],
-                    in_=weighted[g][:, cols, :].rearrange("p r t -> p (r t)"),
-                )
+        def quantise_g(g, r0, r1, src):
+            nc.vector.quantize_mx(out=g_codes[g][:, r0:r1].bitcast(FP8X4), scales=g_scales[g][:, r0:r1], in_=src)
 
-        def stage2(bank, d, groups, first, last):
+        def weigh_last(s):
+            nc.vector.scalar_tensor_tensor(
+                out=last_planes[:, s % PHASES, :], in0=acc[s][:], scalar=token_weight[:, s : s + 1], in1=lam_all[:], op0=MULT, op1=MULT
+            )
+
+        def interleave_last(copy, r0, r1):
+            copy(
+                out=last_grouped[:, PHASES * r0 : PHASES * r1].rearrange("p (c i t) -> p c t i", i=4, t=PHASES),
+                in_=last_planes[:, :, r0:r1].rearrange("p t (c i) -> p c t i", i=4),
+            )
+
+        def stage2(bank, d, groups):
             for g in groups:
                 nc.tensor.matmul_mx(
                     out=bank[:],
-                    lhsT=x_words_sb[:, g, 2 * P * d : 2 * P * (d + 1)].bitcast(FP4X4),
+                    lhsT=x_words_sb[g][:, 2 * P * d : 2 * P * (d + 1)].bitcast(FP4X4),
                     lhsT_scale=x_scales_sb[:, g, P * d : P * (d + 1)],
-                    rhs=g_codes[:, g, :].bitcast(FP8X4),
-                    rhs_scale=g_scales[:, g, :],
-                    start=(g == first),
-                    stop=(g == last),
+                    rhs=g_codes[g][:].bitcast(FP8X4),
+                    rhs_scale=g_scales[g][:],
+                    start=(g == 0),
+                    stop=(g == GROUPS - 1),
                 )
 
-        def early_groups(d):
-            return 1 if d < OPEN + SHORT else 2
-
-        def early_part(d):
-            bank = psum.tile([P, R], F32, name="early", tag="out_bank")
-            stage2(bank, d, range(early_groups(d)), 0, early_groups(d) - 1)
-            nc.scalar.copy(out=result[d][:], in_=bank[:])
-
-        def store(d):
+        def store(d, bank, copy):
+            copy(out=result[d][:], in_=bank[:])
             nc.sync.dma_start(out=out[P * d : P * (d + 1), :], in_=result[d][:])
 
-        widen(0)
-        widen(1)
-        first_early, last_step = 8, TILES + 1
-        done = OPEN
-        for n in range(TILES + 2):
-            if n % 2 == 0 and n < TILES:
-                for s in (n, n + 1):
-                    turn(s)
-                    if s + 2 < TILES:
-                        widen(s + 2)
-            if n == 0:
-                spread_lam()
-            if n < TILES:
-                product(n)
-            if n == 0:
-                interleave_b_hot()
-            if 1 <= n <= TILES:
-                quantise_dy(n - 1)
-            if n == 2:
-                quantise_b_hot()
-            if n >= 2:
-                stage1(n - 2)
-            if n % PHASES == 1 and 5 <= n < TILES:
-                weigh(n // PHASES - 1, nc.gpsimd, GPSIMD_WIDTH)
-            if n % PHASES == 0 and 8 <= n <= TILES:
-                quantise_g(n // PHASES - 2, R)
-            while done - OPEN < (n + 1 - first_early) * (OUT_TILES - OPEN) // (last_step + 1 - first_early):
-                early_part(done)
-                done += 1
+        last = GROUPS - 1
+        widen(0, REST)
+        widen(1, REST)
+        turn(0)
+        nc.gpsimd.tensor_scalar(
+            out=b_grouped[:].rearrange("p (n t) -> p n t", t=PACK),
+            in0=b_raw[:].rearrange("p t n -> p n t"),
+            scalar1=1.0,
+            scalar2=0.0,
+            op0=MULT,
+            op1=ADD,
+        )
+        widen(2, 1)
+        widen(3, 1)
+        nc.scalar.copy(out=token_weight[:], in_=token_weight_bf[:])
+        waiting = {}
 
-        weigh(GROUPS - 1, nc.vector, P)
-        quantise_g(GROUPS - 1, P)
+        def hold(d, tag, bufs):
+            waiting[d] = psum.tile([P, R], F32, name="waiting", tag=tag, bufs=bufs)
+            stage2(waiting[d], d, range(last - 1))
 
-        waiting = []
-        for d in range(OPEN):
-            bank = psum.tile([P, R], F32, name="waiting_bank", tag="turned", bufs=4)
-            stage2(bank, d, range(GROUPS - 1), 0, GROUPS - 1)
-            waiting.append(bank)
-        for i in range(OUT_TILES - OPEN):
-            if i < OPEN:
-                stage2(waiting[i], i, (GROUPS - 1,), 0, GROUPS - 1)
-                nc.scalar.copy(out=result[i][:], in_=waiting[i][:])
-                store(i)
-            d = OPEN + i
-            bank = psum.tile([P, R], F32, name="late", tag=("acc", "out_bank")[i % 2])
-            stage2(bank, d, range(early_groups(d), GROUPS), early_groups(d), GROUPS - 1)
-            nc.vector.tensor_tensor(out=result[d][:], in0=bank[:], in1=result[d][:], op=ADD)
-            store(d)
+        for m in range(PAIRS + 1):
+            g, h = divmod(m - 3, 2)
+            if m >= 3:
+                lam_dst = grouped[m - 1][:, PASSES * K_PASS : PASSES * K_PASS + PHASES * HALF]
+                weigh_ranks(g, h, lam_dst)
+            if m < PAIRS:
+                for j in range(REST):
+                    product(m, j)
+            if m + 1 < PAIRS:
+                turn(m + 1)
+            if m + 1 == PAIRS:
+                for j in range(HELD):
+                    hold(j, "turned_%d" % ((j + REST) % PASSES), 1)
+            if m == PAIRS:
+                for s in range(PHASES * last, TILES):
+                    weigh_last(s)
+                    if s % PHASES < 2:
+                        hold(HELD + s % PHASES, "sum_bank", 4)
+            if m == 0:
+                nc.vector.quantize_mx(out=b_hot_codes[:].bitcast(FP8X4), scales=b_hot_scales[:], in_=b_grouped[:])
+            if m < PAIRS:
+                for s in (2 * m, 2 * m + 1):
+                    quantise_dy(s)
+                    stage1(s)
+            if m >= 3:
+                quantise_g(g, HALF * h, HALF * (h + 1), lam_dst)
+            if m < PAIRS:
+                for s in (2 * m, 2 * m + 1):
+                    if s + 4 < TILES:
+                        widen(s + 4, 1)
+                    if s < PHASES * last:
+                        weigh_tokens(s)
+
+        for d in waiting:
+            stage2(waiting[d], d, (last - 1,))
+
+        interleave_last(nc.scalar.copy, 3 * P, R)
+        interleave_last(nc.vector.tensor_copy, 0, HALF)
+        interleave_last(nc.vector.tensor_copy, HALF, 3 * P)
+        quantise_g(last, 0, HALF, last_grouped[:, 0 : PHASES * HALF])
+        quantise_g(last, HALF, R, last_grouped[:, PHASES * HALF :])
+
+        for d in range(OUT_TILES):
+            if d in waiting:
+                bank = waiting[d]
+                stage2(bank, d, (last,))
+            else:
+                bank = psum.tile([P, R], F32, name="late", tag="sum_bank")
+                stage2(bank, d, range(GROUPS))
+            store(d, bank, (nc.scalar.copy, nc.vector.tensor_copy)[d % 2])

@@ -30,6 +30,7 @@ PAIRS = TILES // 2
 OUT_TILES = D // P
 HELD = 4
 HALF = R // 2
+PARKED = {}
 
 
 def tile_lora_down_gradient_s3_kernel(
@@ -76,14 +77,14 @@ def tile_lora_down_gradient_s3_kernel(
             tile = keep.tile([P, count * C], U8, name="rest_bytes_%d" % s, align_bytes=64)
             nc.sync.dma_start(out=tile[:], in_=bytes_hbm[g][:, t * C : (t + count) * C])
             for i in range(count):
-                rest_bytes[s + i] = tile[:, i * C : (i + 1) * C]
+                rest_bytes[s + i] = tile[:, i * C :]
 
         def load_hot(s, count):
             g, t = divmod(s, PHASES)
             tile = keep.tile([P, count * H], BF16, name="hot_%d" % s, align_bytes=64)
             nc.sync.dma_start(out=tile[:], in_=hot_hbm[g][:, t * H : (t + count) * H])
-            for i in range(count):
-                hot[s + i] = tile[:, i * H : (i + 1) * H]
+            for i in range(count // 2):
+                hot[s // 2 + i] = tile[:, 2 * i * H : 2 * (i + 1) * H]
 
         def load_scale_rows(tile, hbm):
             for q in range(4):
@@ -97,8 +98,8 @@ def tile_lora_down_gradient_s3_kernel(
         nc.sync.dma_start(
             out=channel_scale[:, 0:REST, :], in_=dy_rest_scale.rearrange("o (c p t) -> p (o c) t", p=P, t=PACK)
         )
-        load_hot(0, 2)
         nc.sync.dma_start(out=b_raw[:], in_=b_hot.rearrange("(p t) n -> p t n", t=PACK))
+        load_hot(0, 2)
         load_bytes(2, 2)
         load_hot(2, 2)
         nc.sync.dma_start(out=b_words_sb[:].bitcast(I32), in_=b_rest_words.rearrange("g p b -> p g b").bitcast(I32))
@@ -122,6 +123,7 @@ def tile_lora_down_gradient_s3_kernel(
         nc.vector.tensor_copy(out=channel_scale[:, REST, :], in_=channel_scale[:, 0, :])
 
         widened = {}
+        sorted_words = {}
         banks = {}
         grouped = {}
         dy_codes = {}
@@ -129,21 +131,38 @@ def tile_lora_down_gradient_s3_kernel(
         acc = {}
         sums = {}
 
-        def widen(s, pieces):
-            widened[s] = work.tile([P, C], BF16, name="widened", align_bytes=64, bufs=4)
-            width = C // pieces
-            for k0 in range(0, C, width):
-                nc.scalar.copy(out=widened[s][:, k0 : k0 + width], in_=rest_bytes[s][:, k0 : k0 + width].bitcast(FP8))
+        def widen(m, width):
+            widened[m] = work.tile([P, 2 * C], BF16, name="widened", align_bytes=64, bufs=2)
+            for k0 in range(0, 2 * C, width):
+                i, k = divmod(k0, C)
+                nc.scalar.copy(out=widened[m][:, k0 : k0 + width], in_=rest_bytes[2 * m + i][:, k : k + width].bitcast(FP8))
 
-        def turn_bank(j, words):
+        def bank_words(m, j):
+            if j == REST:
+                return hot[m].bitcast(F32)
+            return widened[m][:, 2 * K_PASS * j : 2 * K_PASS * (j + 1)].bitcast(F32)
+
+        def sort_words(m, j):
+            tile = work.tile([P, K_PASS], F32, name="sorted_words", align_bytes=64, bufs=4)
+            nc.scalar.copy(
+                out=tile[:].rearrange("p (c u n) -> p c u n", c=2, u=2),
+                in_=bank_words(m, j).rearrange("p (c n u) -> p c u n", c=2, u=2),
+            )
+            sorted_words[m, j] = tile
+
+        def turn_bank(m, j):
             bank = psum.tile([P, 2, 2, P], F32, name="turned", tag="turned_%d" % j, bufs=1)
             for c in range(2):
                 for u in range(2):
-                    nc.tensor.transpose(bank[:, u, c, :], words[c][:, u : 2 * P : 2], ident[:])
+                    if (m, j) in sorted_words:
+                        words = sorted_words[m, j][:, P * (2 * c + u) : P * (2 * c + u + 1)]
+                    else:
+                        words = bank_words(m, j)[:, 2 * P * c + u : 2 * P * (c + 1) : 2]
+                    nc.tensor.transpose(bank[:, u, c, :], words, ident[:])
             return bank
 
         def turn_hot(m):
-            bank = turn_bank(REST, [hot[2 * m + i].bitcast(F32) for i in range(2)])
+            bank = turn_bank(m, REST)
             slots = grouped[m][:].bitcast(F32).rearrange("p (c n u) -> p c n u", n=P, u=2)
             nc.scalar.copy(out=slots[:, 0 : 2 * PASSES : 2 * PASSES - 1, :, :], in_=bank[:].rearrange("p u c n -> p c n u"))
 
@@ -151,8 +170,7 @@ def tile_lora_down_gradient_s3_kernel(
             grouped[m] = work.tile([P, 2 * PASSES * K_PASS], BF16, name="grouped", align_bytes=64)
             if m > 0:
                 turn_hot(m)
-            words = [widened[2 * m + i][:, K_PASS * c : K_PASS * (c + 1)].bitcast(F32) for i in range(2) for c in range(REST)]
-            banks[m] = [turn_bank(j, words[2 * j : 2 * j + 2]) for j in range(REST)]
+            banks[m] = [turn_bank(m, j) for j in range(REST)]
             if m == 0:
                 turn_hot(m)
 
@@ -220,7 +238,7 @@ def tile_lora_down_gradient_s3_kernel(
                 in_=last_planes[:, :, r0:r1].rearrange("p t (c i) -> p c t i", i=4),
             )
 
-        def stage2(bank, d, groups):
+        def stage2(bank, d, groups, first=0, final=GROUPS - 1):
             for g in groups:
                 nc.tensor.matmul_mx(
                     out=bank[:],
@@ -228,8 +246,8 @@ def tile_lora_down_gradient_s3_kernel(
                     lhsT_scale=x_scales_sb[:, g, P * d : P * (d + 1)],
                     rhs=g_codes[g][:].bitcast(FP8X4),
                     rhs_scale=g_scales[g][:],
-                    start=(g == 0),
-                    stop=(g == GROUPS - 1),
+                    start=(g == first),
+                    stop=(g == final),
                 )
 
         def store(d, bank, copy):
@@ -237,8 +255,7 @@ def tile_lora_down_gradient_s3_kernel(
             nc.sync.dma_start(out=out[P * d : P * (d + 1), :], in_=result[d][:])
 
         last = GROUPS - 1
-        widen(0, REST)
-        widen(1, REST)
+        widen(0, K_PASS)
         turn(0)
         nc.gpsimd.tensor_scalar(
             out=b_grouped[:].rearrange("p (n t) -> p n t", t=PACK),
@@ -248,10 +265,24 @@ def tile_lora_down_gradient_s3_kernel(
             op0=MULT,
             op1=ADD,
         )
-        widen(2, 1)
-        widen(3, 1)
+        widen(1, C)
         nc.scalar.copy(out=token_weight[:], in_=token_weight_bf[:])
         waiting = {}
+        parked = []
+
+        def park(d):
+            bank = psum.tile([P, R], F32, name="early", tag="sum_bank")
+            stage2(bank, d, (0,), 0, 0)
+            nc.scalar.copy(out=result[d][:], in_=bank[:])
+            parked.append(d)
+
+        def side_jobs(m):
+            n = m + 2
+            if n >= PAIRS:
+                return [], []
+            first = [lambda: widen(n, 2 * C)] + [lambda j=j: sort_words(n, j) for j in (REST,)]
+            return first, [lambda j=j: sort_words(n, j) for j in range(REST) if n >= 7]
+
 
         def hold(d, tag, bufs):
             waiting[d] = psum.tile([P, R], F32, name="waiting", tag=tag, bufs=bufs)
@@ -273,7 +304,7 @@ def tile_lora_down_gradient_s3_kernel(
             if m == PAIRS:
                 for s in range(PHASES * last, TILES):
                     weigh_last(s)
-                    if s % PHASES < 2:
+                    if s % PHASES < 4:
                         hold(HELD + s % PHASES, "sum_bank", 4)
             if m == 0:
                 nc.vector.quantize_mx(out=b_hot_codes[:].bitcast(FP8X4), scales=b_hot_scales[:], in_=b_grouped[:])
@@ -284,11 +315,14 @@ def tile_lora_down_gradient_s3_kernel(
             if m >= 3:
                 quantise_g(g, HALF * h, HALF * (h + 1), lam_dst)
             if m < PAIRS:
+                jobs = side_jobs(m)
                 for s in (2 * m, 2 * m + 1):
-                    if s + 4 < TILES:
-                        widen(s + 4, 1)
+                    for job in jobs[s % 2]:
+                        job()
                     if s < PHASES * last:
                         weigh_tokens(s)
+                for i in range(PARKED.get(m, 0)):
+                    park(OUT_TILES - 1 - len(parked))
 
         for d in waiting:
             stage2(waiting[d], d, (last - 1,))
@@ -299,10 +333,16 @@ def tile_lora_down_gradient_s3_kernel(
         quantise_g(last, 0, HALF, last_grouped[:, 0 : PHASES * HALF])
         quantise_g(last, HALF, R, last_grouped[:, PHASES * HALF :])
 
-        for d in range(OUT_TILES):
+        for d in [4, 5, 6, 7, 0, 1, 2, 3] + list(range(2 * HELD, OUT_TILES)):
             if d in waiting:
                 bank = waiting[d]
                 stage2(bank, d, (last,))
+            elif d in parked:
+                bank = psum.tile([P, R], F32, name="late", tag="sum_bank")
+                stage2(bank, d, range(1, GROUPS), 1)
+                nc.vector.tensor_tensor(out=result[d][:], in0=bank[:], in1=result[d][:], op=ADD)
+                nc.sync.dma_start(out=out[P * d : P * (d + 1), :], in_=result[d][:])
+                continue
             else:
                 bank = psum.tile([P, R], F32, name="late", tag="sum_bank")
                 stage2(bank, d, range(GROUPS))

@@ -30,7 +30,8 @@ PAIRS = TILES // 2
 OUT_TILES = D // P
 HELD = 4
 HALF = R // 2
-PARKED = {}
+PARKED_AFTER_TURN = {}
+PARKED = {4: 2, 5: 2, 6: 2}
 
 
 def tile_lora_down_gradient_s3_kernel(
@@ -193,8 +194,11 @@ def tile_lora_down_gradient_s3_kernel(
                 in_=grouped[m][:, PASSES * K_PASS * i : PASSES * K_PASS * (i + 1)],
             )
 
+        def sum_tag(j):
+            return "sum_%d" % j
+
         def stage1(s):
-            acc[s] = psum.tile([P, R], F32, name="acc", tag="sum_bank")
+            acc[s] = psum.tile([P, R], F32, name="acc", tag=sum_tag(s % 2 + (2 if s >= TILES - 2 else 0)), bufs=1)
             first_rest = 1 - s % 2
             for c in range(PASSES):
                 is_hot = c == REST
@@ -268,20 +272,21 @@ def tile_lora_down_gradient_s3_kernel(
         widen(1, C)
         nc.scalar.copy(out=token_weight[:], in_=token_weight_bf[:])
         waiting = {}
-        parked = []
+        parked = {}
 
-        def park(d):
-            bank = psum.tile([P, R], F32, name="early", tag="sum_bank")
-            stage2(bank, d, (0,), 0, 0)
+        def park(count):
+            d = OUT_TILES - 1 - len(parked)
+            bank = psum.tile([P, R], F32, name="early", tag=sum_tag(2 + d % 2), bufs=1)
+            stage2(bank, d, range(count), 0, count - 1)
             nc.scalar.copy(out=result[d][:], in_=bank[:])
-            parked.append(d)
+            parked[d] = count
 
         def side_jobs(m):
             n = m + 2
             if n >= PAIRS:
                 return [], []
-            first = [lambda: widen(n, 2 * C)] + [lambda j=j: sort_words(n, j) for j in (REST,)]
-            return first, [lambda j=j: sort_words(n, j) for j in range(REST) if n >= 7]
+            first = [lambda: widen(n, 2 * C)] + [lambda j=j: sort_words(n, j) for j in ()]
+            return first, [lambda j=j: sort_words(n, j) for j in range(REST) if n >= 8]
 
 
         def hold(d, tag, bufs):
@@ -298,6 +303,8 @@ def tile_lora_down_gradient_s3_kernel(
                     product(m, j)
             if m + 1 < PAIRS:
                 turn(m + 1)
+            for i in range(PARKED_AFTER_TURN.get(m, 0)):
+                park(1)
             if m + 1 == PAIRS:
                 for j in range(HELD):
                     hold(j, "turned_%d" % ((j + REST) % PASSES), 1)
@@ -305,7 +312,7 @@ def tile_lora_down_gradient_s3_kernel(
                 for s in range(PHASES * last, TILES):
                     weigh_last(s)
                     if s % PHASES < 4:
-                        hold(HELD + s % PHASES, "sum_bank", 4)
+                        hold(HELD + s % PHASES, sum_tag(s % PHASES), 1)
             if m == 0:
                 nc.vector.quantize_mx(out=b_hot_codes[:].bitcast(FP8X4), scales=b_hot_scales[:], in_=b_grouped[:])
             if m < PAIRS:
@@ -322,7 +329,7 @@ def tile_lora_down_gradient_s3_kernel(
                     if s < PHASES * last:
                         weigh_tokens(s)
                 for i in range(PARKED.get(m, 0)):
-                    park(OUT_TILES - 1 - len(parked))
+                    park(m // 2 - 1)
 
         for d in waiting:
             stage2(waiting[d], d, (last - 1,))
@@ -333,17 +340,18 @@ def tile_lora_down_gradient_s3_kernel(
         quantise_g(last, 0, HALF, last_grouped[:, 0 : PHASES * HALF])
         quantise_g(last, HALF, R, last_grouped[:, PHASES * HALF :])
 
-        for d in [4, 5, 6, 7, 0, 1, 2, 3] + list(range(2 * HELD, OUT_TILES)):
+        order = [4, 5, 6, 7, 0, 1, 2, 3] + list(range(2 * HELD, OUT_TILES))
+        for i, d in enumerate(order):
             if d in waiting:
                 bank = waiting[d]
                 stage2(bank, d, (last,))
             elif d in parked:
-                bank = psum.tile([P, R], F32, name="late", tag="sum_bank")
-                stage2(bank, d, range(1, GROUPS), 1)
+                bank = psum.tile([P, R], F32, name="late", tag=sum_tag(i % 4), bufs=1)
+                stage2(bank, d, range(parked[d], GROUPS), parked[d])
                 nc.vector.tensor_tensor(out=result[d][:], in0=bank[:], in1=result[d][:], op=ADD)
                 nc.sync.dma_start(out=out[P * d : P * (d + 1), :], in_=result[d][:])
                 continue
             else:
-                bank = psum.tile([P, R], F32, name="late", tag="sum_bank")
+                bank = psum.tile([P, R], F32, name="late", tag=sum_tag(i % 4), bufs=1)
                 stage2(bank, d, range(GROUPS))
             store(d, bank, (nc.scalar.copy, nc.vector.tensor_copy)[d % 2])

@@ -30,7 +30,9 @@ PAIRS = TILES // 2
 OUT_TILES = D // P
 HELD = 4
 HALF = R // 2
-PARKED_AFTER_TURN = {}
+SPLIT = (3, 4)
+JOBS = {0: ([("w", 2)], []), 1: ([("w", 3)], []), 2: ([("w", 4)], []), 3: ([("w", 5)], [(3, 6)]), 4: ([("w", 6)], [(3, 7)]), 5: ([("w", 7)], [])}
+PARKED_AFTER_TURN = {5: 1, 6: 1}
 PARKED = {4: 2, 5: 2, 6: 2}
 
 
@@ -48,6 +50,8 @@ def tile_lora_down_gradient_s3_kernel(
         ident = keep.tile([P, P], F32, name="ident")
         token_weight_bf = keep.tile([P, TILES], BF16, name="token_weight_bf", align_bytes=64)
         token_weight = keep.tile([P, TILES], F32, name="token_weight", align_bytes=64)
+        lam_bf = keep.tile([P, PACK], BF16, name="lam_bf", align_bytes=64)
+        lam_col = keep.tile([P, PACK], F32, name="lam_col", align_bytes=64)
         lam_all = keep.tile([P, R], BF16, name="lam_all", align_bytes=64)
         channel_scale = keep.tile([P, PASSES, PACK], F32, name="channel_scale", align_bytes=64)
         b_raw = keep.tile([P, PACK, R], BF16, name="b_raw", align_bytes=64)
@@ -62,7 +66,7 @@ def tile_lora_down_gradient_s3_kernel(
         g_scales = [keep.tile([P, R], U8, name="g_scales_%d" % g, align_bytes=64) for g in range(GROUPS)]
         last_planes = keep.tile([P, PHASES, R], BF16, name="last_planes", align_bytes=64)
         last_grouped = keep.tile([P, R * PHASES], BF16, name="last_grouped", align_bytes=64)
-        result = [keep.tile([P, R], F32, name="result_%d" % d, align_bytes=64) for d in range(OUT_TILES)]
+        result = {}
 
         nc.vector.memset(b_scales_sb[:].rearrange("p g n -> p (g n)").bitcast(I32), 0)
         nc.vector.memset(x_scales_sb[:].rearrange("p g n -> p (g n)").bitcast(I32), 0)
@@ -94,7 +98,10 @@ def tile_lora_down_gradient_s3_kernel(
                     in_=hbm[:, 4 * q : 4 * q + 4, :].rearrange("g q n -> q g n").bitcast(I32),
                 )
 
-        load_bytes(0, 1)
+        first_bytes = keep.tile([P, K_PASS], U8, name="first_bytes", align_bytes=64)
+        nc.sync.dma_start(out=first_bytes[:], in_=bytes_hbm[0][:, 0:K_PASS])
+        other_bytes = keep.tile([P, C - K_PASS], U8, name="other_bytes", align_bytes=64)
+        nc.sync.dma_start(out=other_bytes[:], in_=bytes_hbm[0][:, K_PASS:C])
         load_bytes(1, 1)
         nc.sync.dma_start(
             out=channel_scale[:, 0:REST, :], in_=dy_rest_scale.rearrange("o (c p t) -> p (o c) t", p=P, t=PACK)
@@ -109,10 +116,10 @@ def tile_lora_down_gradient_s3_kernel(
             out=token_weight_bf[:].rearrange("m (g t) -> m g t", t=PHASES),
             in_=token_w.rearrange("(g m t) -> m g t", m=P, t=PHASES),
         )
+        nc.sync.dma_start(out=lam_bf[:], in_=lam.rearrange("(p i) -> p i", i=PACK))
         load_bytes(4, 2)
         load_hot(4, 4)
         load_bytes(6, 2)
-        nc.sync.dma_start(out=lam_all[:], in_=lam.partition_broadcast(P))
         for g in range(2, GROUPS):
             load_bytes(PHASES * g, 2)
             load_hot(PHASES * g, 4)
@@ -132,19 +139,30 @@ def tile_lora_down_gradient_s3_kernel(
         acc = {}
         sums = {}
 
-        def widen(m, width):
-            widened[m] = work.tile([P, 2 * C], BF16, name="widened", align_bytes=64, bufs=2)
-            for k0 in range(0, 2 * C, width):
+        def widen(m, width, k_from=0, k_to=2 * C):
+            if k_from == 0:
+                widened[m] = work.tile([P, 2 * C], BF16, name="widened", align_bytes=64, bufs=3)
+            for k0 in range(k_from, k_to, width):
                 i, k = divmod(k0, C)
-                nc.scalar.copy(out=widened[m][:, k0 : k0 + width], in_=rest_bytes[2 * m + i][:, k : k + width].bitcast(FP8))
+                if m == 0 and i == 0:
+                    src = first_bytes[:] if k == 0 else other_bytes[:, k - K_PASS : k - K_PASS + width]
+                else:
+                    src = rest_bytes[2 * m + i][:, k : k + width]
+                nc.scalar.copy(out=widened[m][:, k0 : k0 + width], in_=src.bitcast(FP8))
 
         def bank_words(m, j):
             if j == REST:
                 return hot[m].bitcast(F32)
             return widened[m][:, 2 * K_PASS * j : 2 * K_PASS * (j + 1)].bitcast(F32)
 
+        def spread_lam():
+            bank = psum.tile([P, PACK, P], F32, name="lam_bank", tag=sum_tag(2), bufs=1)
+            for i in range(PACK):
+                nc.tensor.transpose(bank[:, i, :], lam_col[:, i : i + 1].to_broadcast([P, P]), ident[:])
+            return bank
+
         def sort_words(m, j):
-            tile = work.tile([P, K_PASS], F32, name="sorted_words", align_bytes=64, bufs=4)
+            tile = work.tile([P, K_PASS], F32, name="sorted_words", align_bytes=64, bufs=5)
             nc.scalar.copy(
                 out=tile[:].rearrange("p (c u n) -> p c u n", c=2, u=2),
                 in_=bank_words(m, j).rearrange("p (c n u) -> p c u n", c=2, u=2),
@@ -164,49 +182,51 @@ def tile_lora_down_gradient_s3_kernel(
 
         def turn_hot(m):
             bank = turn_bank(m, REST)
-            slots = grouped[m][:].bitcast(F32).rearrange("p (c n u) -> p c n u", n=P, u=2)
-            nc.scalar.copy(out=slots[:, 0 : 2 * PASSES : 2 * PASSES - 1, :, :], in_=bank[:].rearrange("p u c n -> p c n u"))
+            nc.scalar.copy(
+                out=grouped[m][:, 2 * K_PASS * REST :].bitcast(F32).rearrange("p (c n u) -> p c n u", c=2, u=2),
+                in_=bank[:].rearrange("p u c n -> p c n u"),
+            )
 
         def turn(m):
             grouped[m] = work.tile([P, 2 * PASSES * K_PASS], BF16, name="grouped", align_bytes=64)
             if m > 0:
                 turn_hot(m)
-            banks[m] = [turn_bank(m, j) for j in range(REST)]
+            banks[m] = [turn_bank(m, j) for j in range(1 if m - 1 in SPLIT else REST)]
             if m == 0:
                 turn_hot(m)
 
         def product(m, j):
             c0 = 2 * j % REST
             nc.vector.tensor_tensor(
-                out=grouped[m][:, K_PASS * (2 * j + 1) : K_PASS * (2 * j + 3)].rearrange("p (c n u e) -> p c n u e", c=2, u=2, e=2),
+                out=grouped[m][:, 2 * K_PASS * j : 2 * K_PASS * (j + 1)].rearrange("p (c n u e) -> p c n u e", c=2, u=2, e=2),
                 in0=banks[m][j][:].rearrange("p u c n -> p (u c n)").bitcast(BF16).rearrange("p (u c n e) -> p c n u e", u=2, c=2, e=2),
                 in1=channel_scale[:, c0 : c0 + 2, :].unsqueeze(2).to_broadcast([P, 2, P, PACK]).rearrange("p c n (u e) -> p c n u e", u=2),
                 op=MULT,
             )
 
-        def quantise_dy(s):
-            m, i = divmod(s, 2)
-            dy_codes[s] = work.tile([P, PASSES * P], U32, name="dy_codes", align_bytes=64, bufs=4)
-            dy_code_scales[s] = work.tile([P, PASSES * P], U8, name="dy_code_scales", align_bytes=64, bufs=4)
-            nc.vector.quantize_mx(
-                out=dy_codes[s][:].bitcast(FP8X4),
-                scales=dy_code_scales[s][:],
-                in_=grouped[m][:, PASSES * K_PASS * i : PASSES * K_PASS * (i + 1)],
-            )
+        def quantise_dy(m, calls):
+            dy_codes[m] = work.tile([P, 2 * PASSES * P], U32, name="dy_codes", align_bytes=64, bufs=2)
+            dy_code_scales[m] = work.tile([P, 2 * PASSES * P], U8, name="dy_code_scales", align_bytes=64, bufs=2)
+            width = 2 * PASSES * P // calls
+            for c0 in range(0, 2 * PASSES * P, width):
+                nc.vector.quantize_mx(
+                    out=dy_codes[m][:, c0 : c0 + width].bitcast(FP8X4),
+                    scales=dy_code_scales[m][:, c0 : c0 + width],
+                    in_=grouped[m][:, PACK * c0 : PACK * (c0 + width)],
+                )
 
         def sum_tag(j):
             return "sum_%d" % j
 
         def stage1(s):
             acc[s] = psum.tile([P, R], F32, name="acc", tag=sum_tag(s % 2 + (2 if s >= TILES - 2 else 0)), bufs=1)
-            first_rest = 1 - s % 2
             for c in range(PASSES):
                 is_hot = c == REST
-                slot = (first_rest + c) % PASSES
+                slot = 2 * REST + s % 2 if is_hot else REST * (s % 2) + c
                 nc.tensor.matmul_mx(
                     out=acc[s][:],
-                    lhsT=dy_codes[s][:, P * slot : P * (slot + 1)].bitcast(FP8X4),
-                    lhsT_scale=dy_code_scales[s][:, P * slot : P * (slot + 1)],
+                    lhsT=dy_codes[s // 2][:, P * slot : P * (slot + 1)].bitcast(FP8X4),
+                    lhsT_scale=dy_code_scales[s // 2][:, P * slot : P * (slot + 1)],
                     rhs=b_hot_codes[:].bitcast(FP8X4) if is_hot else b_words_sb[:, c, :].bitcast(FP4X4),
                     rhs_scale=b_hot_scales[:] if is_hot else b_scales_sb[:, c, :],
                     start=(c == 0),
@@ -215,6 +235,9 @@ def tile_lora_down_gradient_s3_kernel(
 
         def weigh_tokens(s):
             g, t = divmod(s, PHASES)
+            if s == 0:
+                nc.scalar.copy(out=token_weight[:], in_=token_weight_bf[:])
+                nc.scalar.copy(out=lam_col[:], in_=lam_bf[:])
             if t == 0:
                 sums[g] = work.tile([P, PHASES, R], F32, name="sums", align_bytes=64, bufs=2)
             nc.scalar.activation(out=sums[g][:, t, :], in_=acc[s][:], func=COPY, scale=token_weight[:, s : s + 1])
@@ -242,19 +265,20 @@ def tile_lora_down_gradient_s3_kernel(
                 in_=last_planes[:, :, r0:r1].rearrange("p t (c i) -> p c t i", i=4),
             )
 
-        def stage2(bank, d, groups, first=0, final=GROUPS - 1):
+        def stage2(bank, d, groups, first=0, final=GROUPS - 1, cols=slice(0, R)):
             for g in groups:
                 nc.tensor.matmul_mx(
                     out=bank[:],
                     lhsT=x_words_sb[g][:, 2 * P * d : 2 * P * (d + 1)].bitcast(FP4X4),
                     lhsT_scale=x_scales_sb[:, g, P * d : P * (d + 1)],
-                    rhs=g_codes[g][:].bitcast(FP8X4),
-                    rhs_scale=g_scales[g][:],
+                    rhs=g_codes[g][:, cols].bitcast(FP8X4),
+                    rhs_scale=g_scales[g][:, cols],
                     start=(g == first),
                     stop=(g == final),
                 )
 
         def store(d, bank, copy):
+            result[d] = work.tile([P, R], F32, name="result", align_bytes=64, bufs=8)
             copy(out=result[d][:], in_=bank[:])
             nc.sync.dma_start(out=out[P * d : P * (d + 1), :], in_=result[d][:])
 
@@ -270,7 +294,6 @@ def tile_lora_down_gradient_s3_kernel(
             op1=ADD,
         )
         widen(1, C)
-        nc.scalar.copy(out=token_weight[:], in_=token_weight_bf[:])
         waiting = {}
         parked = {}
 
@@ -278,16 +301,20 @@ def tile_lora_down_gradient_s3_kernel(
             d = OUT_TILES - 1 - len(parked)
             bank = psum.tile([P, R], F32, name="early", tag=sum_tag(2 + d % 2), bufs=1)
             stage2(bank, d, range(count), 0, count - 1)
+            result[d] = keep.tile([P, R], F32, name="parked_%d" % d, align_bytes=64)
             nc.scalar.copy(out=result[d][:], in_=bank[:])
             parked[d] = count
 
         def side_jobs(m):
-            n = m + 2
-            if n >= PAIRS:
-                return [], []
-            first = [lambda: widen(n, 2 * C)] + [lambda j=j: sort_words(n, j) for j in ()]
-            return first, [lambda j=j: sort_words(n, j) for j in range(REST) if n >= 8]
-
+            def job(kind, n):
+                if kind == "w":
+                    return lambda: widen(n, 2 * C)
+                if kind == "wa":
+                    return lambda: widen(n, C, 0, C)
+                if kind == "wb":
+                    return lambda: widen(n, C, C)
+                return lambda: sort_words(n, kind)
+            return [[job(*x) for x in half] for half in JOBS.get(m, ([], []))]
 
         def hold(d, tag, bufs):
             waiting[d] = psum.tile([P, R], F32, name="waiting", tag=tag, bufs=bufs)
@@ -303,6 +330,14 @@ def tile_lora_down_gradient_s3_kernel(
                     product(m, j)
             if m + 1 < PAIRS:
                 turn(m + 1)
+            if m == 1:
+                lam_bank = spread_lam()
+            if m in SPLIT:
+                for job in side_jobs(m - 1)[1]:
+                    job()
+                stage1(2 * m - 1)
+                weigh_tokens(2 * m - 1)
+                banks[m + 1].extend(turn_bank(m + 1, j) for j in range(1, REST))
             for i in range(PARKED_AFTER_TURN.get(m, 0)):
                 park(1)
             if m + 1 == PAIRS:
@@ -315,17 +350,23 @@ def tile_lora_down_gradient_s3_kernel(
                         hold(HELD + s % PHASES, sum_tag(s % PHASES), 1)
             if m == 0:
                 nc.vector.quantize_mx(out=b_hot_codes[:].bitcast(FP8X4), scales=b_hot_scales[:], in_=b_grouped[:])
+            whole = False
+            if m >= 3 and whole:
+                quantise_g(g, HALF * h, HALF * (h + 1), lam_dst)
             if m < PAIRS:
+                quantise_dy(m, 1 if whole else 2)
                 for s in (2 * m, 2 * m + 1):
-                    quantise_dy(s)
-                    stage1(s)
-            if m >= 3:
+                    if s % 2 == 0 or m + 1 not in SPLIT:
+                        stage1(s)
+            if m >= 3 and not whole:
                 quantise_g(g, HALF * h, HALF * (h + 1), lam_dst)
             if m < PAIRS:
                 jobs = side_jobs(m)
-                for s in (2 * m, 2 * m + 1):
+                for s in (2 * m,) if m + 1 in SPLIT else (2 * m, 2 * m + 1):
                     for job in jobs[s % 2]:
                         job()
+                    if s == 2:
+                        nc.scalar.copy(out=lam_all[:].rearrange("p (n i) -> p n i", i=PACK), in_=lam_bank[:].rearrange("p i n -> p n i"))
                     if s < PHASES * last:
                         weigh_tokens(s)
                 for i in range(PARKED.get(m, 0)):
@@ -340,7 +381,7 @@ def tile_lora_down_gradient_s3_kernel(
         quantise_g(last, 0, HALF, last_grouped[:, 0 : PHASES * HALF])
         quantise_g(last, HALF, R, last_grouped[:, PHASES * HALF :])
 
-        order = [4, 5, 6, 7, 0, 1, 2, 3] + list(range(2 * HELD, OUT_TILES))
+        order = [4, 5, 6, 7, 0, 1, 2, 3] + [12, 13, 14, 15, 16, 17, 18, 8, 9, 10, 11]
         for i, d in enumerate(order):
             if d in waiting:
                 bank = waiting[d]
@@ -354,4 +395,12 @@ def tile_lora_down_gradient_s3_kernel(
             else:
                 bank = psum.tile([P, R], F32, name="late", tag=sum_tag(i % 4), bufs=1)
                 stage2(bank, d, range(GROUPS))
-            store(d, bank, (nc.scalar.copy, nc.vector.tensor_copy)[d % 2])
+            store(d, bank, (nc.scalar.copy, nc.vector.tensor_copy)[d % 2 if d < 2 * HELD else 0])
+
+        d = OUT_TILES - 1
+        for j in range(R // P):
+            cols = slice(P * j, P * (j + 1))
+            bank = psum.tile([P, P], F32, name="final", tag="turned_%d" % j, bufs=1)
+            stage2(bank, d, range(parked[d], GROUPS), parked[d], last, cols)
+            nc.vector.tensor_tensor(out=result[d][:, cols], in0=bank[:], in1=result[d][:, cols], op=ADD)
+            nc.sync.dma_start(out=out[P * d : P * (d + 1), cols], in_=result[d][:, cols])

@@ -30,9 +30,9 @@ PAIRS = TILES // 2
 OUT_TILES = D // P
 HELD = 4
 HALF = R // 2
-SPLIT = (3, 4)
-JOBS = {0: ([("w", 2)], []), 1: ([("w", 3)], []), 2: ([("w", 4)], []), 3: ([("w", 5)], [(3, 6)]), 4: ([("w", 6)], [(3, 7)]), 5: ([("w", 7)], [])}
-PARKED_AFTER_TURN = {5: 1, 6: 1}
+SPLIT = ()
+JOBS = {0: ([("w", 2)], []), 1: ([("w", 3)], []), 2: ([("w", 4)], []), 3: ([("w", 5)], []), 4: ([("w", 6)], []), 5: ([("w", 7)], [])}
+PARKED_AFTER_TURN = {}
 PARKED = {4: 2, 5: 2, 6: 2}
 
 
@@ -107,8 +107,8 @@ def tile_lora_down_gradient_s3_kernel(
             out=channel_scale[:, 0:REST, :], in_=dy_rest_scale.rearrange("o (c p t) -> p (o c) t", p=P, t=PACK)
         )
         nc.sync.dma_start(out=b_raw[:], in_=b_hot.rearrange("(p t) n -> p t n", t=PACK))
-        load_hot(0, 2)
         load_bytes(2, 2)
+        load_hot(0, 2)
         load_hot(2, 2)
         nc.sync.dma_start(out=b_words_sb[:].bitcast(I32), in_=b_rest_words.rearrange("g p b -> p g b").bitcast(I32))
         load_scale_rows(b_scales_sb, b_rest_scales)
@@ -169,8 +169,8 @@ def tile_lora_down_gradient_s3_kernel(
             )
             sorted_words[m, j] = tile
 
-        def turn_bank(m, j):
-            bank = psum.tile([P, 2, 2, P], F32, name="turned", tag="turned_%d" % j, bufs=1)
+        def turn_bank(m, j, tag=None):
+            bank = psum.tile([P, 2, 2, P], F32, name="turned", tag=tag or "turned_%d" % j, bufs=1)
             for c in range(2):
                 for u in range(2):
                     if (m, j) in sorted_words:
@@ -180,20 +180,16 @@ def tile_lora_down_gradient_s3_kernel(
                     nc.tensor.transpose(bank[:, u, c, :], words, ident[:])
             return bank
 
-        def turn_hot(m):
-            bank = turn_bank(m, REST)
+        def move_hot(m, bank):
             nc.scalar.copy(
                 out=grouped[m][:, 2 * K_PASS * REST :].bitcast(F32).rearrange("p (c n u) -> p c n u", c=2, u=2),
                 in_=bank[:].rearrange("p u c n -> p c n u"),
             )
 
         def turn(m):
-            grouped[m] = work.tile([P, 2 * PASSES * K_PASS], BF16, name="grouped", align_bytes=64)
-            if m > 0:
-                turn_hot(m)
+            grouped[m] = work.tile([P, 2 * PASSES * K_PASS], BF16, name="grouped", align_bytes=64, bufs=4)
+            move_hot(m, turn_bank(m, REST))
             banks[m] = [turn_bank(m, j) for j in range(1 if m - 1 in SPLIT else REST)]
-            if m == 0:
-                turn_hot(m)
 
         def product(m, j):
             c0 = 2 * j % REST
@@ -204,11 +200,12 @@ def tile_lora_down_gradient_s3_kernel(
                 op=MULT,
             )
 
-        def quantise_dy(m, calls):
-            dy_codes[m] = work.tile([P, 2 * PASSES * P], U32, name="dy_codes", align_bytes=64, bufs=2)
-            dy_code_scales[m] = work.tile([P, 2 * PASSES * P], U8, name="dy_code_scales", align_bytes=64, bufs=2)
+        def quantise_dy(m, calls, halves=(0, 1)):
+            if 0 in halves:
+                dy_codes[m] = work.tile([P, 2 * PASSES * P], U32, name="dy_codes", align_bytes=64, bufs=2)
+                dy_code_scales[m] = work.tile([P, 2 * PASSES * P], U8, name="dy_code_scales", align_bytes=64, bufs=2)
             width = 2 * PASSES * P // calls
-            for c0 in range(0, 2 * PASSES * P, width):
+            for c0 in range(halves[0] * PASSES * P, (halves[-1] + 1) * PASSES * P, width):
                 nc.vector.quantize_mx(
                     out=dy_codes[m][:, c0 : c0 + width].bitcast(FP8X4),
                     scales=dy_code_scales[m][:, c0 : c0 + width],
@@ -218,9 +215,10 @@ def tile_lora_down_gradient_s3_kernel(
         def sum_tag(j):
             return "sum_%d" % j
 
-        def stage1(s):
-            acc[s] = psum.tile([P, R], F32, name="acc", tag=sum_tag(s % 2 + (2 if s >= TILES - 2 else 0)), bufs=1)
-            for c in range(PASSES):
+        def stage1(s, passes=range(PASSES)):
+            if 0 in passes:
+                acc[s] = psum.tile([P, R], F32, name="acc", tag=sum_tag(s % 2 + (2 if s >= TILES - 2 else 0)), bufs=1)
+            for c in passes:
                 is_hot = c == REST
                 slot = 2 * REST + s % 2 if is_hot else REST * (s % 2) + c
                 nc.tensor.matmul_mx(
@@ -283,8 +281,8 @@ def tile_lora_down_gradient_s3_kernel(
             nc.sync.dma_start(out=out[P * d : P * (d + 1), :], in_=result[d][:])
 
         last = GROUPS - 1
-        widen(0, K_PASS)
-        turn(0)
+        widen(0, K_PASS, 0, 4 * K_PASS)
+        widen(0, 2 * K_PASS, 4 * K_PASS)
         nc.gpsimd.tensor_scalar(
             out=b_grouped[:].rearrange("p (n t) -> p n t", t=PACK),
             in0=b_raw[:].rearrange("p t n -> p n t"),
@@ -293,7 +291,23 @@ def tile_lora_down_gradient_s3_kernel(
             op0=MULT,
             op1=ADD,
         )
-        widen(1, C)
+        widen(1, 2 * K_PASS)
+        for m in range(2):
+            grouped[m] = work.tile([P, 2 * PASSES * K_PASS], BF16, name="grouped", align_bytes=64, bufs=4)
+        banks[0] = [turn_bank(0, j) for j in range(REST)]
+        move_hot(0, turn_bank(0, REST))
+        move_hot(1, turn_bank(1, REST, sum_tag(2)))
+        banks[1] = []
+        for j in range(REST):
+            product(0, j)
+            banks[1].append(turn_bank(1, j))
+        quantise_dy(0, 2, (0,))
+        nc.vector.quantize_mx(out=b_hot_codes[:].bitcast(FP8X4), scales=b_hot_scales[:], in_=b_grouped[:])
+        quantise_dy(0, 2, (1,))
+        stage1(0, range(REST))
+        stage1(1, range(REST))
+        stage1(0, (REST,))
+        stage1(1, (REST,))
         waiting = {}
         parked = {}
 
@@ -320,7 +334,11 @@ def tile_lora_down_gradient_s3_kernel(
             waiting[d] = psum.tile([P, R], F32, name="waiting", tag=tag, bufs=bufs)
             stage2(waiting[d], d, range(last - 1))
 
-        for m in range(PAIRS + 1):
+        for job in side_jobs(0)[0]:
+            job()
+        weigh_tokens(0)
+        weigh_tokens(1)
+        for m in range(1, PAIRS + 1):
             g, h = divmod(m - 3, 2)
             if m >= 3:
                 lam_dst = grouped[m - 1][:, PASSES * K_PASS : PASSES * K_PASS + PHASES * HALF]
@@ -348,8 +366,6 @@ def tile_lora_down_gradient_s3_kernel(
                     weigh_last(s)
                     if s % PHASES < 4:
                         hold(HELD + s % PHASES, sum_tag(s % PHASES), 1)
-            if m == 0:
-                nc.vector.quantize_mx(out=b_hot_codes[:].bitcast(FP8X4), scales=b_hot_scales[:], in_=b_grouped[:])
             whole = False
             if m >= 3 and whole:
                 quantise_g(g, HALF * h, HALF * (h + 1), lam_dst)
@@ -358,7 +374,11 @@ def tile_lora_down_gradient_s3_kernel(
                 for s in (2 * m, 2 * m + 1):
                     if s % 2 == 0 or m + 1 not in SPLIT:
                         stage1(s)
-            if m >= 3 and not whole:
+            if m == 3:
+                first_half = lam_dst
+            if m == 4:
+                quantise_g(0, 0, HALF, first_half)
+            if m >= 4 and not whole:
                 quantise_g(g, HALF * h, HALF * (h + 1), lam_dst)
             if m < PAIRS:
                 jobs = side_jobs(m)
@@ -381,7 +401,7 @@ def tile_lora_down_gradient_s3_kernel(
         quantise_g(last, 0, HALF, last_grouped[:, 0 : PHASES * HALF])
         quantise_g(last, HALF, R, last_grouped[:, PHASES * HALF :])
 
-        order = [4, 5, 6, 7, 0, 1, 2, 3] + [12, 13, 14, 15, 16, 17, 18, 8, 9, 10, 11]
+        order = [4, 5, 6, 7, 0, 1, 2, 3] + [14, 15, 16, 17, 18, 8, 9, 10, 11, 12, 13]
         for i, d in enumerate(order):
             if d in waiting:
                 bank = waiting[d]

@@ -263,14 +263,14 @@ def tile_lora_down_gradient_s3_kernel(
                 in_=last_planes[:, :, r0:r1].rearrange("p t (c i) -> p c t i", i=4),
             )
 
-        def stage2(bank, d, groups, first=0, final=GROUPS - 1, cols=slice(0, R)):
+        def stage2(bank, d, groups, first=0, final=GROUPS - 1):
             for g in groups:
                 nc.tensor.matmul_mx(
                     out=bank[:],
                     lhsT=x_words_sb[g][:, 2 * P * d : 2 * P * (d + 1)].bitcast(FP4X4),
                     lhsT_scale=x_scales_sb[:, g, P * d : P * (d + 1)],
-                    rhs=g_codes[g][:, cols].bitcast(FP8X4),
-                    rhs_scale=g_scales[g][:, cols],
+                    rhs=g_codes[g][:].bitcast(FP8X4),
+                    rhs_scale=g_scales[g][:],
                     start=(g == first),
                     stop=(g == final),
                 )
@@ -401,7 +401,7 @@ def tile_lora_down_gradient_s3_kernel(
         quantise_g(last, 0, HALF, last_grouped[:, 0 : PHASES * HALF])
         quantise_g(last, HALF, R, last_grouped[:, PHASES * HALF :])
 
-        order = [4, 5, 6, 7, 0, 1, 2, 3] + [14, 15, 16, 17, 18, 8, 9, 10, 11, 12, 13]
+        order = [4, 5, 6, 7, 0, 1, 2, 3] + list(range(OUT_TILES - 1, 2 * HELD - 1, -1))
         for i, d in enumerate(order):
             if d in waiting:
                 bank = waiting[d]
@@ -416,11 +416,3 @@ def tile_lora_down_gradient_s3_kernel(
                 bank = psum.tile([P, R], F32, name="late", tag=sum_tag(i % 4), bufs=1)
                 stage2(bank, d, range(GROUPS))
             store(d, bank, (nc.scalar.copy, nc.vector.tensor_copy)[d % 2 if d < 2 * HELD else 0])
-
-        d = OUT_TILES - 1
-        for j in range(R // P):
-            cols = slice(P * j, P * (j + 1))
-            bank = psum.tile([P, P], F32, name="final", tag="turned_%d" % j, bufs=1)
-            stage2(bank, d, range(parked[d], GROUPS), parked[d], last, cols)
-            nc.vector.tensor_tensor(out=result[d][:, cols], in0=bank[:], in1=result[d][:, cols], op=ADD)
-            nc.sync.dma_start(out=out[P * d : P * (d + 1), cols], in_=result[d][:, cols])

@@ -30,6 +30,7 @@ PAIRS = TILES // 2
 OUT_TILES = D // P
 HELD = 4
 HALF = R // 2
+PARKED_MID = {5: 1}
 SPLIT = ()
 JOBS = {0: ([("w", 2)], []), 1: ([("w", 3)], []), 2: ([("w", 4)], []), 3: ([("w", 5)], []), 4: ([("w", 6)], []), 5: ([("w", 7)], [])}
 PARKED_AFTER_TURN = {}
@@ -50,8 +51,6 @@ def tile_lora_down_gradient_s3_kernel(
         ident = keep.tile([P, P], F32, name="ident")
         token_weight_bf = keep.tile([P, TILES], BF16, name="token_weight_bf", align_bytes=64)
         token_weight = keep.tile([P, TILES], F32, name="token_weight", align_bytes=64)
-        lam_bf = keep.tile([P, PACK], BF16, name="lam_bf", align_bytes=64)
-        lam_col = keep.tile([P, PACK], F32, name="lam_col", align_bytes=64)
         lam_all = keep.tile([P, R], BF16, name="lam_all", align_bytes=64)
         channel_scale = keep.tile([P, PASSES, PACK], F32, name="channel_scale", align_bytes=64)
         b_raw = keep.tile([P, PACK, R], BF16, name="b_raw", align_bytes=64)
@@ -116,10 +115,10 @@ def tile_lora_down_gradient_s3_kernel(
             out=token_weight_bf[:].rearrange("m (g t) -> m g t", t=PHASES),
             in_=token_w.rearrange("(g m t) -> m g t", m=P, t=PHASES),
         )
-        nc.sync.dma_start(out=lam_bf[:], in_=lam.rearrange("(p i) -> p i", i=PACK))
         load_bytes(4, 2)
         load_hot(4, 4)
         load_bytes(6, 2)
+        nc.sync.dma_start(out=lam_all[:], in_=lam.partition_broadcast(P))
         for g in range(2, GROUPS):
             load_bytes(PHASES * g, 2)
             load_hot(PHASES * g, 4)
@@ -155,12 +154,6 @@ def tile_lora_down_gradient_s3_kernel(
                 return hot[m].bitcast(F32)
             return widened[m][:, 2 * K_PASS * j : 2 * K_PASS * (j + 1)].bitcast(F32)
 
-        def spread_lam():
-            bank = psum.tile([P, PACK, P], F32, name="lam_bank", tag=sum_tag(2), bufs=1)
-            for i in range(PACK):
-                nc.tensor.transpose(bank[:, i, :], lam_col[:, i : i + 1].to_broadcast([P, P]), ident[:])
-            return bank
-
         def sort_words(m, j):
             tile = work.tile([P, K_PASS], F32, name="sorted_words", align_bytes=64, bufs=5)
             nc.scalar.copy(
@@ -189,7 +182,10 @@ def tile_lora_down_gradient_s3_kernel(
         def turn(m):
             grouped[m] = work.tile([P, 2 * PASSES * K_PASS], BF16, name="grouped", align_bytes=64, bufs=4)
             move_hot(m, turn_bank(m, REST))
-            banks[m] = [turn_bank(m, j) for j in range(1 if m - 1 in SPLIT else REST)]
+            banks[m] = [turn_bank(m, j) for j in range(REST - 1)]
+            for i in range(PARKED_MID.get(m - 1, 0)):
+                park(1)
+            banks[m].append(turn_bank(m, REST - 1))
 
         def product(m, j):
             c0 = 2 * j % REST
@@ -235,7 +231,6 @@ def tile_lora_down_gradient_s3_kernel(
             g, t = divmod(s, PHASES)
             if s == 0:
                 nc.scalar.copy(out=token_weight[:], in_=token_weight_bf[:])
-                nc.scalar.copy(out=lam_col[:], in_=lam_bf[:])
             if t == 0:
                 sums[g] = work.tile([P, PHASES, R], F32, name="sums", align_bytes=64, bufs=2)
             nc.scalar.activation(out=sums[g][:, t, :], in_=acc[s][:], func=COPY, scale=token_weight[:, s : s + 1])
@@ -348,8 +343,6 @@ def tile_lora_down_gradient_s3_kernel(
                     product(m, j)
             if m + 1 < PAIRS:
                 turn(m + 1)
-            if m == 1:
-                lam_bank = spread_lam()
             if m in SPLIT:
                 for job in side_jobs(m - 1)[1]:
                     job()
@@ -385,14 +378,12 @@ def tile_lora_down_gradient_s3_kernel(
                 for s in (2 * m,) if m + 1 in SPLIT else (2 * m, 2 * m + 1):
                     for job in jobs[s % 2]:
                         job()
-                    if s == 2:
-                        nc.scalar.copy(out=lam_all[:].rearrange("p (n i) -> p n i", i=PACK), in_=lam_bank[:].rearrange("p i n -> p n i"))
                     if s < PHASES * last:
                         weigh_tokens(s)
                 for i in range(PARKED.get(m, 0)):
                     park(m // 2 - 1)
 
-        for d in waiting:
+        for d in list(waiting)[:5]:
             stage2(waiting[d], d, (last - 1,))
 
         interleave_last(nc.scalar.copy, 3 * P, R)
@@ -401,11 +392,11 @@ def tile_lora_down_gradient_s3_kernel(
         quantise_g(last, 0, HALF, last_grouped[:, 0 : PHASES * HALF])
         quantise_g(last, HALF, R, last_grouped[:, PHASES * HALF :])
 
-        order = [4, 5, 6, 7, 0, 1, 2, 3] + list(range(OUT_TILES - 1, 2 * HELD - 1, -1))
+        order = list(range(2 * HELD)) + list(range(OUT_TILES - 1, 2 * HELD - 1, -1))
         for i, d in enumerate(order):
             if d in waiting:
                 bank = waiting[d]
-                stage2(bank, d, (last,))
+                stage2(bank, d, (last,) if d < 5 else (last - 1, last))
             elif d in parked:
                 bank = psum.tile([P, R], F32, name="late", tag=sum_tag(i % 4), bufs=1)
                 stage2(bank, d, range(parked[d], GROUPS), parked[d])

@@ -28,13 +28,17 @@ REST = C // K_PASS
 PASSES = REST + 1
 PAIRS = TILES // 2
 OUT_TILES = D // P
-HELD = 4
 HALF = R // 2
-PARKED_MID = {5: 1}
-SPLIT = ()
-JOBS = {0: ([("w", 2)], []), 1: ([("w", 3)], []), 2: ([("w", 4)], []), 3: ([("w", 5)], []), 4: ([("w", 6)], []), 5: ([("w", 7)], [])}
-PARKED_AFTER_TURN = {}
-PARKED = {4: 2, 5: 2, 6: 2}
+BANK = 2 * K_PASS
+LAG2 = False
+LATE = 64
+AHEAD = {0: 0, 1: 0, 2: 0, 3: 0, 4: 0, 5: 0, 6: 0}
+SORT_S = (18,21,22,23)
+SORT_G = {2:(4,5)}
+UNITS = {1: 4, 2: 4, 3: 4, 4: 4, 5: 4, 6: 4}
+PARKS = {5: ("sum_0", "sum_1"), 6: ("sum_0", "sum_1","hot"), 7: ("hot", "x")}
+LEAD = 0
+FIRST = {1: 3}
 
 
 def tile_lora_down_gradient_s3_kernel(
@@ -45,7 +49,7 @@ def tile_lora_down_gradient_s3_kernel(
     with ExitStack() as ctx:
         keep = ctx.enter_context(tc.tile_pool(name="keep", bufs=1))
         work = ctx.enter_context(tc.tile_pool(name="work", bufs=3))
-        psum = ctx.enter_context(tc.psum_pool(name="psum", bufs=4))
+        psum = ctx.enter_context(tc.psum_pool(name="psum", bufs=1))
         ctx.enter_context(tc.manual_schedule())
 
         ident = keep.tile([P, P], F32, name="ident")
@@ -64,7 +68,6 @@ def tile_lora_down_gradient_s3_kernel(
         g_codes = [keep.tile([P, R], U32, name="g_codes_%d" % g, align_bytes=64) for g in range(GROUPS)]
         g_scales = [keep.tile([P, R], U8, name="g_scales_%d" % g, align_bytes=64) for g in range(GROUPS)]
         last_planes = keep.tile([P, PHASES, R], BF16, name="last_planes", align_bytes=64)
-        last_grouped = keep.tile([P, R * PHASES], BF16, name="last_grouped", align_bytes=64)
         result = {}
 
         nc.vector.memset(b_scales_sb[:].rearrange("p g n -> p (g n)").bitcast(I32), 0)
@@ -73,22 +76,22 @@ def tile_lora_down_gradient_s3_kernel(
 
         bytes_hbm = dy_rest_bytes.rearrange("(g m t) k -> g m (t k)", m=P, t=PHASES)
         hot_hbm = dy_hot.rearrange("(g m t) k -> g m (t k)", m=P, t=PHASES)
-        rest_bytes = {}
+        pair_bytes = {}
         hot = {}
 
-        def load_bytes(s, count):
-            g, t = divmod(s, PHASES)
-            tile = keep.tile([P, count * C], U8, name="rest_bytes_%d" % s, align_bytes=64)
-            nc.sync.dma_start(out=tile[:], in_=bytes_hbm[g][:, t * C : (t + count) * C])
-            for i in range(count):
-                rest_bytes[s + i] = tile[:, i * C :]
+        def load_bytes(m):
+            g, t = divmod(2 * m, PHASES)
+            tile = keep.tile([P, 2 * C], U8, name="rest_bytes_%d" % m, align_bytes=64)
+            nc.sync.dma_start(out=tile[:], in_=bytes_hbm[g][:, t * C : (t + 2) * C])
+            for j in range(REST):
+                pair_bytes[m, j] = tile[:, BANK * j : BANK * (j + 1)]
 
-        def load_hot(s, count):
-            g, t = divmod(s, PHASES)
-            tile = keep.tile([P, count * H], BF16, name="hot_%d" % s, align_bytes=64)
-            nc.sync.dma_start(out=tile[:], in_=hot_hbm[g][:, t * H : (t + count) * H])
-            for i in range(count // 2):
-                hot[s // 2 + i] = tile[:, 2 * i * H : 2 * (i + 1) * H]
+        def load_hot(m, count):
+            g, t = divmod(2 * m, PHASES)
+            tile = keep.tile([P, 2 * count * H], BF16, name="hot_%d" % m, align_bytes=64)
+            nc.sync.dma_start(out=tile[:], in_=hot_hbm[g][:, t * H : (t + 2 * count) * H])
+            for i in range(count):
+                hot[m + i] = tile[:, BANK * i : BANK * (i + 1)]
 
         def load_scale_rows(tile, hbm):
             for q in range(4):
@@ -101,28 +104,32 @@ def tile_lora_down_gradient_s3_kernel(
         nc.sync.dma_start(out=first_bytes[:], in_=bytes_hbm[0][:, 0:K_PASS])
         other_bytes = keep.tile([P, C - K_PASS], U8, name="other_bytes", align_bytes=64)
         nc.sync.dma_start(out=other_bytes[:], in_=bytes_hbm[0][:, K_PASS:C])
-        load_bytes(1, 1)
+        second_tile = keep.tile([P, C], U8, name="second_tile", align_bytes=64)
+        nc.sync.dma_start(out=second_tile[:], in_=bytes_hbm[0][:, C : 2 * C])
         nc.sync.dma_start(
             out=channel_scale[:, 0:REST, :], in_=dy_rest_scale.rearrange("o (c p t) -> p (o c) t", p=P, t=PACK)
         )
         nc.sync.dma_start(out=b_raw[:], in_=b_hot.rearrange("(p t) n -> p t n", t=PACK))
-        load_bytes(2, 2)
-        load_hot(0, 2)
-        load_hot(2, 2)
+        load_bytes(1)
+        load_hot(0, 1)
+        load_hot(1, 1)
         nc.sync.dma_start(out=b_words_sb[:].bitcast(I32), in_=b_rest_words.rearrange("g p b -> p g b").bitcast(I32))
         load_scale_rows(b_scales_sb, b_rest_scales)
+        load_bytes(2)
         nc.sync.dma_start(
             out=token_weight_bf[:].rearrange("m (g t) -> m g t", t=PHASES),
             in_=token_w.rearrange("(g m t) -> m g t", m=P, t=PHASES),
         )
-        load_bytes(4, 2)
-        load_hot(4, 4)
-        load_bytes(6, 2)
+        load_hot(2, 1)
+        load_bytes(3)
+        load_hot(3, 1)
+        load_hot(4, 2)
+        load_bytes(4)
         nc.sync.dma_start(out=lam_all[:], in_=lam.partition_broadcast(P))
-        for g in range(2, GROUPS):
-            load_bytes(PHASES * g, 2)
-            load_hot(PHASES * g, 4)
-            load_bytes(PHASES * g + 2, 2)
+        load_bytes(5)
+        load_bytes(6)
+        load_hot(6, 2)
+        load_bytes(7)
         load_scale_rows(x_scales_sb, x_scales)
         for g in range(GROUPS):
             nc.sync.dma_start(out=x_words_sb[g][:].bitcast(I32), in_=x_words[g].bitcast(I32))
@@ -137,90 +144,90 @@ def tile_lora_down_gradient_s3_kernel(
         dy_code_scales = {}
         acc = {}
         sums = {}
+        tag_of_acc = {}
+        tag_of_held = {}
 
-        def widen(m, width, k_from=0, k_to=2 * C):
-            if k_from == 0:
-                widened[m] = work.tile([P, 2 * C], BF16, name="widened", align_bytes=64, bufs=3)
-            for k0 in range(k_from, k_to, width):
-                i, k = divmod(k0, C)
-                if m == 0 and i == 0:
-                    src = first_bytes[:] if k == 0 else other_bytes[:, k - K_PASS : k - K_PASS + width]
-                else:
-                    src = rest_bytes[2 * m + i][:, k : k + width]
-                nc.scalar.copy(out=widened[m][:, k0 : k0 + width], in_=src.bitcast(FP8))
+        def widen(m, j, copy=nc.scalar.copy):
+            widened[m, j] = work.tile([P, BANK], BF16, name="widened", align_bytes=64, bufs=9)
+            copy(out=widened[m, j][:], in_=pair_bytes[m, j].bitcast(FP8))
 
-        def bank_words(m, j):
-            if j == REST:
-                return hot[m].bitcast(F32)
-            return widened[m][:, 2 * K_PASS * j : 2 * K_PASS * (j + 1)].bitcast(F32)
-
-        def sort_words(m, j):
-            tile = work.tile([P, K_PASS], F32, name="sorted_words", align_bytes=64, bufs=5)
-            nc.scalar.copy(
-                out=tile[:].rearrange("p (c u n) -> p c u n", c=2, u=2),
-                in_=bank_words(m, j).rearrange("p (c n u) -> p c u n", c=2, u=2),
+        def sort_words(m, j, copy):
+            tile = work.tile([P, K_PASS], F32, name="sorted_words", align_bytes=64, bufs=4)
+            copy(
+                out=tile[:].rearrange("p (u n) -> p u n", u=2),
+                in_=widened[m, j][:].bitcast(F32).rearrange("p (n u) -> p u n", u=2),
             )
-            sorted_words[m, j] = tile
+            sorted_words[m, j] = tile[:]
 
-        def turn_bank(m, j, tag=None):
-            bank = psum.tile([P, 2, 2, P], F32, name="turned", tag=tag or "turned_%d" % j, bufs=1)
+        def sort_hot(m, dst):
+            nc.gpsimd.tensor_scalar(
+                out=dst.rearrange("p (u n e) -> p u n e", u=2, e=2),
+                in0=hot[m].rearrange("p (n u e) -> p u n e", u=2, e=2),
+                scalar1=1.0,
+                scalar2=0.0,
+                op0=MULT,
+                op1=ADD,
+            )
+            sorted_words[m, REST] = dst.bitcast(F32)
+
+        def turn_bank(m, j, tag):
+            bank = psum.tile([P, 2, 2, P], F32, name="turned", tag=tag)
             for c in range(2):
                 for u in range(2):
                     if (m, j) in sorted_words:
-                        words = sorted_words[m, j][:, P * (2 * c + u) : P * (2 * c + u + 1)]
+                        words = sorted_words[m, j][:, P * (2 * u + c) : P * (2 * u + c + 1)]
                     else:
-                        words = bank_words(m, j)[:, 2 * P * c + u : 2 * P * (c + 1) : 2]
+                        src = hot[m] if j == REST else widened[m, j][:]
+                        words = src.bitcast(F32)[:, 2 * P * c + u : 2 * P * (c + 1) : 2]
                     nc.tensor.transpose(bank[:, u, c, :], words, ident[:])
-            return bank
+            banks[m, j] = bank
 
-        def move_hot(m, bank):
+        def new_grouped(m):
+            if m not in grouped:
+                grouped[m] = work.tile([P, 2 * PASSES, K_PASS], BF16, name="grouped", align_bytes=64, bufs=4)
+
+        def move_hot(m):
+            new_grouped(m)
             nc.scalar.copy(
-                out=grouped[m][:, 2 * K_PASS * REST :].bitcast(F32).rearrange("p (c n u) -> p c n u", c=2, u=2),
-                in_=bank[:].rearrange("p u c n -> p c n u"),
+                out=(grouped[m][:, 0 : 2 * PASSES : 2 * PASSES - 1, :] if m > 0 else grouped[m][:, 2 * REST :, :]).bitcast(F32).rearrange("p c (n u) -> p c n u", u=2),
+                in_=banks[m, REST][:].rearrange("p u c n -> p c n u"),
             )
-
-        def turn(m):
-            grouped[m] = work.tile([P, 2 * PASSES * K_PASS], BF16, name="grouped", align_bytes=64, bufs=4)
-            move_hot(m, turn_bank(m, REST))
-            banks[m] = [turn_bank(m, j) for j in range(REST - 1)]
-            for i in range(PARKED_MID.get(m - 1, 0)):
-                park(1)
-            banks[m].append(turn_bank(m, REST - 1))
 
         def product(m, j):
             c0 = 2 * j % REST
+            new_grouped(m)
             nc.vector.tensor_tensor(
-                out=grouped[m][:, 2 * K_PASS * j : 2 * K_PASS * (j + 1)].rearrange("p (c n u e) -> p c n u e", c=2, u=2, e=2),
-                in0=banks[m][j][:].rearrange("p u c n -> p (u c n)").bitcast(BF16).rearrange("p (u c n e) -> p c n u e", u=2, c=2, e=2),
+                out=grouped[m][:, 2 * j + min(m, 1) : 2 * j + 2 + min(m, 1), :].rearrange("p c (n u e) -> p c n u e", u=2, e=2),
+                in0=banks[m, j][:].rearrange("p u c n -> p (u c n)").bitcast(BF16).rearrange("p (u c n e) -> p c n u e", u=2, c=2, e=2),
                 in1=channel_scale[:, c0 : c0 + 2, :].unsqueeze(2).to_broadcast([P, 2, P, PACK]).rearrange("p c n (u e) -> p c n u e", u=2),
                 op=MULT,
             )
 
-        def quantise_dy(m, calls, halves=(0, 1)):
-            if 0 in halves:
-                dy_codes[m] = work.tile([P, 2 * PASSES * P], U32, name="dy_codes", align_bytes=64, bufs=2)
-                dy_code_scales[m] = work.tile([P, 2 * PASSES * P], U8, name="dy_code_scales", align_bytes=64, bufs=2)
-            width = 2 * PASSES * P // calls
-            for c0 in range(halves[0] * PASSES * P, (halves[-1] + 1) * PASSES * P, width):
-                nc.vector.quantize_mx(
-                    out=dy_codes[m][:, c0 : c0 + width].bitcast(FP8X4),
-                    scales=dy_code_scales[m][:, c0 : c0 + width],
-                    in_=grouped[m][:, PACK * c0 : PACK * (c0 + width)],
-                )
+        def quantise_dy(s):
+            m, i = divmod(s, 2)
+            dy_codes[s] = work.tile([P, PASSES * P], U32, name="dy_codes", align_bytes=64, bufs=4)
+            dy_code_scales[s] = work.tile([P, PASSES * P], U8, name="dy_code_scales", align_bytes=64, bufs=4)
+            nc.vector.quantize_mx(
+                out=dy_codes[s][:].bitcast(FP8X4),
+                scales=dy_code_scales[s][:],
+                in_=grouped[m][:, PASSES * i : PASSES * (i + 1), :].rearrange("p c k -> p (c k)"),
+            )
 
-        def sum_tag(j):
-            return "sum_%d" % j
-
-        def stage1(s, passes=range(PASSES)):
+        def stage1(s, tag, passes=range(PASSES)):
+            m, i = divmod(s, 2)
             if 0 in passes:
-                acc[s] = psum.tile([P, R], F32, name="acc", tag=sum_tag(s % 2 + (2 if s >= TILES - 2 else 0)), bufs=1)
+                acc[s] = psum.tile([P, R], F32, name="acc", tag=tag)
             for c in passes:
                 is_hot = c == REST
-                slot = 2 * REST + s % 2 if is_hot else REST * (s % 2) + c
+                if m == 0:
+                    slot = 2 * REST + i if is_hot else REST * i + c
+                else:
+                    slot = (2 * PASSES - 1) * i if is_hot else REST * i + c + 1
+                half, slot = divmod(slot, PASSES)
                 nc.tensor.matmul_mx(
                     out=acc[s][:],
-                    lhsT=dy_codes[s // 2][:, P * slot : P * (slot + 1)].bitcast(FP8X4),
-                    lhsT_scale=dy_code_scales[s // 2][:, P * slot : P * (slot + 1)],
+                    lhsT=dy_codes[2 * m + half][:, P * slot : P * (slot + 1)].bitcast(FP8X4),
+                    lhsT_scale=dy_code_scales[2 * m + half][:, P * slot : P * (slot + 1)],
                     rhs=b_hot_codes[:].bitcast(FP8X4) if is_hot else b_words_sb[:, c, :].bitcast(FP4X4),
                     rhs_scale=b_hot_scales[:] if is_hot else b_scales_sb[:, c, :],
                     start=(c == 0),
@@ -235,12 +242,12 @@ def tile_lora_down_gradient_s3_kernel(
                 sums[g] = work.tile([P, PHASES, R], F32, name="sums", align_bytes=64, bufs=2)
             nc.scalar.activation(out=sums[g][:, t, :], in_=acc[s][:], func=COPY, scale=token_weight[:, s : s + 1])
 
-        def weigh_ranks(g, h, dst):
-            cols = slice(HALF * h, HALF * (h + 1))
+        def weigh_ranks(g, r0, r1, t0, t1, dst):
+            n = t1 - t0
             nc.gpsimd.tensor_tensor(
-                out=dst.rearrange("p (c i t) -> p c t i", i=4, t=PHASES),
-                in0=sums[g][:, :, cols].rearrange("p t (c i) -> p c t i", i=4),
-                in1=lam_all[:, cols].rearrange("p (c i) -> p c i", i=4).unsqueeze(2).to_broadcast([P, HALF // 4, PHASES, 4]),
+                out=dst.rearrange("p (c i t) -> p c t i", i=4, t=PHASES)[:, :, t0:t1, :],
+                in0=sums[g][:, t0:t1, r0:r1].rearrange("p t (c i) -> p c t i", i=4),
+                in1=lam_all[:, r0:r1].rearrange("p (c i) -> p c i", i=4).unsqueeze(2).to_broadcast([P, (r1 - r0) // 4, n, 4]),
                 op=MULT,
             )
 
@@ -254,7 +261,7 @@ def tile_lora_down_gradient_s3_kernel(
 
         def interleave_last(copy, r0, r1):
             copy(
-                out=last_grouped[:, PHASES * r0 : PHASES * r1].rearrange("p (c i t) -> p c t i", i=4, t=PHASES),
+                out=b_grouped[:, PHASES * r0 : PHASES * r1].rearrange("p (c i t) -> p c t i", i=4, t=PHASES),
                 in_=last_planes[:, :, r0:r1].rearrange("p t (c i) -> p c t i", i=4),
             )
 
@@ -270,14 +277,70 @@ def tile_lora_down_gradient_s3_kernel(
                     stop=(g == final),
                 )
 
-        def store(d, bank, copy):
-            result[d] = work.tile([P, R], F32, name="result", align_bytes=64, bufs=8)
-            copy(out=result[d][:], in_=bank[:])
-            nc.sync.dma_start(out=out[P * d : P * (d + 1), :], in_=result[d][:])
+        def second_half(m):
+            return grouped[m][:, PASSES:, :].rearrange("p c k -> p (c k)")
 
         last = GROUPS - 1
-        widen(0, K_PASS, 0, 4 * K_PASS)
-        widen(0, 2 * K_PASS, 4 * K_PASS)
+        held = {}
+        added = {}
+        parked = {}
+
+        def hold(tag, upto):
+            d = len(held)
+            held[d] = psum.tile([P, R], F32, name="held", tag=tag)
+            added[d] = 0
+            tag_of_held[d] = tag
+            add(d, upto)
+
+        def add(d, upto):
+            stage2(held[d], d, range(added[d], upto))
+            added[d] = upto
+
+        def park(count, tag):
+            d = OUT_TILES - 1 - len(parked)
+            bank = psum.tile([P, R], F32, name="early", tag=tag)
+            stage2(bank, d, range(count), 0, count - 1)
+            result[d] = keep.tile([P, R], F32, name="parked_%d" % d, align_bytes=64)
+            nc.scalar.copy(out=result[d][:], in_=bank[:])
+            parked[d] = count
+
+        units = []
+        for n in range(REST * 2, REST * PAIRS):
+            units.append((widen, n))
+            if n in SORT_S:
+                units.append((lambda m_, j_: sort_words(m_, j_, nc.scalar.copy), n))
+
+        def run_units(count, upto=-1):
+            while units and (count > 0 or units[0][1] <= upto):
+                f, n_ = units.pop(0)
+                f(*divmod(n_, REST))
+                count = count - 1
+
+        free = ["bank_%d" % i for i in range(5)]
+        tag_of = {}
+        turned = [0]
+
+        def turn_upto(n1):
+            for n_ in range(turned[0], n1):
+                tag_of[n_] = free.pop(0)
+                turn_bank(n_ // REST, n_ % REST, tag_of[n_])
+            turned[0] = max(n1, turned[0])
+
+        done = [0]
+
+        def products(n1):
+            for n_ in range(done[0], n1):
+                product(*divmod(n_, REST))
+                free.append(tag_of[n_])
+            done[0] = max(n1, done[0])
+
+        for j in range(REST):
+            widened[0, j] = work.tile([P, BANK], BF16, name="widened", align_bytes=64, bufs=9)
+        nc.scalar.copy(out=widened[0, 0][:, 0:K_PASS], in_=first_bytes[:].bitcast(FP8))
+        nc.scalar.copy(out=widened[0, 0][:, K_PASS:], in_=other_bytes[:, 0:K_PASS].bitcast(FP8))
+        nc.scalar.copy(out=widened[0, 1][:, 0:K_PASS], in_=other_bytes[:, K_PASS:].bitcast(FP8))
+        nc.scalar.copy(out=widened[0, 1][:, K_PASS:], in_=second_tile[:, 0:K_PASS].bitcast(FP8))
+        nc.scalar.copy(out=widened[0, 2][:], in_=second_tile[:, K_PASS:].bitcast(FP8))
         nc.gpsimd.tensor_scalar(
             out=b_grouped[:].rearrange("p (n t) -> p n t", t=PACK),
             in0=b_raw[:].rearrange("p t n -> p n t"),
@@ -286,124 +349,111 @@ def tile_lora_down_gradient_s3_kernel(
             op0=MULT,
             op1=ADD,
         )
-        widen(1, 2 * K_PASS)
-        for m in range(2):
-            grouped[m] = work.tile([P, 2 * PASSES * K_PASS], BF16, name="grouped", align_bytes=64, bufs=4)
-        banks[0] = [turn_bank(0, j) for j in range(REST)]
-        move_hot(0, turn_bank(0, REST))
-        move_hot(1, turn_bank(1, REST, sum_tag(2)))
-        banks[1] = []
         for j in range(REST):
-            product(0, j)
-            banks[1].append(turn_bank(1, j))
-        quantise_dy(0, 2, (0,))
-        nc.vector.quantize_mx(out=b_hot_codes[:].bitcast(FP8X4), scales=b_hot_scales[:], in_=b_grouped[:])
-        quantise_dy(0, 2, (1,))
-        stage1(0, range(REST))
-        stage1(1, range(REST))
-        stage1(0, (REST,))
-        stage1(1, (REST,))
-        waiting = {}
-        parked = {}
-
-        def park(count):
-            d = OUT_TILES - 1 - len(parked)
-            bank = psum.tile([P, R], F32, name="early", tag=sum_tag(2 + d % 2), bufs=1)
-            stage2(bank, d, range(count), 0, count - 1)
-            result[d] = keep.tile([P, R], F32, name="parked_%d" % d, align_bytes=64)
-            nc.scalar.copy(out=result[d][:], in_=bank[:])
-            parked[d] = count
-
-        def side_jobs(m):
-            def job(kind, n):
-                if kind == "w":
-                    return lambda: widen(n, 2 * C)
-                if kind == "wa":
-                    return lambda: widen(n, C, 0, C)
-                if kind == "wb":
-                    return lambda: widen(n, C, C)
-                return lambda: sort_words(n, kind)
-            return [[job(*x) for x in half] for half in JOBS.get(m, ([], []))]
-
-        def hold(d, tag, bufs):
-            waiting[d] = psum.tile([P, R], F32, name="waiting", tag=tag, bufs=bufs)
-            stage2(waiting[d], d, range(last - 1))
-
-        for job in side_jobs(0)[0]:
-            job()
-        weigh_tokens(0)
-        weigh_tokens(1)
-        for m in range(1, PAIRS + 1):
-            g, h = divmod(m - 3, 2)
-            if m >= 3:
-                lam_dst = grouped[m - 1][:, PASSES * K_PASS : PASSES * K_PASS + PHASES * HALF]
-                weigh_ranks(g, h, lam_dst)
-            if m < PAIRS:
-                for j in range(REST):
-                    product(m, j)
-            if m + 1 < PAIRS:
-                turn(m + 1)
-            if m in SPLIT:
-                for job in side_jobs(m - 1)[1]:
-                    job()
-                stage1(2 * m - 1)
-                weigh_tokens(2 * m - 1)
-                banks[m + 1].extend(turn_bank(m + 1, j) for j in range(1, REST))
-            for i in range(PARKED_AFTER_TURN.get(m, 0)):
-                park(1)
-            if m + 1 == PAIRS:
-                for j in range(HELD):
-                    hold(j, "turned_%d" % ((j + REST) % PASSES), 1)
-            if m == PAIRS:
-                for s in range(PHASES * last, TILES):
-                    weigh_last(s)
-                    if s % PHASES < 4:
-                        hold(HELD + s % PHASES, sum_tag(s % PHASES), 1)
-            whole = False
-            if m >= 3 and whole:
-                quantise_g(g, HALF * h, HALF * (h + 1), lam_dst)
-            if m < PAIRS:
-                quantise_dy(m, 1 if whole else 2)
-                for s in (2 * m, 2 * m + 1):
-                    if s % 2 == 0 or m + 1 not in SPLIT:
-                        stage1(s)
-            if m == 3:
-                first_half = lam_dst
-            if m == 4:
-                quantise_g(0, 0, HALF, first_half)
-            if m >= 4 and not whole:
-                quantise_g(g, HALF * h, HALF * (h + 1), lam_dst)
-            if m < PAIRS:
-                jobs = side_jobs(m)
-                for s in (2 * m,) if m + 1 in SPLIT else (2 * m, 2 * m + 1):
-                    for job in jobs[s % 2]:
-                        job()
+            widen(1, j)
+        turn_upto(3)
+        turn_bank(0, REST, "hot")
+        move_hot(0)
+        turn_bank(1, REST, "sum_1")
+        move_hot(1)
+        g_in = {}
+        for m in range(PAIRS + 1):
+            lag = 2 if LAG2 else 3
+            ready = (m - lag) // 2
+            g, h = divmod(m - lag, 2)
+            if m in SORT_G:
+                for i, n in enumerate(SORT_G[m]):
+                    sort_hot(n, second_half(m - 1)[:, BANK * (1 - i) : BANK * (2 - i)])
+            if LAG2 and m >= 2 and h == 0 and g < last:
+                g_in[g] = second_half(m - 1)[:, 0 : PHASES * (R - LATE)]
+                weigh_ranks(g, 0, R - LATE, 0, 2, g_in[g])
+            if LAG2 and m >= 2 and h == 1:
+                g_late = second_half(m - 1)[:, 0 : PHASES * LATE]
+                weigh_ranks(g, R - LATE, R, 0, PHASES, g_late)
+                weigh_ranks(g, 0, R - LATE, 2, PHASES, g_in[g])
+            if not LAG2 and m >= 3:
+                g_in[g, h] = second_half(m - 1)[:, 0 : PHASES * HALF]
+                weigh_ranks(g, HALF * h, HALF * (h + 1), 0, PHASES, g_in[g, h])
+            budget = UNITS.get(m, 0)
+            parks = list(PARKS.get(m, ()))
+            if 1 <= m < PAIRS:
+                for i in range(2):
+                    s = 2 * (m - 1) + i
+                    if m == 1 and i == 0:
+                        stage1(0, "sum_0", range(REST))
+                        stage1(1, "sum_1", range(REST))
+                    stage1(s, "sum_%d" % i, (REST,) if m == 1 else range(PASSES))
                     if s < PHASES * last:
+                        k = min(budget, FIRST.get(m, 1) if i == 0 else 1)
+                        run_units(k)
+                        budget = budget - k
                         weigh_tokens(s)
-                for i in range(PARKED.get(m, 0)):
-                    park(m // 2 - 1)
+            if m == PAIRS:
+                break
+            if ready > 0:
+                for d in held:
+                    add(d, ready)
+                if parks:
+                    park(ready, parks.pop(0))
+            products(REST * (m + 1) + (LEAD if m == 0 else 0))
+            if m + 1 < PAIRS:
+                upto = min(REST * (m + 2) + AHEAD[m], REST * PAIRS)
+                run_units(budget, upto - 1)
+                if m > 0:
+                    turn_bank(m + 1, REST, "hot")
+                    move_hot(m + 1)
+                turn_upto(upto)
+                while free and m + 2 < PAIRS and ready > 0:
+                    hold(free.pop(0), ready)
+            if m + 1 == PAIRS:
+                last_tags = ["hot", free.pop(0)]
+                parks = [last_tags[1]] if parks else []
+            for tag in parks:
+                park(ready, tag)
+            if m + 1 == PAIRS:
+                hold(free.pop(0), ready)
+            quantise_dy(2 * m)
+            if m == 0:
+                nc.vector.quantize_mx(out=b_hot_codes[:].bitcast(FP8X4), scales=b_hot_scales[:], in_=b_grouped[:])
+            quantise_dy(2 * m + 1)
+            if LAG2 and m >= 3 and h == 1:
+                quantise_g(g, 0, HALF, g_in[g][:, 0 : PHASES * HALF])
+                quantise_g(g, HALF, 3 * P, g_in[g][:, PHASES * HALF : PHASES * 3 * P])
+                quantise_g(g, 3 * P, R - LATE, g_in[g][:, PHASES * 3 * P :])
+                quantise_g(g, R - LATE, R, g_late)
+            if not LAG2 and m >= 3:
+                quantise_g(g, HALF * h, HALF * (h + 1), g_in[g, h])
 
-        for d in list(waiting)[:5]:
-            stage2(waiting[d], d, (last - 1,))
-
+        weigh_last(TILES - 4)
+        weigh_last(TILES - 3)
+        for i in range(2):
+            stage1(TILES - 2 + i, last_tags[i])
+            weigh_last(TILES - 2 + i)
+        if not LAG2:
+            quantise_g(last - 1, HALF, R, g_in[last - 1, 1])
+        hold(free.pop(0), last - 1)
+        for tag in ("sum_0", "sum_1"):
+            hold(tag, last - 1)
+        for d in list(held):
+            add(d, last)
         interleave_last(nc.scalar.copy, 3 * P, R)
         interleave_last(nc.vector.tensor_copy, 0, HALF)
         interleave_last(nc.vector.tensor_copy, HALF, 3 * P)
-        quantise_g(last, 0, HALF, last_grouped[:, 0 : PHASES * HALF])
-        quantise_g(last, HALF, R, last_grouped[:, PHASES * HALF :])
+        quantise_g(last, 0, HALF, b_grouped[:, 0 : PHASES * HALF])
+        quantise_g(last, HALF, R, b_grouped[:, PHASES * HALF :])
 
-        order = list(range(2 * HELD)) + list(range(OUT_TILES - 1, 2 * HELD - 1, -1))
+        tags = last_tags + [tag_of_held[0], tag_of_held[1]]
+        order = list(held) + list(range(OUT_TILES - 1, len(held) - 1, -1))
         for i, d in enumerate(order):
-            if d in waiting:
-                bank = waiting[d]
-                stage2(bank, d, (last,) if d < 5 else (last - 1, last))
-            elif d in parked:
-                bank = psum.tile([P, R], F32, name="late", tag=sum_tag(i % 4), bufs=1)
-                stage2(bank, d, range(parked[d], GROUPS), parked[d])
-                nc.vector.tensor_tensor(out=result[d][:], in0=bank[:], in1=result[d][:], op=ADD)
-                nc.sync.dma_start(out=out[P * d : P * (d + 1), :], in_=result[d][:])
-                continue
+            if d in held:
+                add(d, GROUPS)
+                bank = held[d]
             else:
-                bank = psum.tile([P, R], F32, name="late", tag=sum_tag(i % 4), bufs=1)
-                stage2(bank, d, range(GROUPS))
-            store(d, bank, (nc.scalar.copy, nc.vector.tensor_copy)[d % 2 if d < 2 * HELD else 0])
+                bank = psum.tile([P, R], F32, name="late", tag=tags[(i - len(held)) % 4])
+                stage2(bank, d, range(parked.get(d, 0), GROUPS), parked.get(d, 0))
+            if d in parked:
+                nc.vector.tensor_tensor(out=result[d][:], in0=bank[:], in1=result[d][:], op=ADD)
+            else:
+                result[d] = work.tile([P, R], F32, name="result", align_bytes=64, bufs=8)
+                (nc.scalar.copy, nc.vector.tensor_copy)[d % 2 if d in held else 0](out=result[d][:], in_=bank[:])
+            nc.sync.dma_start(out=out[P * d : P * (d + 1), :], in_=result[d][:])

@@ -30,15 +30,17 @@ PAIRS = TILES // 2
 OUT_TILES = D // P
 HALF = R // 2
 BANK = 2 * K_PASS
-LAG2 = False
-LATE = 64
-AHEAD = {0: 0, 1: 0, 2: 0, 3: 0, 4: 0, 5: 0, 6: 0}
-SORT_S = (18,21,22,23)
-SORT_G = {2:(4,5)}
-UNITS = {1: 4, 2: 4, 3: 4, 4: 4, 5: 4, 6: 4}
-PARKS = {5: ("sum_0", "sum_1"), 6: ("sum_0", "sum_1","hot"), 7: ("hot", "x")}
-LEAD = 0
-FIRST = {1: 3}
+AHEAD = {1: 0, 2: 0, 3: 0, 4: 0, 5: 0, 6: 0}
+SORT_S = ((6, 0), (7, 0), (7, 1), (7, 2))
+SORT_G = {2: (4, 5)}
+UNITS = {2: 4, 3: 4, 4: 4, 5: 4, 6: 4}
+PARKS = {5: (0, 1), 6: (0, 2), 7: (1, 1)}
+HOLD = {5: 2, 6: 2, 7: 2}
+W3 = 0
+EXTRA = 2
+SLOTS = {4: 2, 5: 2, 6: 2}
+SORT_HOT = ()
+LAST_HOLD = 1
 
 
 def tile_lora_down_gradient_s3_kernel(
@@ -58,7 +60,7 @@ def tile_lora_down_gradient_s3_kernel(
         lam_all = keep.tile([P, R], BF16, name="lam_all", align_bytes=64)
         channel_scale = keep.tile([P, PASSES, PACK], F32, name="channel_scale", align_bytes=64)
         b_raw = keep.tile([P, PACK, R], BF16, name="b_raw", align_bytes=64)
-        b_grouped = keep.tile([P, R * PACK], BF16, name="b_grouped", align_bytes=64)
+        last_grouped = keep.tile([P, R * PACK], BF16, name="last_grouped", align_bytes=64)
         b_hot_codes = keep.tile([P, R], U32, name="b_hot_codes", align_bytes=64)
         b_hot_scales = keep.tile([P, R], U8, name="b_hot_scales", align_bytes=64)
         b_words_sb = keep.tile([P, REST, 2 * R], U8, name="b_words_sb", align_bytes=64)
@@ -83,8 +85,7 @@ def tile_lora_down_gradient_s3_kernel(
             g, t = divmod(2 * m, PHASES)
             tile = keep.tile([P, 2 * C], U8, name="rest_bytes_%d" % m, align_bytes=64)
             nc.sync.dma_start(out=tile[:], in_=bytes_hbm[g][:, t * C : (t + 2) * C])
-            for j in range(REST):
-                pair_bytes[m, j] = tile[:, BANK * j : BANK * (j + 1)]
+            pair_bytes[m] = tile
 
         def load_hot(m, count):
             g, t = divmod(2 * m, PHASES)
@@ -109,19 +110,19 @@ def tile_lora_down_gradient_s3_kernel(
         nc.sync.dma_start(
             out=channel_scale[:, 0:REST, :], in_=dy_rest_scale.rearrange("o (c p t) -> p (o c) t", p=P, t=PACK)
         )
-        nc.sync.dma_start(out=b_raw[:], in_=b_hot.rearrange("(p t) n -> p t n", t=PACK))
         load_bytes(1)
         load_hot(0, 1)
         load_hot(1, 1)
+        load_bytes(2)
+        nc.sync.dma_start(out=b_raw[:], in_=b_hot.rearrange("(p t) n -> p t n", t=PACK))
         nc.sync.dma_start(out=b_words_sb[:].bitcast(I32), in_=b_rest_words.rearrange("g p b -> p g b").bitcast(I32))
         load_scale_rows(b_scales_sb, b_rest_scales)
-        load_bytes(2)
+        load_hot(2, 1)
+        load_bytes(3)
         nc.sync.dma_start(
             out=token_weight_bf[:].rearrange("m (g t) -> m g t", t=PHASES),
             in_=token_w.rearrange("(g m t) -> m g t", m=P, t=PHASES),
         )
-        load_hot(2, 1)
-        load_bytes(3)
         load_hot(3, 1)
         load_hot(4, 2)
         load_bytes(4)
@@ -136,6 +137,8 @@ def tile_lora_down_gradient_s3_kernel(
 
         nc.vector.tensor_copy(out=channel_scale[:, REST, :], in_=channel_scale[:, 0, :])
 
+        free = ["bank_%d" % i for i in range(8)]
+        tag_of = {}
         widened = {}
         sorted_words = {}
         banks = {}
@@ -147,15 +150,16 @@ def tile_lora_down_gradient_s3_kernel(
         tag_of_acc = {}
         tag_of_held = {}
 
-        def widen(m, j, copy=nc.scalar.copy):
-            widened[m, j] = work.tile([P, BANK], BF16, name="widened", align_bytes=64, bufs=9)
-            copy(out=widened[m, j][:], in_=pair_bytes[m, j].bitcast(FP8))
+        def widen(m, j0=0, j1=REST):
+            if j0 == 0:
+                widened[m] = work.tile([P, 2 * C], BF16, name="widened", align_bytes=64, bufs=3)
+            nc.scalar.copy(out=widened[m][:, BANK * j0 : BANK * j1], in_=pair_bytes[m][:, BANK * j0 : BANK * j1].bitcast(FP8))
 
         def sort_words(m, j, copy):
-            tile = work.tile([P, K_PASS], F32, name="sorted_words", align_bytes=64, bufs=4)
+            tile = work.tile([P, K_PASS], F32, name="sorted_words", align_bytes=64, bufs=6)
             copy(
                 out=tile[:].rearrange("p (u n) -> p u n", u=2),
-                in_=widened[m, j][:].bitcast(F32).rearrange("p (n u) -> p u n", u=2),
+                in_=(hot[m] if j == REST else widened[m][:, BANK * j : BANK * (j + 1)]).bitcast(F32).rearrange("p (n u) -> p u n", u=2),
             )
             sorted_words[m, j] = tile[:]
 
@@ -170,14 +174,15 @@ def tile_lora_down_gradient_s3_kernel(
             )
             sorted_words[m, REST] = dst.bitcast(F32)
 
-        def turn_bank(m, j, tag):
-            bank = psum.tile([P, 2, 2, P], F32, name="turned", tag=tag)
+        def turn_bank(m, j):
+            tag_of["turned", m, j] = free.pop(0)
+            bank = psum.tile([P, 2, 2, P], F32, name="turned", tag=tag_of["turned", m, j])
             for c in range(2):
                 for u in range(2):
                     if (m, j) in sorted_words:
                         words = sorted_words[m, j][:, P * (2 * u + c) : P * (2 * u + c + 1)]
                     else:
-                        src = hot[m] if j == REST else widened[m, j][:]
+                        src = hot[m] if j == REST else widened[m][:, BANK * j : BANK * (j + 1)]
                         words = src.bitcast(F32)[:, 2 * P * c + u : 2 * P * (c + 1) : 2]
                     nc.tensor.transpose(bank[:, u, c, :], words, ident[:])
             banks[m, j] = bank
@@ -189,19 +194,21 @@ def tile_lora_down_gradient_s3_kernel(
         def move_hot(m):
             new_grouped(m)
             nc.scalar.copy(
-                out=(grouped[m][:, 0 : 2 * PASSES : 2 * PASSES - 1, :] if m > 0 else grouped[m][:, 2 * REST :, :]).bitcast(F32).rearrange("p c (n u) -> p c n u", u=2),
+                out=grouped[m][:, 0 : 2 * PASSES : 2 * PASSES - 1, :].bitcast(F32).rearrange("p c (n u) -> p c n u", u=2),
                 in_=banks[m, REST][:].rearrange("p u c n -> p c n u"),
             )
+            free.append(tag_of["turned", m, REST])
 
         def product(m, j):
             c0 = 2 * j % REST
             new_grouped(m)
             nc.vector.tensor_tensor(
-                out=grouped[m][:, 2 * j + min(m, 1) : 2 * j + 2 + min(m, 1), :].rearrange("p c (n u e) -> p c n u e", u=2, e=2),
+                out=grouped[m][:, 2 * j + 1 : 2 * j + 3, :].rearrange("p c (n u e) -> p c n u e", u=2, e=2),
                 in0=banks[m, j][:].rearrange("p u c n -> p (u c n)").bitcast(BF16).rearrange("p (u c n e) -> p c n u e", u=2, c=2, e=2),
                 in1=channel_scale[:, c0 : c0 + 2, :].unsqueeze(2).to_broadcast([P, 2, P, PACK]).rearrange("p c n (u e) -> p c n u e", u=2),
                 op=MULT,
             )
+            free.append(tag_of["turned", m, j])
 
         def quantise_dy(s):
             m, i = divmod(s, 2)
@@ -213,17 +220,14 @@ def tile_lora_down_gradient_s3_kernel(
                 in_=grouped[m][:, PASSES * i : PASSES * (i + 1), :].rearrange("p c k -> p (c k)"),
             )
 
-        def stage1(s, tag, passes=range(PASSES)):
+        def stage1(s, passes=range(PASSES)):
             m, i = divmod(s, 2)
             if 0 in passes:
-                acc[s] = psum.tile([P, R], F32, name="acc", tag=tag)
+                tag_of["acc", s] = free.pop(0)
+                acc[s] = psum.tile([P, R], F32, name="acc", tag=tag_of["acc", s])
             for c in passes:
                 is_hot = c == REST
-                if m == 0:
-                    slot = 2 * REST + i if is_hot else REST * i + c
-                else:
-                    slot = (2 * PASSES - 1) * i if is_hot else REST * i + c + 1
-                half, slot = divmod(slot, PASSES)
+                half, slot = divmod((2 * PASSES - 1) * i if is_hot else REST * i + c + 1, PASSES)
                 nc.tensor.matmul_mx(
                     out=acc[s][:],
                     lhsT=dy_codes[2 * m + half][:, P * slot : P * (slot + 1)].bitcast(FP8X4),
@@ -241,6 +245,7 @@ def tile_lora_down_gradient_s3_kernel(
             if t == 0:
                 sums[g] = work.tile([P, PHASES, R], F32, name="sums", align_bytes=64, bufs=2)
             nc.scalar.activation(out=sums[g][:, t, :], in_=acc[s][:], func=COPY, scale=token_weight[:, s : s + 1])
+            free.append(tag_of["acc", s])
 
         def weigh_ranks(g, r0, r1, t0, t1, dst):
             n = t1 - t0
@@ -258,10 +263,11 @@ def tile_lora_down_gradient_s3_kernel(
             nc.vector.scalar_tensor_tensor(
                 out=last_planes[:, s % PHASES, :], in0=acc[s][:], scalar=token_weight[:, s : s + 1], in1=lam_all[:], op0=MULT, op1=MULT
             )
+            free.append(tag_of["acc", s])
 
         def interleave_last(copy, r0, r1):
             copy(
-                out=b_grouped[:, PHASES * r0 : PHASES * r1].rearrange("p (c i t) -> p c t i", i=4, t=PHASES),
+                out=last_grouped[:, PHASES * r0 : PHASES * r1].rearrange("p (c i t) -> p c t i", i=4, t=PHASES),
                 in_=last_planes[:, :, r0:r1].rearrange("p t (c i) -> p c t i", i=4),
             )
 
@@ -284,46 +290,45 @@ def tile_lora_down_gradient_s3_kernel(
         held = {}
         added = {}
         parked = {}
+        pending = []
 
-        def hold(tag, upto):
+        def hold(upto):
             d = len(held)
-            held[d] = psum.tile([P, R], F32, name="held", tag=tag)
+            tag_of["held", d] = free.pop(0)
+            held[d] = psum.tile([P, R], F32, name="held", tag=tag_of["held", d])
             added[d] = 0
-            tag_of_held[d] = tag
             add(d, upto)
 
         def add(d, upto):
             stage2(held[d], d, range(added[d], upto))
             added[d] = upto
 
-        def park(count, tag):
+        def park(count):
             d = OUT_TILES - 1 - len(parked)
+            tag = free.pop(0)
             bank = psum.tile([P, R], F32, name="early", tag=tag)
             stage2(bank, d, range(count), 0, count - 1)
-            result[d] = keep.tile([P, R], F32, name="parked_%d" % d, align_bytes=64)
-            nc.scalar.copy(out=result[d][:], in_=bank[:])
             parked[d] = count
+            pending.append((d, bank, tag))
 
-        units = []
-        for n in range(REST * 2, REST * PAIRS):
-            units.append((widen, n))
-            if n in SORT_S:
-                units.append((lambda m_, j_: sort_words(m_, j_, nc.scalar.copy), n))
+        def empty_parked():
+            while pending:
+                d, bank, tag = pending.pop(0)
+                result[d] = keep.tile([P, R], F32, name="parked_%d" % d, align_bytes=64)
+                nc.scalar.copy(out=result[d][:], in_=bank[:])
+                free.append(tag)
 
-        def run_units(count, upto=-1):
-            while units and (count > 0 or units[0][1] <= upto):
-                f, n_ = units.pop(0)
-                f(*divmod(n_, REST))
-                count = count - 1
+        sorts = list(SORT_S)
 
-        free = ["bank_%d" % i for i in range(5)]
-        tag_of = {}
+        def sort_next(m):
+            if sorts and sorts[0][0] in widened and sorts[0][0] <= m:
+                sort_words(*sorts.pop(0), nc.scalar.copy)
+
         turned = [0]
 
         def turn_upto(n1):
             for n_ in range(turned[0], n1):
-                tag_of[n_] = free.pop(0)
-                turn_bank(n_ // REST, n_ % REST, tag_of[n_])
+                turn_bank(n_ // REST, n_ % REST)
             turned[0] = max(n1, turned[0])
 
         done = [0]
@@ -331,129 +336,134 @@ def tile_lora_down_gradient_s3_kernel(
         def products(n1):
             for n_ in range(done[0], n1):
                 product(*divmod(n_, REST))
-                free.append(tag_of[n_])
             done[0] = max(n1, done[0])
 
+        widened[0] = work.tile([P, 2 * C], BF16, name="widened", align_bytes=64, bufs=3)
+        nc.scalar.copy(out=widened[0][:, 0:K_PASS], in_=first_bytes[:].bitcast(FP8))
+        nc.scalar.copy(out=widened[0][:, K_PASS:BANK], in_=other_bytes[:, 0:K_PASS].bitcast(FP8))
+        nc.scalar.copy(out=widened[0][:, BANK:C], in_=other_bytes[:, K_PASS:].bitcast(FP8))
+        nc.scalar.copy(out=widened[0][:, C : 2 * BANK], in_=second_tile[:, 0:K_PASS].bitcast(FP8))
+        nc.scalar.copy(out=widened[0][:, 2 * BANK :], in_=second_tile[:, K_PASS:].bitcast(FP8))
         for j in range(REST):
-            widened[0, j] = work.tile([P, BANK], BF16, name="widened", align_bytes=64, bufs=9)
-        nc.scalar.copy(out=widened[0, 0][:, 0:K_PASS], in_=first_bytes[:].bitcast(FP8))
-        nc.scalar.copy(out=widened[0, 0][:, K_PASS:], in_=other_bytes[:, 0:K_PASS].bitcast(FP8))
-        nc.scalar.copy(out=widened[0, 1][:, 0:K_PASS], in_=other_bytes[:, K_PASS:].bitcast(FP8))
-        nc.scalar.copy(out=widened[0, 1][:, K_PASS:], in_=second_tile[:, 0:K_PASS].bitcast(FP8))
-        nc.scalar.copy(out=widened[0, 2][:], in_=second_tile[:, K_PASS:].bitcast(FP8))
+            widen(1, j, j + 1)
+        turn_upto(3)
+        turn_bank(0, REST)
+        move_hot(0)
+        turn_upto(6)
+        turn_bank(1, REST)
+        products(3)
+        widen(2, 0, 1)
+        widen(2, 1, 2)
+        move_hot(1)
+        widen(2, 2, 3)
+        quantise_dy(0)
+        b_grouped = grouped[0][:, 0:PASSES, :].rearrange("p c k -> p (c k)")
         nc.gpsimd.tensor_scalar(
-            out=b_grouped[:].rearrange("p (n t) -> p n t", t=PACK),
+            out=b_grouped.rearrange("p (n t) -> p n t", t=PACK),
             in0=b_raw[:].rearrange("p t n -> p n t"),
             scalar1=1.0,
             scalar2=0.0,
             op0=MULT,
             op1=ADD,
         )
-        for j in range(REST):
-            widen(1, j)
-        turn_upto(3)
-        turn_bank(0, REST, "hot")
-        move_hot(0)
-        turn_bank(1, REST, "sum_1")
-        move_hot(1)
+        turn_upto(8)
+        stage1(0, range(REST))
+        products(6)
+        turn_upto(9)
+        turn_bank(2, REST)
+        if W3 == 0:
+            widen(3)
+        move_hot(2)
+        if W3 == 1:
+            widen(3)
+        quantise_dy(1)
+        nc.vector.quantize_mx(out=b_hot_codes[:].bitcast(FP8X4), scales=b_hot_scales[:], in_=b_grouped)
+        quantise_dy(2)
+        quantise_dy(3)
+        stage1(1, range(REST))
+        for s in range(2):
+            stage1(s, (REST,))
+            weigh_tokens(s)
         g_in = {}
-        for m in range(PAIRS + 1):
-            lag = 2 if LAG2 else 3
-            ready = (m - lag) // 2
-            g, h = divmod(m - lag, 2)
+        for m in range(2, PAIRS):
+            ready = (m - 3) // 2
+            g, h = divmod(m - 3, 2)
             if m in SORT_G:
                 for i, n in enumerate(SORT_G[m]):
                     sort_hot(n, second_half(m - 1)[:, BANK * (1 - i) : BANK * (2 - i)])
-            if LAG2 and m >= 2 and h == 0 and g < last:
-                g_in[g] = second_half(m - 1)[:, 0 : PHASES * (R - LATE)]
-                weigh_ranks(g, 0, R - LATE, 0, 2, g_in[g])
-            if LAG2 and m >= 2 and h == 1:
-                g_late = second_half(m - 1)[:, 0 : PHASES * LATE]
-                weigh_ranks(g, R - LATE, R, 0, PHASES, g_late)
-                weigh_ranks(g, 0, R - LATE, 2, PHASES, g_in[g])
-            if not LAG2 and m >= 3:
+            if m >= 3:
                 g_in[g, h] = second_half(m - 1)[:, 0 : PHASES * HALF]
                 weigh_ranks(g, HALF * h, HALF * (h + 1), 0, PHASES, g_in[g, h])
-            budget = UNITS.get(m, 0)
-            parks = list(PARKS.get(m, ()))
-            if 1 <= m < PAIRS:
-                for i in range(2):
-                    s = 2 * (m - 1) + i
-                    if m == 1 and i == 0:
-                        stage1(0, "sum_0", range(REST))
-                        stage1(1, "sum_1", range(REST))
-                    stage1(s, "sum_%d" % i, (REST,) if m == 1 else range(PASSES))
-                    if s < PHASES * last:
-                        k = min(budget, FIRST.get(m, 1) if i == 0 else 1)
-                        run_units(k)
-                        budget = budget - k
-                        weigh_tokens(s)
-            if m == PAIRS:
-                break
+            before, after = PARKS.get(m, (0, 0))
+            stage1(2 * m - 2)
+            stage1(2 * m - 1)
             if ready > 0:
                 for d in held:
                     add(d, ready)
-                if parks:
-                    park(ready, parks.pop(0))
-            products(REST * (m + 1) + (LEAD if m == 0 else 0))
+                while len(held) < HOLD.get(m, 0):
+                    hold(ready)
+                for i in range(before):
+                    park(ready)
+            for i in range(2):
+                products(REST * m + i + 1)
+                if m + 1 < PAIRS:
+                    weigh_tokens(2 * m - 2 + i)
+                    if i < SLOTS.get(m, 0):
+                        sort_next(m + 2)
+            empty_parked()
             if m + 1 < PAIRS:
-                upto = min(REST * (m + 2) + AHEAD[m], REST * PAIRS)
-                run_units(budget, upto - 1)
-                if m > 0:
-                    turn_bank(m + 1, REST, "hot")
-                    move_hot(m + 1)
-                turn_upto(upto)
-                while free and m + 2 < PAIRS and ready > 0:
-                    hold(free.pop(0), ready)
+                turn_bank(m + 1, REST)
+                turn_upto(REST * (m + 1) + 2)
+                products(REST * (m + 1))
+                turn_upto(min(REST * (m + 2) + AHEAD[m], REST * PAIRS))
+                move_hot(m + 1)
+            for n in range(len(widened), min(m + (4 if m >= EXTRA else 3), PAIRS)):
+                widen(n)
+            for i in range(after):
+                park(ready)
+                empty_parked()
+            products(REST * (m + 1))
             if m + 1 == PAIRS:
-                last_tags = ["hot", free.pop(0)]
-                parks = [last_tags[1]] if parks else []
-            for tag in parks:
-                park(ready, tag)
-            if m + 1 == PAIRS:
-                hold(free.pop(0), ready)
+                for i in range(LAST_HOLD):
+                    hold(ready)
             quantise_dy(2 * m)
-            if m == 0:
-                nc.vector.quantize_mx(out=b_hot_codes[:].bitcast(FP8X4), scales=b_hot_scales[:], in_=b_grouped[:])
             quantise_dy(2 * m + 1)
-            if LAG2 and m >= 3 and h == 1:
-                quantise_g(g, 0, HALF, g_in[g][:, 0 : PHASES * HALF])
-                quantise_g(g, HALF, 3 * P, g_in[g][:, PHASES * HALF : PHASES * 3 * P])
-                quantise_g(g, 3 * P, R - LATE, g_in[g][:, PHASES * 3 * P :])
-                quantise_g(g, R - LATE, R, g_late)
-            if not LAG2 and m >= 3:
+            if m >= 3:
                 quantise_g(g, HALF * h, HALF * (h + 1), g_in[g, h])
 
+        g_in[last - 1, 1] = second_half(PAIRS - 1)[:, 0 : PHASES * HALF]
+        weigh_ranks(last - 1, HALF, R, 0, PHASES, g_in[last - 1, 1])
+        for s in (TILES - 2, TILES - 1):
+            stage1(s)
         weigh_last(TILES - 4)
         weigh_last(TILES - 3)
-        for i in range(2):
-            stage1(TILES - 2 + i, last_tags[i])
-            weigh_last(TILES - 2 + i)
-        if not LAG2:
-            quantise_g(last - 1, HALF, R, g_in[last - 1, 1])
-        hold(free.pop(0), last - 1)
-        for tag in ("sum_0", "sum_1"):
-            hold(tag, last - 1)
+        while free:
+            hold(last - 1)
+        weigh_last(TILES - 2)
+        weigh_last(TILES - 1)
+        quantise_g(last - 1, HALF, R, g_in[last - 1, 1])
         for d in list(held):
             add(d, last)
         interleave_last(nc.scalar.copy, 3 * P, R)
         interleave_last(nc.vector.tensor_copy, 0, HALF)
         interleave_last(nc.vector.tensor_copy, HALF, 3 * P)
-        quantise_g(last, 0, HALF, b_grouped[:, 0 : PHASES * HALF])
-        quantise_g(last, HALF, R, b_grouped[:, PHASES * HALF :])
+        quantise_g(last, 0, HALF, last_grouped[:, 0 : PHASES * HALF])
+        quantise_g(last, HALF, R, last_grouped[:, PHASES * HALF :])
 
-        tags = last_tags + [tag_of_held[0], tag_of_held[1]]
         order = list(held) + list(range(OUT_TILES - 1, len(held) - 1, -1))
         for i, d in enumerate(order):
             if d in held:
                 add(d, GROUPS)
                 bank = held[d]
+                tag = tag_of["held", d]
             else:
-                bank = psum.tile([P, R], F32, name="late", tag=tags[(i - len(held)) % 4])
+                tag = free.pop(0)
+                bank = psum.tile([P, R], F32, name="late", tag=tag)
                 stage2(bank, d, range(parked.get(d, 0), GROUPS), parked.get(d, 0))
             if d in parked:
                 nc.vector.tensor_tensor(out=result[d][:], in0=bank[:], in1=result[d][:], op=ADD)
             else:
                 result[d] = work.tile([P, R], F32, name="result", align_bytes=64, bufs=8)
                 (nc.scalar.copy, nc.vector.tensor_copy)[d % 2 if d in held else 0](out=result[d][:], in_=bank[:])
+            free.append(tag)
             nc.sync.dma_start(out=out[P * d : P * (d + 1), :], in_=result[d][:])

@@ -31,14 +31,18 @@ OUT_TILES = D // P
 HALF = R // 2
 BANK = 2 * K_PASS
 AHEAD = {1: 0, 2: 0, 3: 0, 4: 0, 5: 0, 6: 0}
-SORT_S = ((6, 0), (7, 0), (7, 1), (7, 2))
+SORT_S = ((7,0),(7,1),(7,2))
 SORT_G = {2: (4, 5)}
 UNITS = {2: 4, 3: 4, 4: 4, 5: 4, 6: 4}
-PARKS = {5: (0, 1), 6: (0, 2), 7: (1, 1)}
+PARKS = {4:(0,1),5: (1, 2), 6: (1, 2), 7: (1, 1)}
 HOLD = {5: 2, 6: 2, 7: 2}
-W3 = 0
+LAG2 = False
+GCOPY = False
+WHOLE = ()
+HOLD_AFTER = {4: 2}
+LATE = 64
 EXTRA = 2
-SLOTS = {4: 2, 5: 2, 6: 2}
+SLOTS = {5:2,6:2}
 SORT_HOT = ()
 LAST_HOLD = 1
 
@@ -110,29 +114,33 @@ def tile_lora_down_gradient_s3_kernel(
         nc.sync.dma_start(
             out=channel_scale[:, 0:REST, :], in_=dy_rest_scale.rearrange("o (c p t) -> p (o c) t", p=P, t=PACK)
         )
+        nc.sync.dma_start(out=b_raw[:], in_=b_hot.rearrange("(p t) n -> p t n", t=PACK))
         load_bytes(1)
         load_hot(0, 1)
         load_hot(1, 1)
-        load_bytes(2)
-        nc.sync.dma_start(out=b_raw[:], in_=b_hot.rearrange("(p t) n -> p t n", t=PACK))
         nc.sync.dma_start(out=b_words_sb[:].bitcast(I32), in_=b_rest_words.rearrange("g p b -> p g b").bitcast(I32))
         load_scale_rows(b_scales_sb, b_rest_scales)
-        load_hot(2, 1)
-        load_bytes(3)
+        load_bytes(2)
         nc.sync.dma_start(
             out=token_weight_bf[:].rearrange("m (g t) -> m g t", t=PHASES),
             in_=token_w.rearrange("(g m t) -> m g t", m=P, t=PHASES),
         )
+        load_hot(2, 1)
+        load_bytes(3)
+        if LAG2:
+            nc.sync.dma_start(out=lam_all[:], in_=lam.partition_broadcast(P))
         load_hot(3, 1)
         load_hot(4, 2)
         load_bytes(4)
-        nc.sync.dma_start(out=lam_all[:], in_=lam.partition_broadcast(P))
+        if not LAG2:
+            nc.sync.dma_start(out=lam_all[:], in_=lam.partition_broadcast(P))
         load_bytes(5)
         load_bytes(6)
         load_hot(6, 2)
-        load_bytes(7)
         load_scale_rows(x_scales_sb, x_scales)
-        for g in range(GROUPS):
+        nc.sync.dma_start(out=x_words_sb[0][:].bitcast(I32), in_=x_words[0].bitcast(I32))
+        load_bytes(7)
+        for g in range(1, GROUPS):
             nc.sync.dma_start(out=x_words_sb[g][:].bitcast(I32), in_=x_words[g].bitcast(I32))
 
         nc.vector.tensor_copy(out=channel_scale[:, REST, :], in_=channel_scale[:, 0, :])
@@ -164,6 +172,10 @@ def tile_lora_down_gradient_s3_kernel(
             sorted_words[m, j] = tile[:]
 
         def sort_hot(m, dst):
+            if GCOPY:
+                nc.gpsimd.tensor_copy(out=dst.bitcast(F32).rearrange("p (u n) -> p u n", u=2), in_=hot[m].bitcast(F32).rearrange("p (n u) -> p u n", u=2))
+                sorted_words[m, REST] = dst.bitcast(F32)
+                return
             nc.gpsimd.tensor_scalar(
                 out=dst.rearrange("p (u n e) -> p u n e", u=2, e=2),
                 in0=hot[m].rearrange("p (n u e) -> p u n e", u=2, e=2),
@@ -194,7 +206,7 @@ def tile_lora_down_gradient_s3_kernel(
         def move_hot(m):
             new_grouped(m)
             nc.scalar.copy(
-                out=grouped[m][:, 0 : 2 * PASSES : 2 * PASSES - 1, :].bitcast(F32).rearrange("p c (n u) -> p c n u", u=2),
+                out=(grouped[m][:, 0 : 2 * PASSES : 2 * PASSES - 1, :] if m > 0 else grouped[m][:, 2 * REST :, :]).bitcast(F32).rearrange("p c (n u) -> p c n u", u=2),
                 in_=banks[m, REST][:].rearrange("p u c n -> p c n u"),
             )
             free.append(tag_of["turned", m, REST])
@@ -203,7 +215,7 @@ def tile_lora_down_gradient_s3_kernel(
             c0 = 2 * j % REST
             new_grouped(m)
             nc.vector.tensor_tensor(
-                out=grouped[m][:, 2 * j + 1 : 2 * j + 3, :].rearrange("p c (n u e) -> p c n u e", u=2, e=2),
+                out=grouped[m][:, 2 * j + min(m, 1) : 2 * j + 2 + min(m, 1), :].rearrange("p c (n u e) -> p c n u e", u=2, e=2),
                 in0=banks[m, j][:].rearrange("p u c n -> p (u c n)").bitcast(BF16).rearrange("p (u c n e) -> p c n u e", u=2, c=2, e=2),
                 in1=channel_scale[:, c0 : c0 + 2, :].unsqueeze(2).to_broadcast([P, 2, P, PACK]).rearrange("p c n (u e) -> p c n u e", u=2),
                 op=MULT,
@@ -220,6 +232,14 @@ def tile_lora_down_gradient_s3_kernel(
                 in_=grouped[m][:, PASSES * i : PASSES * (i + 1), :].rearrange("p c k -> p (c k)"),
             )
 
+        def quantise_pair(m):
+            codes = work.tile([P, 2 * PASSES * P], U32, name="pair_codes", align_bytes=64, bufs=2)
+            scales = work.tile([P, 2 * PASSES * P], U8, name="pair_scales", align_bytes=64, bufs=2)
+            nc.vector.quantize_mx(out=codes[:].bitcast(FP8X4), scales=scales[:], in_=grouped[m][:].rearrange("p c k -> p (c k)"))
+            for i in range(2):
+                dy_codes[2 * m + i] = codes[:, PASSES * P * i : PASSES * P * (i + 1)]
+                dy_code_scales[2 * m + i] = scales[:, PASSES * P * i : PASSES * P * (i + 1)]
+
         def stage1(s, passes=range(PASSES)):
             m, i = divmod(s, 2)
             if 0 in passes:
@@ -227,7 +247,11 @@ def tile_lora_down_gradient_s3_kernel(
                 acc[s] = psum.tile([P, R], F32, name="acc", tag=tag_of["acc", s])
             for c in passes:
                 is_hot = c == REST
-                half, slot = divmod((2 * PASSES - 1) * i if is_hot else REST * i + c + 1, PASSES)
+                if m == 0:
+                    slot = 2 * REST + i if is_hot else REST * i + c
+                else:
+                    slot = (2 * PASSES - 1) * i if is_hot else REST * i + c + 1
+                half, slot = divmod(slot, PASSES)
                 nc.tensor.matmul_mx(
                     out=acc[s][:],
                     lhsT=dy_codes[2 * m + half][:, P * slot : P * (slot + 1)].bitcast(FP8X4),
@@ -344,20 +368,7 @@ def tile_lora_down_gradient_s3_kernel(
         nc.scalar.copy(out=widened[0][:, BANK:C], in_=other_bytes[:, K_PASS:].bitcast(FP8))
         nc.scalar.copy(out=widened[0][:, C : 2 * BANK], in_=second_tile[:, 0:K_PASS].bitcast(FP8))
         nc.scalar.copy(out=widened[0][:, 2 * BANK :], in_=second_tile[:, K_PASS:].bitcast(FP8))
-        for j in range(REST):
-            widen(1, j, j + 1)
-        turn_upto(3)
-        turn_bank(0, REST)
-        move_hot(0)
-        turn_upto(6)
-        turn_bank(1, REST)
-        products(3)
-        widen(2, 0, 1)
-        widen(2, 1, 2)
-        move_hot(1)
-        widen(2, 2, 3)
-        quantise_dy(0)
-        b_grouped = grouped[0][:, 0:PASSES, :].rearrange("p c k -> p (c k)")
+        b_grouped = last_grouped[:]
         nc.gpsimd.tensor_scalar(
             out=b_grouped.rearrange("p (n t) -> p n t", t=PACK),
             in0=b_raw[:].rearrange("p t n -> p n t"),
@@ -366,34 +377,52 @@ def tile_lora_down_gradient_s3_kernel(
             op0=MULT,
             op1=ADD,
         )
-        turn_upto(8)
-        stage1(0, range(REST))
-        products(6)
-        turn_upto(9)
-        turn_bank(2, REST)
-        if W3 == 0:
-            widen(3)
-        move_hot(2)
-        if W3 == 1:
-            widen(3)
-        quantise_dy(1)
+        for j in range(REST):
+            widen(1, j, j + 1)
+        turn_upto(3)
+        turn_bank(0, REST)
+        move_hot(0)
+        turn_bank(1, REST)
+        move_hot(1)
+        turn_upto(6)
+        products(3)
+        quantise_dy(0)
         nc.vector.quantize_mx(out=b_hot_codes[:].bitcast(FP8X4), scales=b_hot_scales[:], in_=b_grouped)
-        quantise_dy(2)
-        quantise_dy(3)
+        quantise_dy(1)
+        widen(2)
+        stage1(0, range(REST))
         stage1(1, range(REST))
         for s in range(2):
             stage1(s, (REST,))
-            weigh_tokens(s)
+        products(4)
+        weigh_tokens(0)
+        products(5)
+        weigh_tokens(1)
+        turn_bank(2, REST)
+        turn_upto(8)
+        products(6)
+        turn_upto(9)
+        move_hot(2)
+        widen(3)
+        quantise_dy(2)
+        quantise_dy(3)
         g_in = {}
         for m in range(2, PAIRS):
-            ready = (m - 3) // 2
-            g, h = divmod(m - 3, 2)
+            ready = (m - (2 if LAG2 else 3)) // 2
+            g, h = divmod(m - (2 if LAG2 else 3), 2)
+            if LAG2 and h == 0:
+                g_in[g] = second_half(m - 1)[:, 0 : PHASES * (R - LATE)]
+                weigh_ranks(g, 0, R - LATE, 0, 2, g_in[g])
+            if LAG2 and h == 1:
+                g_late = second_half(m - 1)[:, 0 : PHASES * LATE]
+                weigh_ranks(g, R - LATE, R, 0, PHASES, g_late)
+                weigh_ranks(g, 0, R - LATE, 2, PHASES, g_in[g])
+            if m >= 3 and not LAG2:
+                g_in[g, h] = second_half(m - 1)[:, 0 : PHASES * HALF]
+                weigh_ranks(g, HALF * h, HALF * (h + 1), 0, PHASES, g_in[g, h])
             if m in SORT_G:
                 for i, n in enumerate(SORT_G[m]):
                     sort_hot(n, second_half(m - 1)[:, BANK * (1 - i) : BANK * (2 - i)])
-            if m >= 3:
-                g_in[g, h] = second_half(m - 1)[:, 0 : PHASES * HALF]
-                weigh_ranks(g, HALF * h, HALF * (h + 1), 0, PHASES, g_in[g, h])
             before, after = PARKS.get(m, (0, 0))
             stage1(2 * m - 2)
             stage1(2 * m - 1)
@@ -419,20 +448,37 @@ def tile_lora_down_gradient_s3_kernel(
                 move_hot(m + 1)
             for n in range(len(widened), min(m + (4 if m >= EXTRA else 3), PAIRS)):
                 widen(n)
+            products(REST * (m + 1))
+            if m >= 3 and h == 1:
+                quantise_g(g, HALF * h, HALF * (h + 1), g_in[g, h])
+                ready = (m - 2) // 2
+            if ready > 0:
+                for d in held:
+                    add(d, ready)
+                while len(held) < HOLD_AFTER.get(m, 0):
+                    hold(ready)
             for i in range(after):
                 park(ready)
                 empty_parked()
-            products(REST * (m + 1))
             if m + 1 == PAIRS:
                 for i in range(LAST_HOLD):
                     hold(ready)
-            quantise_dy(2 * m)
-            quantise_dy(2 * m + 1)
-            if m >= 3:
+            if m in WHOLE:
+                quantise_pair(m)
+            else:
+                quantise_dy(2 * m)
+                quantise_dy(2 * m + 1)
+            if m >= 3 and h == 0:
                 quantise_g(g, HALF * h, HALF * (h + 1), g_in[g, h])
+            if LAG2 and h == 1:
+                quantise_g(g, 0, HALF, g_in[g][:, 0 : PHASES * HALF])
+                quantise_g(g, HALF, 3 * P, g_in[g][:, PHASES * HALF : PHASES * 3 * P])
+                quantise_g(g, 3 * P, R - LATE, g_in[g][:, PHASES * 3 * P :])
+                quantise_g(g, R - LATE, R, g_late)
 
-        g_in[last - 1, 1] = second_half(PAIRS - 1)[:, 0 : PHASES * HALF]
-        weigh_ranks(last - 1, HALF, R, 0, PHASES, g_in[last - 1, 1])
+        if not LAG2:
+            g_in[last - 1, 1] = second_half(PAIRS - 1)[:, 0 : PHASES * HALF]
+            weigh_ranks(last - 1, HALF, R, 0, PHASES, g_in[last - 1, 1])
         for s in (TILES - 2, TILES - 1):
             stage1(s)
         weigh_last(TILES - 4)
@@ -441,7 +487,8 @@ def tile_lora_down_gradient_s3_kernel(
             hold(last - 1)
         weigh_last(TILES - 2)
         weigh_last(TILES - 1)
-        quantise_g(last - 1, HALF, R, g_in[last - 1, 1])
+        if not LAG2:
+            quantise_g(last - 1, HALF, R, g_in[last - 1, 1])
         for d in list(held):
             add(d, last)
         interleave_last(nc.scalar.copy, 3 * P, R)

@@ -32,11 +32,15 @@ HALF = R // 2
 BANK = 2 * K_PASS
 AHEAD = {1: 0, 2: 0, 3: 0, 4: 0, 5: 0, 6: 0}
 SORT_S = ((7,0),(7,1),(7,2))
-SORT_G = {2: (4, 5)}
+SORT_G = {2:(4,)}
 UNITS = {2: 4, 3: 4, 4: 4, 5: 4, 6: 4}
-PARKS = {4:(0,1),5: (1, 2), 6: (1, 2), 7: (1, 1)}
+PARKS = {4:(0,0),5: (1, 2), 6: (1, 2), 7: (1, 1)}
 HOLD = {5: 2, 6: 2, 7: 2}
 LAG2 = False
+EARLY = 5
+OFF = (2,)
+CUT = 256
+W30 = False
 GCOPY = False
 WHOLE = ()
 HOLD_AFTER = {4: 2}
@@ -185,6 +189,40 @@ def tile_lora_down_gradient_s3_kernel(
                 op1=ADD,
             )
             sorted_words[m, REST] = dst.bitcast(F32)
+
+        spread = keep.tile([P, 2, 2, P, 2], F32, name="spread", align_bytes=64)
+
+        def spread_scales():
+            for c in range(2):
+                tag = free.pop(0)
+                bank = psum.tile([P, PACK, P], F32, name="spreading", tag=tag)
+                for t in range(PACK):
+                    nc.tensor.transpose(bank[:, t, :], channel_scale[:, c, t : t + 1].to_broadcast([P, P]), ident[:])
+                spreading.append((c, bank, tag))
+
+        spreading = []
+
+        def empty_spread():
+            for c, bank, tag in spreading:
+                nc.scalar.copy(out=spread[:, :, c, :, :], in_=bank[:].rearrange("p (u e) n -> p u n e", u=2))
+                free.append(tag)
+
+        def scale_first(m, dst):
+            nc.gpsimd.tensor_tensor(
+                out=dst.rearrange("p (u n e) -> p u n e", u=2, e=2),
+                in0=widened[m][:, 0:BANK].rearrange("p (n u e) -> p u n e", u=2, e=2),
+                in1=spread[:].rearrange("p u c n e -> p u (c n) e"),
+                op=MULT,
+            )
+            sorted_words[m, 0] = dst.bitcast(F32)
+
+        def move_first(m):
+            new_grouped(m)
+            nc.scalar.copy(
+                out=grouped[m][:, 1:3, :].bitcast(F32).rearrange("p c (n u) -> p c n u", u=2),
+                in_=banks[m, 0][:].rearrange("p u c n -> p c n u"),
+            )
+            free.append(tag_of["turned", m, 0])
 
         def turn_bank(m, j):
             tag_of["turned", m, j] = free.pop(0)
@@ -352,14 +390,16 @@ def tile_lora_down_gradient_s3_kernel(
 
         def turn_upto(n1):
             for n_ in range(turned[0], n1):
-                turn_bank(n_ // REST, n_ % REST)
+                if not (n_ % REST == 0 and n_ // REST in OFF):
+                    turn_bank(n_ // REST, n_ % REST)
             turned[0] = max(n1, turned[0])
 
         done = [0]
 
         def products(n1):
             for n_ in range(done[0], n1):
-                product(*divmod(n_, REST))
+                if not (n_ % REST == 0 and n_ // REST in OFF):
+                    product(*divmod(n_, REST))
             done[0] = max(n1, done[0])
 
         widened[0] = work.tile([P, 2 * C], BF16, name="widened", align_bytes=64, bufs=3)
@@ -377,19 +417,26 @@ def tile_lora_down_gradient_s3_kernel(
             op0=MULT,
             op1=ADD,
         )
+        turn_upto(3)
+        spread_scales()
         for j in range(REST):
             widen(1, j, j + 1)
-        turn_upto(3)
         turn_bank(0, REST)
-        move_hot(0)
         turn_bank(1, REST)
+        products(3)
+        move_hot(0)
         move_hot(1)
         turn_upto(6)
-        products(3)
+        empty_spread()
         quantise_dy(0)
         nc.vector.quantize_mx(out=b_hot_codes[:].bitcast(FP8X4), scales=b_hot_scales[:], in_=b_grouped)
         quantise_dy(1)
-        widen(2)
+        widen(2, 0, 1)
+        if 2 in OFF:
+            scale_first(2, second_half(0)[:, 0:BANK])
+        widen(2, 1, 3)
+        if W30:
+            widen(3, 0, 1)
         stage1(0, range(REST))
         stage1(1, range(REST))
         for s in range(2):
@@ -402,8 +449,14 @@ def tile_lora_down_gradient_s3_kernel(
         turn_upto(8)
         products(6)
         turn_upto(9)
+        if 2 in OFF:
+            turn_bank(2, 0)
         move_hot(2)
-        widen(3)
+        if not W30:
+            widen(3, 0, 1)
+        widen(3, 1, 3)
+        if 2 in OFF:
+            move_first(2)
         quantise_dy(2)
         quantise_dy(3)
         g_in = {}
@@ -418,11 +471,14 @@ def tile_lora_down_gradient_s3_kernel(
                 weigh_ranks(g, R - LATE, R, 0, PHASES, g_late)
                 weigh_ranks(g, 0, R - LATE, 2, PHASES, g_in[g])
             if m >= 3 and not LAG2:
-                g_in[g, h] = second_half(m - 1)[:, 0 : PHASES * HALF]
-                weigh_ranks(g, HALF * h, HALF * (h + 1), 0, PHASES, g_in[g, h])
+                r0, r1 = ((0, CUT), (CUT, R))[h] if g == 0 else (HALF * h, HALF * (h + 1))
+                g_in[g, h] = second_half(m - 1)[:, 0 : PHASES * (r1 - r0)]
+                weigh_ranks(g, r0, r1, 0, PHASES, g_in[g, h])
             if m in SORT_G:
                 for i, n in enumerate(SORT_G[m]):
                     sort_hot(n, second_half(m - 1)[:, BANK * (1 - i) : BANK * (2 - i)])
+            if m + 1 in OFF:
+                scale_first(m + 1, second_half(m - 1)[:, BANK:])
             before, after = PARKS.get(m, (0, 0))
             stage1(2 * m - 2)
             stage1(2 * m - 1)
@@ -445,12 +501,17 @@ def tile_lora_down_gradient_s3_kernel(
                 turn_upto(REST * (m + 1) + 2)
                 products(REST * (m + 1))
                 turn_upto(min(REST * (m + 2) + AHEAD[m], REST * PAIRS))
+                if m + 1 in OFF:
+                    turn_bank(m + 1, 0)
                 move_hot(m + 1)
+                if m + 1 in OFF:
+                    move_first(m + 1)
             for n in range(len(widened), min(m + (4 if m >= EXTRA else 3), PAIRS)):
                 widen(n)
             products(REST * (m + 1))
             if m >= 3 and h == 1:
-                quantise_g(g, HALF * h, HALF * (h + 1), g_in[g, h])
+                for q0, q1 in [(r0, r1)] if r1 - r0 in (P, HALF) else [(r0, r0 + P), (r0 + P, r1)]:
+                    quantise_g(g, q0, q1, g_in[g, h][:, PHASES * (q0 - r0) : PHASES * (q1 - r0)])
                 ready = (m - 2) // 2
             if ready > 0:
                 for d in held:
@@ -469,7 +530,8 @@ def tile_lora_down_gradient_s3_kernel(
                 quantise_dy(2 * m)
                 quantise_dy(2 * m + 1)
             if m >= 3 and h == 0:
-                quantise_g(g, HALF * h, HALF * (h + 1), g_in[g, h])
+                for q0, q1 in [(r0, r1)] if r1 - r0 in (P, HALF) else [(r0, r0 + P), (r0 + P, r1)]:
+                    quantise_g(g, q0, q1, g_in[g, h][:, PHASES * (q0 - r0) : PHASES * (q1 - r0)])
             if LAG2 and h == 1:
                 quantise_g(g, 0, HALF, g_in[g][:, 0 : PHASES * HALF])
                 quantise_g(g, HALF, 3 * P, g_in[g][:, PHASES * HALF : PHASES * 3 * P])
@@ -489,7 +551,7 @@ def tile_lora_down_gradient_s3_kernel(
         weigh_last(TILES - 1)
         if not LAG2:
             quantise_g(last - 1, HALF, R, g_in[last - 1, 1])
-        for d in list(held):
+        for d in list(held)[:EARLY]:
             add(d, last)
         interleave_last(nc.scalar.copy, 3 * P, R)
         interleave_last(nc.vector.tensor_copy, 0, HALF)

@@ -30,25 +30,19 @@ PAIRS = TILES // 2
 OUT_TILES = D // P
 HALF = R // 2
 BANK = 2 * K_PASS
-AHEAD = {1: 0, 2: 0, 3: 0, 4: 0, 5: 0, 6: 0}
-SORT_S = ((7,0),(7,1),(7,2))
-SORT_G = {2:(4,)}
-UNITS = {2: 4, 3: 4, 4: 4, 5: 4, 6: 4}
-PARKS = {4:(0,0),5: (1, 2), 6: (1, 2), 7: (1, 1)}
-HOLD = {5: 2, 6: 2, 7: 2}
-LAG2 = False
-EARLY = 5
-OFF = (2,)
-CUT = 256
-W30 = False
-GCOPY = False
-WHOLE = ()
-HOLD_AFTER = {4: 2}
-LATE = 64
-EXTRA = 2
-SLOTS = {5:2,6:2}
-SORT_HOT = ()
+HOT = REST
+ON_GPSIMD = (2, 3)
+SORTS = {7: (HOT, 0, 1, 2)}
+GSORTS = {}
+SLOTS = {1: (0, 0, 1, 2), 2: (1, 0, 0, 2), 3: (1, 0, 0, 3), 4: (1, 0, 0, 3), 5: (1, 0, 0, 2), 6: (2, 0, 0, 0)}
+PARKS = {5: (1, 2), 6: (1, 1), 7: (1, 1)}
+TURNS = 0
+SPLIT = 0
+VSORT = {2: (3, HOT), 3: (4, HOT)}
+HELD = 2
 LAST_HOLD = 1
+EARLY = 5
+SCALAR_RANKS = 128
 
 
 def tile_lora_down_gradient_s3_kernel(
@@ -68,7 +62,7 @@ def tile_lora_down_gradient_s3_kernel(
         lam_all = keep.tile([P, R], BF16, name="lam_all", align_bytes=64)
         channel_scale = keep.tile([P, PASSES, PACK], F32, name="channel_scale", align_bytes=64)
         b_raw = keep.tile([P, PACK, R], BF16, name="b_raw", align_bytes=64)
-        last_grouped = keep.tile([P, R * PACK], BF16, name="last_grouped", align_bytes=64)
+        b_grouped = keep.tile([P, R * PACK], BF16, name="b_grouped", align_bytes=64)
         b_hot_codes = keep.tile([P, R], U32, name="b_hot_codes", align_bytes=64)
         b_hot_scales = keep.tile([P, R], U8, name="b_hot_scales", align_bytes=64)
         b_words_sb = keep.tile([P, REST, 2 * R], U8, name="b_words_sb", align_bytes=64)
@@ -78,7 +72,7 @@ def tile_lora_down_gradient_s3_kernel(
         g_codes = [keep.tile([P, R], U32, name="g_codes_%d" % g, align_bytes=64) for g in range(GROUPS)]
         g_scales = [keep.tile([P, R], U8, name="g_scales_%d" % g, align_bytes=64) for g in range(GROUPS)]
         last_planes = keep.tile([P, PHASES, R], BF16, name="last_planes", align_bytes=64)
-        result = {}
+        spread = keep.tile([P, 2, 2, P, 2], F32, name="spread", align_bytes=64)
 
         nc.vector.memset(b_scales_sb[:].rearrange("p g n -> p (g n)").bitcast(I32), 0)
         nc.vector.memset(x_scales_sb[:].rearrange("p g n -> p (g n)").bitcast(I32), 0)
@@ -131,20 +125,16 @@ def tile_lora_down_gradient_s3_kernel(
         )
         load_hot(2, 1)
         load_bytes(3)
-        if LAG2:
-            nc.sync.dma_start(out=lam_all[:], in_=lam.partition_broadcast(P))
         load_hot(3, 1)
-        load_hot(4, 2)
         load_bytes(4)
-        if not LAG2:
-            nc.sync.dma_start(out=lam_all[:], in_=lam.partition_broadcast(P))
+        nc.sync.dma_start(out=lam_all[:], in_=lam.partition_broadcast(P))
+        load_hot(4, 2)
         load_bytes(5)
         load_bytes(6)
         load_hot(6, 2)
-        load_scale_rows(x_scales_sb, x_scales)
-        nc.sync.dma_start(out=x_words_sb[0][:].bitcast(I32), in_=x_words[0].bitcast(I32))
         load_bytes(7)
-        for g in range(1, GROUPS):
+        load_scale_rows(x_scales_sb, x_scales)
+        for g in range(GROUPS):
             nc.sync.dma_start(out=x_words_sb[g][:].bitcast(I32), in_=x_words[g].bitcast(I32))
 
         nc.vector.tensor_copy(out=channel_scale[:, REST, :], in_=channel_scale[:, 0, :])
@@ -159,106 +149,91 @@ def tile_lora_down_gradient_s3_kernel(
         dy_code_scales = {}
         acc = {}
         sums = {}
-        tag_of_acc = {}
-        tag_of_held = {}
 
-        def widen(m, j0=0, j1=REST):
+        def take(key, shape):
+            tag_of[key] = free.pop(0)
+            return psum.tile(shape, F32, name=key[0], tag=tag_of[key])
+
+        def release(key):
+            free.append(tag_of[key])
+
+        def widen(m, j0, j1):
             if j0 == 0:
                 widened[m] = work.tile([P, 2 * C], BF16, name="widened", align_bytes=64, bufs=3)
             nc.scalar.copy(out=widened[m][:, BANK * j0 : BANK * j1], in_=pair_bytes[m][:, BANK * j0 : BANK * j1].bitcast(FP8))
+
+        def values(m, j):
+            return hot[m] if j == HOT else widened[m][:, BANK * j : BANK * (j + 1)]
 
         def sort_words(m, j, copy):
             tile = work.tile([P, K_PASS], F32, name="sorted_words", align_bytes=64, bufs=6)
             copy(
                 out=tile[:].rearrange("p (u n) -> p u n", u=2),
-                in_=(hot[m] if j == REST else widened[m][:, BANK * j : BANK * (j + 1)]).bitcast(F32).rearrange("p (n u) -> p u n", u=2),
+                in_=values(m, j).bitcast(F32).rearrange("p (n u) -> p u n", u=2),
             )
             sorted_words[m, j] = tile[:]
 
-        def sort_hot(m, dst):
-            if GCOPY:
-                nc.gpsimd.tensor_copy(out=dst.bitcast(F32).rearrange("p (u n) -> p u n", u=2), in_=hot[m].bitcast(F32).rearrange("p (n u) -> p u n", u=2))
-                sorted_words[m, REST] = dst.bitcast(F32)
-                return
-            nc.gpsimd.tensor_scalar(
-                out=dst.rearrange("p (u n e) -> p u n e", u=2, e=2),
-                in0=hot[m].rearrange("p (n u e) -> p u n e", u=2, e=2),
-                scalar1=1.0,
-                scalar2=0.0,
-                op0=MULT,
-                op1=ADD,
+        def sort_into(m, j, dst):
+            nc.gpsimd.tensor_copy(
+                out=dst.bitcast(F32).rearrange("p (u n) -> p u n", u=2),
+                in_=values(m, j).bitcast(F32).rearrange("p (n u) -> p u n", u=2),
             )
-            sorted_words[m, REST] = dst.bitcast(F32)
+            sorted_words[m, j] = dst.bitcast(F32)
 
-        spread = keep.tile([P, 2, 2, P, 2], F32, name="spread", align_bytes=64)
+        def spread_scales(c):
+            banks["spread", c] = take(("spreading", c), [P, PACK, P])
+            for t in range(PACK):
+                nc.tensor.transpose(banks["spread", c][:, t, :], channel_scale[:, c, t : t + 1].to_broadcast([P, P]), ident[:])
 
-        def spread_scales():
-            for c in range(2):
-                tag = free.pop(0)
-                bank = psum.tile([P, PACK, P], F32, name="spreading", tag=tag)
-                for t in range(PACK):
-                    nc.tensor.transpose(bank[:, t, :], channel_scale[:, c, t : t + 1].to_broadcast([P, P]), ident[:])
-                spreading.append((c, bank, tag))
-
-        spreading = []
-
-        def empty_spread():
-            for c, bank, tag in spreading:
-                nc.scalar.copy(out=spread[:, :, c, :, :], in_=bank[:].rearrange("p (u e) n -> p u n e", u=2))
-                free.append(tag)
+        def empty_spread(c):
+            nc.scalar.copy(out=spread[:, :, c, :, :], in_=banks["spread", c][:].rearrange("p (u e) n -> p u n e", u=2))
+            release(("spreading", c))
 
         def scale_first(m, dst):
             nc.gpsimd.tensor_tensor(
                 out=dst.rearrange("p (u n e) -> p u n e", u=2, e=2),
-                in0=widened[m][:, 0:BANK].rearrange("p (n u e) -> p u n e", u=2, e=2),
+                in0=values(m, 0).rearrange("p (n u e) -> p u n e", u=2, e=2),
                 in1=spread[:].rearrange("p u c n e -> p u (c n) e"),
                 op=MULT,
             )
             sorted_words[m, 0] = dst.bitcast(F32)
 
-        def move_first(m):
-            new_grouped(m)
-            nc.scalar.copy(
-                out=grouped[m][:, 1:3, :].bitcast(F32).rearrange("p c (n u) -> p c n u", u=2),
-                in_=banks[m, 0][:].rearrange("p u c n -> p c n u"),
-            )
-            free.append(tag_of["turned", m, 0])
-
-        def turn_bank(m, j):
-            tag_of["turned", m, j] = free.pop(0)
-            bank = psum.tile([P, 2, 2, P], F32, name="turned", tag=tag_of["turned", m, j])
+        def turn(m, j):
+            bank = take(("turned", m, j), [P, 2, 2, P])
             for c in range(2):
                 for u in range(2):
                     if (m, j) in sorted_words:
                         words = sorted_words[m, j][:, P * (2 * u + c) : P * (2 * u + c + 1)]
                     else:
-                        src = hot[m] if j == REST else widened[m][:, BANK * j : BANK * (j + 1)]
-                        words = src.bitcast(F32)[:, 2 * P * c + u : 2 * P * (c + 1) : 2]
+                        words = values(m, j).bitcast(F32)[:, 2 * P * c + u : 2 * P * (c + 1) : 2]
                     nc.tensor.transpose(bank[:, u, c, :], words, ident[:])
             banks[m, j] = bank
 
-        def new_grouped(m):
+        def slots(m, j):
             if m not in grouped:
                 grouped[m] = work.tile([P, 2 * PASSES, K_PASS], BF16, name="grouped", align_bytes=64, bufs=4)
+            if m == 0:
+                return grouped[m][:, 2 * j : 2 * j + 2, :]
+            if j == HOT:
+                return grouped[m][:, 0 : 2 * PASSES : 2 * PASSES - 1, :]
+            return grouped[m][:, 2 * j + 1 : 2 * j + 3, :]
 
-        def move_hot(m):
-            new_grouped(m)
+        def move(m, j):
             nc.scalar.copy(
-                out=(grouped[m][:, 0 : 2 * PASSES : 2 * PASSES - 1, :] if m > 0 else grouped[m][:, 2 * REST :, :]).bitcast(F32).rearrange("p c (n u) -> p c n u", u=2),
-                in_=banks[m, REST][:].rearrange("p u c n -> p c n u"),
+                out=slots(m, j).bitcast(F32).rearrange("p c (n u) -> p c n u", u=2),
+                in_=banks[m, j][:].rearrange("p u c n -> p c n u"),
             )
-            free.append(tag_of["turned", m, REST])
+            release(("turned", m, j))
 
         def product(m, j):
             c0 = 2 * j % REST
-            new_grouped(m)
             nc.vector.tensor_tensor(
-                out=grouped[m][:, 2 * j + min(m, 1) : 2 * j + 2 + min(m, 1), :].rearrange("p c (n u e) -> p c n u e", u=2, e=2),
+                out=slots(m, j).rearrange("p c (n u e) -> p c n u e", u=2, e=2),
                 in0=banks[m, j][:].rearrange("p u c n -> p (u c n)").bitcast(BF16).rearrange("p (u c n e) -> p c n u e", u=2, c=2, e=2),
                 in1=channel_scale[:, c0 : c0 + 2, :].unsqueeze(2).to_broadcast([P, 2, P, PACK]).rearrange("p c n (u e) -> p c n u e", u=2),
                 op=MULT,
             )
-            free.append(tag_of["turned", m, j])
+            release(("turned", m, j))
 
         def quantise_dy(s):
             m, i = divmod(s, 2)
@@ -270,21 +245,12 @@ def tile_lora_down_gradient_s3_kernel(
                 in_=grouped[m][:, PASSES * i : PASSES * (i + 1), :].rearrange("p c k -> p (c k)"),
             )
 
-        def quantise_pair(m):
-            codes = work.tile([P, 2 * PASSES * P], U32, name="pair_codes", align_bytes=64, bufs=2)
-            scales = work.tile([P, 2 * PASSES * P], U8, name="pair_scales", align_bytes=64, bufs=2)
-            nc.vector.quantize_mx(out=codes[:].bitcast(FP8X4), scales=scales[:], in_=grouped[m][:].rearrange("p c k -> p (c k)"))
-            for i in range(2):
-                dy_codes[2 * m + i] = codes[:, PASSES * P * i : PASSES * P * (i + 1)]
-                dy_code_scales[2 * m + i] = scales[:, PASSES * P * i : PASSES * P * (i + 1)]
-
-        def stage1(s, passes=range(PASSES)):
+        def stage1(s, passes):
             m, i = divmod(s, 2)
             if 0 in passes:
-                tag_of["acc", s] = free.pop(0)
-                acc[s] = psum.tile([P, R], F32, name="acc", tag=tag_of["acc", s])
+                acc[s] = take(("acc", s), [P, R])
             for c in passes:
-                is_hot = c == REST
+                is_hot = c == HOT
                 if m == 0:
                     slot = 2 * REST + i if is_hot else REST * i + c
                 else:
@@ -302,39 +268,41 @@ def tile_lora_down_gradient_s3_kernel(
 
         def weigh_tokens(s):
             g, t = divmod(s, PHASES)
-            if s == 0:
-                nc.scalar.copy(out=token_weight[:], in_=token_weight_bf[:])
             if t == 0:
                 sums[g] = work.tile([P, PHASES, R], F32, name="sums", align_bytes=64, bufs=2)
             nc.scalar.activation(out=sums[g][:, t, :], in_=acc[s][:], func=COPY, scale=token_weight[:, s : s + 1])
-            free.append(tag_of["acc", s])
+            release(("acc", s))
 
-        def weigh_ranks(g, r0, r1, t0, t1, dst):
-            n = t1 - t0
+        def weigh_ranks(g, h, dst):
+            ranks = slice(HALF * h, HALF * (h + 1))
             nc.gpsimd.tensor_tensor(
-                out=dst.rearrange("p (c i t) -> p c t i", i=4, t=PHASES)[:, :, t0:t1, :],
-                in0=sums[g][:, t0:t1, r0:r1].rearrange("p t (c i) -> p c t i", i=4),
-                in1=lam_all[:, r0:r1].rearrange("p (c i) -> p c i", i=4).unsqueeze(2).to_broadcast([P, (r1 - r0) // 4, n, 4]),
+                out=dst.rearrange("p (c i t) -> p c t i", i=4, t=PHASES),
+                in0=sums[g][:, :, ranks].rearrange("p t (c i) -> p c t i", i=4),
+                in1=lam_all[:, ranks].rearrange("p (c i) -> p c i", i=4).unsqueeze(2).to_broadcast([P, HALF // 4, PHASES, 4]),
                 op=MULT,
             )
 
-        def quantise_g(g, r0, r1, src):
-            nc.vector.quantize_mx(out=g_codes[g][:, r0:r1].bitcast(FP8X4), scales=g_scales[g][:, r0:r1], in_=src)
+        def quantise_g(g, h, src):
+            ranks = slice(HALF * h, HALF * (h + 1))
+            nc.vector.quantize_mx(out=g_codes[g][:, ranks].bitcast(FP8X4), scales=g_scales[g][:, ranks], in_=src)
 
         def weigh_last(s):
             nc.vector.scalar_tensor_tensor(
                 out=last_planes[:, s % PHASES, :], in0=acc[s][:], scalar=token_weight[:, s : s + 1], in1=lam_all[:], op0=MULT, op1=MULT
             )
-            free.append(tag_of["acc", s])
+            release(("acc", s))
 
         def interleave_last(copy, r0, r1):
             copy(
-                out=last_grouped[:, PHASES * r0 : PHASES * r1].rearrange("p (c i t) -> p c t i", i=4, t=PHASES),
+                out=b_grouped[:, PHASES * r0 : PHASES * r1].rearrange("p (c i t) -> p c t i", i=4, t=PHASES),
                 in_=last_planes[:, :, r0:r1].rearrange("p t (c i) -> p c t i", i=4),
             )
 
-        def stage2(bank, d, groups, first=0, final=GROUPS - 1):
-            for g in groups:
+        def just_read(m, i):
+            return grouped[m][:, PASSES + 2 * i : PASSES + 2 * (i + 1), :].rearrange("p c k -> p (c k)")
+
+        def stage2(bank, d, g0, g1, first, final):
+            for g in range(g0, g1):
                 nc.tensor.matmul_mx(
                     out=bank[:],
                     lhsT=x_words_sb[g][:, 2 * P * d : 2 * P * (d + 1)].bitcast(FP4X4),
@@ -345,62 +313,32 @@ def tile_lora_down_gradient_s3_kernel(
                     stop=(g == final),
                 )
 
-        def second_half(m):
-            return grouped[m][:, PASSES:, :].rearrange("p c k -> p (c k)")
-
-        last = GROUPS - 1
         held = {}
         added = {}
         parked = {}
+        result = {}
         pending = []
 
-        def hold(upto):
-            d = len(held)
-            tag_of["held", d] = free.pop(0)
-            held[d] = psum.tile([P, R], F32, name="held", tag=tag_of["held", d])
-            added[d] = 0
-            add(d, upto)
-
-        def add(d, upto):
-            stage2(held[d], d, range(added[d], upto))
+        def hold(d, upto):
+            if d not in held:
+                held[d] = take(("held", d), [P, R])
+                added[d] = 0
+            stage2(held[d], d, added[d], upto, 0, GROUPS - 1)
             added[d] = upto
 
         def park(count):
             d = OUT_TILES - 1 - len(parked)
-            tag = free.pop(0)
-            bank = psum.tile([P, R], F32, name="early", tag=tag)
-            stage2(bank, d, range(count), 0, count - 1)
+            bank = take(("early", d), [P, R])
+            stage2(bank, d, 0, count, 0, count - 1)
             parked[d] = count
-            pending.append((d, bank, tag))
+            pending.append((d, bank))
 
         def empty_parked():
             while pending:
-                d, bank, tag = pending.pop(0)
+                d, bank = pending.pop(0)
                 result[d] = keep.tile([P, R], F32, name="parked_%d" % d, align_bytes=64)
                 nc.scalar.copy(out=result[d][:], in_=bank[:])
-                free.append(tag)
-
-        sorts = list(SORT_S)
-
-        def sort_next(m):
-            if sorts and sorts[0][0] in widened and sorts[0][0] <= m:
-                sort_words(*sorts.pop(0), nc.scalar.copy)
-
-        turned = [0]
-
-        def turn_upto(n1):
-            for n_ in range(turned[0], n1):
-                if not (n_ % REST == 0 and n_ // REST in OFF):
-                    turn_bank(n_ // REST, n_ % REST)
-            turned[0] = max(n1, turned[0])
-
-        done = [0]
-
-        def products(n1):
-            for n_ in range(done[0], n1):
-                if not (n_ % REST == 0 and n_ // REST in OFF):
-                    product(*divmod(n_, REST))
-            done[0] = max(n1, done[0])
+                release(("early", d))
 
         widened[0] = work.tile([P, 2 * C], BF16, name="widened", align_bytes=64, bufs=3)
         nc.scalar.copy(out=widened[0][:, 0:K_PASS], in_=first_bytes[:].bitcast(FP8))
@@ -408,171 +346,173 @@ def tile_lora_down_gradient_s3_kernel(
         nc.scalar.copy(out=widened[0][:, BANK:C], in_=other_bytes[:, K_PASS:].bitcast(FP8))
         nc.scalar.copy(out=widened[0][:, C : 2 * BANK], in_=second_tile[:, 0:K_PASS].bitcast(FP8))
         nc.scalar.copy(out=widened[0][:, 2 * BANK :], in_=second_tile[:, K_PASS:].bitcast(FP8))
-        b_grouped = last_grouped[:]
         nc.gpsimd.tensor_scalar(
-            out=b_grouped.rearrange("p (n t) -> p n t", t=PACK),
+            out=b_grouped[:].rearrange("p (n t) -> p n t", t=PACK),
             in0=b_raw[:].rearrange("p t n -> p n t"),
             scalar1=1.0,
             scalar2=0.0,
             op0=MULT,
             op1=ADD,
         )
-        turn_upto(3)
-        spread_scales()
+        for j in range(REST):
+            turn(0, j)
+        for c in range(2):
+            spread_scales(c)
         for j in range(REST):
             widen(1, j, j + 1)
-        turn_bank(0, REST)
-        turn_bank(1, REST)
-        products(3)
-        move_hot(0)
-        move_hot(1)
-        turn_upto(6)
-        empty_spread()
+        turn(0, HOT)
+        turn(1, HOT)
+        for j in range(REST):
+            product(0, j)
+        move(0, HOT)
+        move(1, HOT)
+        for j in range(REST):
+            turn(1, j)
+        for c in range(2):
+            empty_spread(c)
         quantise_dy(0)
-        nc.vector.quantize_mx(out=b_hot_codes[:].bitcast(FP8X4), scales=b_hot_scales[:], in_=b_grouped)
+        nc.vector.quantize_mx(out=b_hot_codes[:].bitcast(FP8X4), scales=b_hot_scales[:], in_=b_grouped[:])
         quantise_dy(1)
         widen(2, 0, 1)
-        if 2 in OFF:
-            scale_first(2, second_half(0)[:, 0:BANK])
-        widen(2, 1, 3)
-        if W30:
-            widen(3, 0, 1)
-        stage1(0, range(REST))
-        stage1(1, range(REST))
-        for s in range(2):
-            stage1(s, (REST,))
-        products(4)
-        weigh_tokens(0)
-        products(5)
-        weigh_tokens(1)
-        turn_bank(2, REST)
-        turn_upto(8)
-        products(6)
-        turn_upto(9)
-        if 2 in OFF:
-            turn_bank(2, 0)
-        move_hot(2)
-        if not W30:
-            widen(3, 0, 1)
-        widen(3, 1, 3)
-        if 2 in OFF:
-            move_first(2)
-        quantise_dy(2)
-        quantise_dy(3)
-        g_in = {}
-        for m in range(2, PAIRS):
-            ready = (m - (2 if LAG2 else 3)) // 2
-            g, h = divmod(m - (2 if LAG2 else 3), 2)
-            if LAG2 and h == 0:
-                g_in[g] = second_half(m - 1)[:, 0 : PHASES * (R - LATE)]
-                weigh_ranks(g, 0, R - LATE, 0, 2, g_in[g])
-            if LAG2 and h == 1:
-                g_late = second_half(m - 1)[:, 0 : PHASES * LATE]
-                weigh_ranks(g, R - LATE, R, 0, PHASES, g_late)
-                weigh_ranks(g, 0, R - LATE, 2, PHASES, g_in[g])
-            if m >= 3 and not LAG2:
-                r0, r1 = ((0, CUT), (CUT, R))[h] if g == 0 else (HALF * h, HALF * (h + 1))
-                g_in[g, h] = second_half(m - 1)[:, 0 : PHASES * (r1 - r0)]
-                weigh_ranks(g, r0, r1, 0, PHASES, g_in[g, h])
-            if m in SORT_G:
-                for i, n in enumerate(SORT_G[m]):
-                    sort_hot(n, second_half(m - 1)[:, BANK * (1 - i) : BANK * (2 - i)])
-            if m + 1 in OFF:
-                scale_first(m + 1, second_half(m - 1)[:, BANK:])
+
+        last = GROUPS - 1
+        ready = 0
+        jobs = []
+        for n in range(3, PAIRS):
+            jobs.extend(("widen", n, j) for j in range(REST))
+            jobs.extend(("sort", n, j) for j in SORTS.get(n, ()))
+
+        def spare(count):
+            for i in range(min(count, len(jobs))):
+                kind, n, j = jobs.pop(0)
+                if kind == "widen":
+                    widen(n, j, j + 1)
+                else:
+                    assert (n, j) not in banks
+                    sort_words(n, j, nc.scalar.copy)
+
+        for m in range(1, PAIRS):
+            mine = [j for j in range(REST) if not (j == 0 and m in ON_GPSIMD)]
+            ahead = [j for j in range(REST) if not (j == 0 and m + 1 in ON_GPSIMD)] if m + 1 < PAIRS else []
+            g, h = divmod(m - 3, 2)
             before, after = PARKS.get(m, (0, 0))
-            stage1(2 * m - 2)
-            stage1(2 * m - 1)
+            if m in VSORT:
+                sort_words(*VSORT[m], nc.vector.tensor_copy)
+            if m + 1 in ON_GPSIMD:
+                scale_first(m + 1, just_read(m - 1, 0))
+            if m >= 3:
+                weigh_ranks(g, h, just_read(m - 1, 0))
+            for i, (pair, j) in enumerate(GSORTS.get(m, ())):
+                if m < 3 and i == 0 and m + 1 not in ON_GPSIMD:
+                    sort_into(pair, j, just_read(m - 1, 0))
+                else:
+                    sort_words(pair, j, nc.gpsimd.tensor_copy)
+            if m == 1:
+                widen(2, 1, REST)
+                nc.scalar.copy(out=token_weight[:], in_=token_weight_bf[:])
+                stage1(0, range(REST))
+                stage1(1, range(REST))
+                stage1(0, (HOT,))
+                stage1(1, (HOT,))
+            else:
+                stage1(2 * m - 2, range(PASSES))
+                stage1(2 * m - 1, range(PASSES))
+            product(m, mine[0])
             if ready > 0:
-                for d in held:
-                    add(d, ready)
-                while len(held) < HOLD.get(m, 0):
-                    hold(ready)
+                for d in range(HELD):
+                    hold(d, ready)
                 for i in range(before):
                     park(ready)
-            for i in range(2):
-                products(REST * m + i + 1)
-                if m + 1 < PAIRS:
+            for j in mine[1:]:
+                product(m, j)
+            if m + 1 < PAIRS:
+                for i in range(2):
+                    spare(SLOTS[m][i])
                     weigh_tokens(2 * m - 2 + i)
-                    if i < SLOTS.get(m, 0):
-                        sort_next(m + 2)
             empty_parked()
             if m + 1 < PAIRS:
-                turn_bank(m + 1, REST)
-                turn_upto(REST * (m + 1) + 2)
-                products(REST * (m + 1))
-                turn_upto(min(REST * (m + 2) + AHEAD[m], REST * PAIRS))
-                if m + 1 in OFF:
-                    turn_bank(m + 1, 0)
-                move_hot(m + 1)
-                if m + 1 in OFF:
-                    move_first(m + 1)
-            for n in range(len(widened), min(m + (4 if m >= EXTRA else 3), PAIRS)):
-                widen(n)
-            products(REST * (m + 1))
+                turn(m + 1, HOT)
+                for j in ahead[:2]:
+                    turn(m + 1, j)
+                move(m + 1, HOT)
+            for j in ahead[2:]:
+                turn(m + 1, j)
+            if m + 1 < PAIRS:
+                spare(SLOTS[m][2])
+            if m + 1 in ON_GPSIMD:
+                turn(m + 1, 0)
+                move(m + 1, 0)
+            if m + 1 < PAIRS:
+                spare(SLOTS[m][3])
             if m >= 3 and h == 1:
-                for q0, q1 in [(r0, r1)] if r1 - r0 in (P, HALF) else [(r0, r0 + P), (r0 + P, r1)]:
-                    quantise_g(g, q0, q1, g_in[g, h][:, PHASES * (q0 - r0) : PHASES * (q1 - r0)])
-                ready = (m - 2) // 2
-            if ready > 0:
-                for d in held:
-                    add(d, ready)
-                while len(held) < HOLD_AFTER.get(m, 0):
-                    hold(ready)
+                quantise_g(g, h, just_read(m - 1, 0))
+                ready += 1
+                for d in range(HELD):
+                    hold(d, ready)
             for i in range(after):
                 park(ready)
                 empty_parked()
             if m + 1 == PAIRS:
-                for i in range(LAST_HOLD):
-                    hold(ready)
-            if m in WHOLE:
-                quantise_pair(m)
-            else:
-                quantise_dy(2 * m)
-                quantise_dy(2 * m + 1)
+                for d in range(HELD, HELD + LAST_HOLD):
+                    hold(d, ready)
+            quantise_dy(2 * m)
+            quantise_dy(2 * m + 1)
             if m >= 3 and h == 0:
-                for q0, q1 in [(r0, r1)] if r1 - r0 in (P, HALF) else [(r0, r0 + P), (r0 + P, r1)]:
-                    quantise_g(g, q0, q1, g_in[g, h][:, PHASES * (q0 - r0) : PHASES * (q1 - r0)])
-            if LAG2 and h == 1:
-                quantise_g(g, 0, HALF, g_in[g][:, 0 : PHASES * HALF])
-                quantise_g(g, HALF, 3 * P, g_in[g][:, PHASES * HALF : PHASES * 3 * P])
-                quantise_g(g, 3 * P, R - LATE, g_in[g][:, PHASES * 3 * P :])
-                quantise_g(g, R - LATE, R, g_late)
+                quantise_g(g, h, just_read(m - 1, 0))
 
-        if not LAG2:
-            g_in[last - 1, 1] = second_half(PAIRS - 1)[:, 0 : PHASES * HALF]
-            weigh_ranks(last - 1, HALF, R, 0, PHASES, g_in[last - 1, 1])
+        assert not jobs
+        weigh_ranks(last - 1, 1, just_read(PAIRS - 1, 0))
         for s in (TILES - 2, TILES - 1):
-            stage1(s)
+            stage1(s, range(PASSES))
         weigh_last(TILES - 4)
         weigh_last(TILES - 3)
         while free:
-            hold(last - 1)
+            hold(len(held), last - 1)
         weigh_last(TILES - 2)
         weigh_last(TILES - 1)
-        if not LAG2:
-            quantise_g(last - 1, HALF, R, g_in[last - 1, 1])
-        for d in list(held)[:EARLY]:
-            add(d, last)
-        interleave_last(nc.scalar.copy, 3 * P, R)
+        quantise_g(last - 1, 1, just_read(PAIRS - 1, 0))
+        for d in range(EARLY):
+            hold(d, last)
+        interleave_last(nc.scalar.copy, R - SCALAR_RANKS, R)
         interleave_last(nc.vector.tensor_copy, 0, HALF)
-        interleave_last(nc.vector.tensor_copy, HALF, 3 * P)
-        quantise_g(last, 0, HALF, last_grouped[:, 0 : PHASES * HALF])
-        quantise_g(last, HALF, R, last_grouped[:, PHASES * HALF :])
+        interleave_last(nc.vector.tensor_copy, HALF, R - SCALAR_RANKS)
+        for h in range(2):
+            quantise_g(last, h, b_grouped[:, PHASES * HALF * h : PHASES * HALF * (h + 1)])
 
-        order = list(held) + list(range(OUT_TILES - 1, len(held) - 1, -1))
-        for i, d in enumerate(order):
+        plain = [d for d in range(len(held), OUT_TILES) if d not in parked]
+        order = list(parked) + plain
+        if TURNS:
+            order = [d for both in zip(parked, plain) for d in both] + list(parked)[len(plain) :] + plain[len(parked) :]
+        for d in list(held) + order:
+            if SPLIT and d == order[-1]:
+                for h, copy in enumerate((nc.scalar.copy, nc.vector.tensor_copy)):
+                    ranks = slice(HALF * h, HALF * (h + 1))
+                    bank = take(("end", h), [P, HALF])
+                    for g in range(GROUPS):
+                        nc.tensor.matmul_mx(
+                            out=bank[:],
+                            lhsT=x_words_sb[g][:, 2 * P * d : 2 * P * (d + 1)].bitcast(FP4X4),
+                            lhsT_scale=x_scales_sb[:, g, P * d : P * (d + 1)],
+                            rhs=g_codes[g][:, ranks].bitcast(FP8X4),
+                            rhs_scale=g_scales[g][:, ranks],
+                            start=(g == 0),
+                            stop=(g == last),
+                        )
+                    part = work.tile([P, HALF], F32, name="end", align_bytes=64, bufs=2)
+                    copy(out=part[:], in_=bank[:])
+                    nc.sync.dma_start(out=out[P * d : P * (d + 1), ranks], in_=part[:])
+                continue
             if d in held:
-                add(d, GROUPS)
-                bank = held[d]
-                tag = tag_of["held", d]
+                hold(d, GROUPS)
+                bank, key = held[d], ("held", d)
             else:
-                tag = free.pop(0)
-                bank = psum.tile([P, R], F32, name="late", tag=tag)
-                stage2(bank, d, range(parked.get(d, 0), GROUPS), parked.get(d, 0))
+                key = ("late", d)
+                bank = take(key, [P, R])
+                stage2(bank, d, parked.get(d, 0), GROUPS, parked.get(d, 0), last)
             if d in parked:
                 nc.vector.tensor_tensor(out=result[d][:], in0=bank[:], in1=result[d][:], op=ADD)
             else:
                 result[d] = work.tile([P, R], F32, name="result", align_bytes=64, bufs=8)
                 (nc.scalar.copy, nc.vector.tensor_copy)[d % 2 if d in held else 0](out=result[d][:], in_=bank[:])
-            free.append(tag)
+            release(key)
             nc.sync.dma_start(out=out[P * d : P * (d + 1), :], in_=result[d][:])

@@ -39,6 +39,7 @@ PARKS = {5: (1, 2), 6: (1, 1), 7: (1, 1)}
 TURNS = 0
 SPLIT = 0
 VSORT = {2: (3, HOT), 3: (4, HOT)}
+B_CUT = 512
 HELD = 2
 LAST_HOLD = 1
 EARLY = 5
@@ -74,6 +75,10 @@ def tile_lora_down_gradient_s3_kernel(
         last_planes = keep.tile([P, PHASES, R], BF16, name="last_planes", align_bytes=64)
         spread = keep.tile([P, 2, 2, P, 2], F32, name="spread", align_bytes=64)
 
+        lam_row = keep.tile([P, R], BF16, name="lam_row", align_bytes=64)
+        ones = keep.tile([P, P], BF16, name="ones", align_bytes=64)
+        nc.vector.memset(lam_row[:], 0.0)
+        nc.vector.memset(ones[:], 1.0)
         nc.vector.memset(b_scales_sb[:].rearrange("p g n -> p (g n)").bitcast(I32), 0)
         nc.vector.memset(x_scales_sb[:].rearrange("p g n -> p (g n)").bitcast(I32), 0)
         make_identity(nc, ident[:])
@@ -107,6 +112,7 @@ def tile_lora_down_gradient_s3_kernel(
         nc.sync.dma_start(out=first_bytes[:], in_=bytes_hbm[0][:, 0:K_PASS])
         other_bytes = keep.tile([P, C - K_PASS], U8, name="other_bytes", align_bytes=64)
         nc.sync.dma_start(out=other_bytes[:], in_=bytes_hbm[0][:, K_PASS:C])
+        nc.sync.dma_start(out=lam_row[0:1, :], in_=lam.rearrange("(o r) -> o r", o=1))
         second_tile = keep.tile([P, C], U8, name="second_tile", align_bytes=64)
         nc.sync.dma_start(out=second_tile[:], in_=bytes_hbm[0][:, C : 2 * C])
         nc.sync.dma_start(
@@ -127,14 +133,14 @@ def tile_lora_down_gradient_s3_kernel(
         load_bytes(3)
         load_hot(3, 1)
         load_bytes(4)
-        nc.sync.dma_start(out=lam_all[:], in_=lam.partition_broadcast(P))
         load_hot(4, 2)
         load_bytes(5)
         load_bytes(6)
-        load_hot(6, 2)
-        load_bytes(7)
         load_scale_rows(x_scales_sb, x_scales)
-        for g in range(GROUPS):
+        nc.sync.dma_start(out=x_words_sb[0][:].bitcast(I32), in_=x_words[0].bitcast(I32))
+        load_bytes(7)
+        load_hot(6, 2)
+        for g in range(1, GROUPS):
             nc.sync.dma_start(out=x_words_sb[g][:].bitcast(I32), in_=x_words[g].bitcast(I32))
 
         nc.vector.tensor_copy(out=channel_scale[:, REST, :], in_=channel_scale[:, 0, :])
@@ -347,17 +353,27 @@ def tile_lora_down_gradient_s3_kernel(
         nc.scalar.copy(out=widened[0][:, C : 2 * BANK], in_=second_tile[:, 0:K_PASS].bitcast(FP8))
         nc.scalar.copy(out=widened[0][:, 2 * BANK :], in_=second_tile[:, K_PASS:].bitcast(FP8))
         nc.gpsimd.tensor_scalar(
-            out=b_grouped[:].rearrange("p (n t) -> p n t", t=PACK),
-            in0=b_raw[:].rearrange("p t n -> p n t"),
+            out=b_grouped[:, 0 : PACK * B_CUT].rearrange("p (n t) -> p n t", t=PACK),
+            in0=b_raw[:, :, 0:B_CUT].rearrange("p t n -> p n t"),
             scalar1=1.0,
             scalar2=0.0,
             op0=MULT,
             op1=ADD,
         )
-        for j in range(REST):
-            turn(0, j)
+        turn(0, 0)
+        turn(0, 1)
+        lam_bank = take(("lam", 0), [P, R])
+        nc.tensor.matmul(lam_bank[:], lhsT=ones[:], rhs=lam_row[:], start=True, stop=True)
+        turn(0, 2)
         for c in range(2):
             spread_scales(c)
+        nc.scalar.copy(out=lam_all[:], in_=lam_bank[:])
+        release(("lam", 0))
+        if B_CUT < R:
+            nc.scalar.copy(
+                out=b_grouped[:, PACK * B_CUT :].rearrange("p (c i t) -> p c t i", i=4, t=PACK),
+                in_=b_raw[:, :, B_CUT:].rearrange("p t (c i) -> p c t i", i=4),
+            )
         for j in range(REST):
             widen(1, j, j + 1)
         turn(0, HOT)

@@ -22,27 +22,22 @@ P = 128
 PACK = 4
 K_PASS = P * PACK
 GROUPS = T // K_PASS
-PHASES = PACK
-TILES = GROUPS * PHASES
+TILES = GROUPS * PACK
+PAIRS = TILES // 2
 REST = C // K_PASS
 PASSES = REST + 1
-PAIRS = TILES // 2
+HOT = REST
+BANK = 2 * K_PASS
 OUT_TILES = D // P
 HALF = R // 2
-BANK = 2 * K_PASS
-HOT = REST
-ON_GPSIMD = (2, 3)
-SORTS = {7: (HOT, 0, 1, 2)}
-GSORTS = {}
-SLOTS = {1: (0, 0, 1, 2), 2: (1, 0, 0, 2), 3: (1, 0, 0, 3), 4: (1, 0, 0, 3), 5: (1, 0, 0, 2), 6: (2, 0, 0, 0)}
-PARKS = {5: (1, 2), 6: (1, 1), 7: (1, 1)}
-TURNS = 0
-SPLIT = 0
-VSORT = {2: (3, HOT), 3: (4, HOT)}
-B_CUT = 512
+LAST = GROUPS - 1
+
+FIRST_LAM_STEP = 3
+ON_GPSIMD = range(2, FIRST_LAM_STEP + 1)
 HELD = 2
-LAST_HOLD = 1
-EARLY = 5
+SPARE_JOBS = 3
+FIRST_PARK_STEP = 5
+AHEAD_OF_LAST = 5
 SCALAR_RANKS = 128
 
 
@@ -61,9 +56,9 @@ def tile_lora_down_gradient_s3_kernel(
         token_weight_bf = keep.tile([P, TILES], BF16, name="token_weight_bf", align_bytes=64)
         token_weight = keep.tile([P, TILES], F32, name="token_weight", align_bytes=64)
         lam_all = keep.tile([P, R], BF16, name="lam_all", align_bytes=64)
-        channel_scale = keep.tile([P, PASSES, PACK], F32, name="channel_scale", align_bytes=64)
+        channel_scale = keep.tile([P, REST + 1, PACK], F32, name="channel_scale", align_bytes=64)
         b_raw = keep.tile([P, PACK, R], BF16, name="b_raw", align_bytes=64)
-        b_grouped = keep.tile([P, R * PACK], BF16, name="b_grouped", align_bytes=64)
+        interleaved = keep.tile([P, R * PACK], BF16, name="interleaved", align_bytes=64)
         b_hot_codes = keep.tile([P, R], U32, name="b_hot_codes", align_bytes=64)
         b_hot_scales = keep.tile([P, R], U8, name="b_hot_scales", align_bytes=64)
         b_words_sb = keep.tile([P, REST, 2 * R], U8, name="b_words_sb", align_bytes=64)
@@ -72,31 +67,30 @@ def tile_lora_down_gradient_s3_kernel(
         x_scales_sb = keep.tile([P, GROUPS, D], U8, name="x_scales_sb", align_bytes=64)
         g_codes = [keep.tile([P, R], U32, name="g_codes_%d" % g, align_bytes=64) for g in range(GROUPS)]
         g_scales = [keep.tile([P, R], U8, name="g_scales_%d" % g, align_bytes=64) for g in range(GROUPS)]
-        last_planes = keep.tile([P, PHASES, R], BF16, name="last_planes", align_bytes=64)
+        last_tiles = keep.tile([P, PACK, R], BF16, name="last_tiles", align_bytes=64)
         spread = keep.tile([P, 2, 2, P, 2], F32, name="spread", align_bytes=64)
-
         lam_row = keep.tile([P, R], BF16, name="lam_row", align_bytes=64)
         ones = keep.tile([P, P], BF16, name="ones", align_bytes=64)
+
         nc.vector.memset(lam_row[:], 0.0)
         nc.vector.memset(ones[:], 1.0)
-        nc.vector.memset(b_scales_sb[:].rearrange("p g n -> p (g n)").bitcast(I32), 0)
+        nc.vector.memset(b_scales_sb[:].rearrange("p c n -> p (c n)").bitcast(I32), 0)
         nc.vector.memset(x_scales_sb[:].rearrange("p g n -> p (g n)").bitcast(I32), 0)
         make_identity(nc, ident[:])
 
-        bytes_hbm = dy_rest_bytes.rearrange("(g m t) k -> g m (t k)", m=P, t=PHASES)
-        hot_hbm = dy_hot.rearrange("(g m t) k -> g m (t k)", m=P, t=PHASES)
+        bytes_hbm = dy_rest_bytes.rearrange("(g m t) k -> g m (t k)", m=P, t=PACK)
+        hot_hbm = dy_hot.rearrange("(g m t) k -> g m (t k)", m=P, t=PACK)
         pair_bytes = {}
         hot = {}
 
         def load_bytes(m):
-            g, t = divmod(2 * m, PHASES)
-            tile = keep.tile([P, 2 * C], U8, name="rest_bytes_%d" % m, align_bytes=64)
-            nc.sync.dma_start(out=tile[:], in_=bytes_hbm[g][:, t * C : (t + 2) * C])
-            pair_bytes[m] = tile
+            g, t = divmod(2 * m, PACK)
+            pair_bytes[m] = keep.tile([P, 2 * C], U8, name="rest_bytes_%d" % m, align_bytes=64)
+            nc.sync.dma_start(out=pair_bytes[m][:], in_=bytes_hbm[g][:, t * C : (t + 2) * C])
 
         def load_hot(m, count):
-            g, t = divmod(2 * m, PHASES)
-            tile = keep.tile([P, 2 * count * H], BF16, name="hot_%d" % m, align_bytes=64)
+            g, t = divmod(2 * m, PACK)
+            tile = keep.tile([P, count * BANK], BF16, name="hot_%d" % m, align_bytes=64)
             nc.sync.dma_start(out=tile[:], in_=hot_hbm[g][:, t * H : (t + 2 * count) * H])
             for i in range(count):
                 hot[m + i] = tile[:, BANK * i : BANK * (i + 1)]
@@ -108,13 +102,16 @@ def tile_lora_down_gradient_s3_kernel(
                     in_=hbm[:, 4 * q : 4 * q + 4, :].rearrange("g q n -> q g n").bitcast(I32),
                 )
 
+        def load_x(g):
+            nc.sync.dma_start(out=x_words_sb[g][:].bitcast(I32), in_=x_words[g].bitcast(I32))
+
         first_bytes = keep.tile([P, K_PASS], U8, name="first_bytes", align_bytes=64)
-        nc.sync.dma_start(out=first_bytes[:], in_=bytes_hbm[0][:, 0:K_PASS])
         other_bytes = keep.tile([P, C - K_PASS], U8, name="other_bytes", align_bytes=64)
+        second_bytes = keep.tile([P, C], U8, name="second_bytes", align_bytes=64)
+        nc.sync.dma_start(out=first_bytes[:], in_=bytes_hbm[0][:, 0:K_PASS])
         nc.sync.dma_start(out=other_bytes[:], in_=bytes_hbm[0][:, K_PASS:C])
         nc.sync.dma_start(out=lam_row[0:1, :], in_=lam.rearrange("(o r) -> o r", o=1))
-        second_tile = keep.tile([P, C], U8, name="second_tile", align_bytes=64)
-        nc.sync.dma_start(out=second_tile[:], in_=bytes_hbm[0][:, C : 2 * C])
+        nc.sync.dma_start(out=second_bytes[:], in_=bytes_hbm[0][:, C : 2 * C])
         nc.sync.dma_start(
             out=channel_scale[:, 0:REST, :], in_=dy_rest_scale.rearrange("o (c p t) -> p (o c) t", p=P, t=PACK)
         )
@@ -122,12 +119,12 @@ def tile_lora_down_gradient_s3_kernel(
         load_bytes(1)
         load_hot(0, 1)
         load_hot(1, 1)
-        nc.sync.dma_start(out=b_words_sb[:].bitcast(I32), in_=b_rest_words.rearrange("g p b -> p g b").bitcast(I32))
+        nc.sync.dma_start(out=b_words_sb[:].bitcast(I32), in_=b_rest_words.rearrange("c p b -> p c b").bitcast(I32))
         load_scale_rows(b_scales_sb, b_rest_scales)
         load_bytes(2)
         nc.sync.dma_start(
-            out=token_weight_bf[:].rearrange("m (g t) -> m g t", t=PHASES),
-            in_=token_w.rearrange("(g m t) -> m g t", m=P, t=PHASES),
+            out=token_weight_bf[:].rearrange("m (g t) -> m g t", t=PACK),
+            in_=token_w.rearrange("(g m t) -> m g t", m=P, t=PACK),
         )
         load_hot(2, 1)
         load_bytes(3)
@@ -137,24 +134,14 @@ def tile_lora_down_gradient_s3_kernel(
         load_bytes(5)
         load_bytes(6)
         load_scale_rows(x_scales_sb, x_scales)
-        nc.sync.dma_start(out=x_words_sb[0][:].bitcast(I32), in_=x_words[0].bitcast(I32))
+        load_x(0)
         load_bytes(7)
         load_hot(6, 2)
         for g in range(1, GROUPS):
-            nc.sync.dma_start(out=x_words_sb[g][:].bitcast(I32), in_=x_words[g].bitcast(I32))
-
-        nc.vector.tensor_copy(out=channel_scale[:, REST, :], in_=channel_scale[:, 0, :])
+            load_x(g)
 
         free = ["bank_%d" % i for i in range(8)]
         tag_of = {}
-        widened = {}
-        sorted_words = {}
-        banks = {}
-        grouped = {}
-        dy_codes = {}
-        dy_code_scales = {}
-        acc = {}
-        sums = {}
 
         def take(key, shape):
             tag_of[key] = free.pop(0)
@@ -163,10 +150,18 @@ def tile_lora_down_gradient_s3_kernel(
         def release(key):
             free.append(tag_of[key])
 
+        widened = {}
+        sorted_words = {}
+        turned = {}
+        grouped = {}
+        dy_codes = {}
+        dy_scales = {}
+
         def widen(m, j0, j1):
             if j0 == 0:
-                widened[m] = work.tile([P, 2 * C], BF16, name="widened", align_bytes=64, bufs=3)
-            nc.scalar.copy(out=widened[m][:, BANK * j0 : BANK * j1], in_=pair_bytes[m][:, BANK * j0 : BANK * j1].bitcast(FP8))
+                widened[m] = work.tile([P, 2 * C], BF16, name="widened", align_bytes=64)
+            cols = slice(BANK * j0, BANK * j1)
+            nc.scalar.copy(out=widened[m][:, cols], in_=pair_bytes[m][:, cols].bitcast(FP8))
 
         def values(m, j):
             return hot[m] if j == HOT else widened[m][:, BANK * j : BANK * (j + 1)]
@@ -179,23 +174,7 @@ def tile_lora_down_gradient_s3_kernel(
             )
             sorted_words[m, j] = tile[:]
 
-        def sort_into(m, j, dst):
-            nc.gpsimd.tensor_copy(
-                out=dst.bitcast(F32).rearrange("p (u n) -> p u n", u=2),
-                in_=values(m, j).bitcast(F32).rearrange("p (n u) -> p u n", u=2),
-            )
-            sorted_words[m, j] = dst.bitcast(F32)
-
-        def spread_scales(c):
-            banks["spread", c] = take(("spreading", c), [P, PACK, P])
-            for t in range(PACK):
-                nc.tensor.transpose(banks["spread", c][:, t, :], channel_scale[:, c, t : t + 1].to_broadcast([P, P]), ident[:])
-
-        def empty_spread(c):
-            nc.scalar.copy(out=spread[:, :, c, :, :], in_=banks["spread", c][:].rearrange("p (u e) n -> p u n e", u=2))
-            release(("spreading", c))
-
-        def scale_first(m, dst):
+        def scale_before_turning(m, dst):
             nc.gpsimd.tensor_tensor(
                 out=dst.rearrange("p (u n e) -> p u n e", u=2, e=2),
                 in0=values(m, 0).rearrange("p (n u e) -> p u n e", u=2, e=2),
@@ -205,110 +184,122 @@ def tile_lora_down_gradient_s3_kernel(
             sorted_words[m, 0] = dst.bitcast(F32)
 
         def turn(m, j):
-            bank = take(("turned", m, j), [P, 2, 2, P])
+            turned[m, j] = take(("turned", m, j), [P, 2, 2, P])
             for c in range(2):
                 for u in range(2):
                     if (m, j) in sorted_words:
                         words = sorted_words[m, j][:, P * (2 * u + c) : P * (2 * u + c + 1)]
                     else:
                         words = values(m, j).bitcast(F32)[:, 2 * P * c + u : 2 * P * (c + 1) : 2]
-                    nc.tensor.transpose(bank[:, u, c, :], words, ident[:])
-            banks[m, j] = bank
+                    nc.tensor.transpose(turned[m, j][:, u, c, :], words, ident[:])
 
-        def slots(m, j):
+        def place(m, i, c):
+            if m == 0:
+                return 2 * REST + i if c == HOT else REST * i + c
+            return (2 * PASSES - 1) * i if c == HOT else REST * i + c + 1
+
+        def places(m, j):
             if m not in grouped:
                 grouped[m] = work.tile([P, 2 * PASSES, K_PASS], BF16, name="grouped", align_bytes=64, bufs=4)
-            if m == 0:
-                return grouped[m][:, 2 * j : 2 * j + 2, :]
-            if j == HOT:
-                return grouped[m][:, 0 : 2 * PASSES : 2 * PASSES - 1, :]
-            return grouped[m][:, 2 * j + 1 : 2 * j + 3, :]
+            a, b = (place(m, 0, HOT), place(m, 1, HOT)) if j == HOT else (place(m, 0, 0) + 2 * j, place(m, 0, 0) + 2 * j + 1)
+            return grouped[m][:, a : b + 1 : b - a, :]
 
         def move(m, j):
             nc.scalar.copy(
-                out=slots(m, j).bitcast(F32).rearrange("p c (n u) -> p c n u", u=2),
-                in_=banks[m, j][:].rearrange("p u c n -> p c n u"),
+                out=places(m, j).bitcast(F32).rearrange("p c (n u) -> p c n u", u=2),
+                in_=turned[m, j][:].rearrange("p u c n -> p c n u"),
             )
             release(("turned", m, j))
 
         def product(m, j):
             c0 = 2 * j % REST
+            halves = turned[m, j][:].rearrange("p u c n -> p (u c n)").bitcast(BF16)
+            scales = channel_scale[:, c0 : c0 + 2, :].unsqueeze(2).to_broadcast([P, 2, P, PACK])
             nc.vector.tensor_tensor(
-                out=slots(m, j).rearrange("p c (n u e) -> p c n u e", u=2, e=2),
-                in0=banks[m, j][:].rearrange("p u c n -> p (u c n)").bitcast(BF16).rearrange("p (u c n e) -> p c n u e", u=2, c=2, e=2),
-                in1=channel_scale[:, c0 : c0 + 2, :].unsqueeze(2).to_broadcast([P, 2, P, PACK]).rearrange("p c n (u e) -> p c n u e", u=2),
+                out=places(m, j).rearrange("p c (n u e) -> p c n u e", u=2, e=2),
+                in0=halves.rearrange("p (u c n e) -> p c n u e", u=2, c=2, e=2),
+                in1=scales.rearrange("p c n (u e) -> p c n u e", u=2),
                 op=MULT,
             )
             release(("turned", m, j))
 
-        def quantise_dy(s):
-            m, i = divmod(s, 2)
-            dy_codes[s] = work.tile([P, PASSES * P], U32, name="dy_codes", align_bytes=64, bufs=4)
-            dy_code_scales[s] = work.tile([P, PASSES * P], U8, name="dy_code_scales", align_bytes=64, bufs=4)
+        def quantise_dy(m, i):
+            dy_codes[m, i] = work.tile([P, PASSES * P], U32, name="dy_codes", align_bytes=64, bufs=4)
+            dy_scales[m, i] = work.tile([P, PASSES * P], U8, name="dy_scales", align_bytes=64, bufs=4)
             nc.vector.quantize_mx(
-                out=dy_codes[s][:].bitcast(FP8X4),
-                scales=dy_code_scales[s][:],
+                out=dy_codes[m, i][:].bitcast(FP8X4),
+                scales=dy_scales[m, i][:],
                 in_=grouped[m][:, PASSES * i : PASSES * (i + 1), :].rearrange("p c k -> p (c k)"),
             )
+
+        def just_read(m):
+            return grouped[m][:, PASSES : PASSES + 2, :].rearrange("p c k -> p (c k)")
+
+        acc = {}
+        sums = {}
 
         def stage1(s, passes):
             m, i = divmod(s, 2)
             if 0 in passes:
                 acc[s] = take(("acc", s), [P, R])
             for c in passes:
-                is_hot = c == HOT
-                if m == 0:
-                    slot = 2 * REST + i if is_hot else REST * i + c
-                else:
-                    slot = (2 * PASSES - 1) * i if is_hot else REST * i + c + 1
-                half, slot = divmod(slot, PASSES)
+                call, at = divmod(place(m, i, c), PASSES)
                 nc.tensor.matmul_mx(
                     out=acc[s][:],
-                    lhsT=dy_codes[2 * m + half][:, P * slot : P * (slot + 1)].bitcast(FP8X4),
-                    lhsT_scale=dy_code_scales[2 * m + half][:, P * slot : P * (slot + 1)],
-                    rhs=b_hot_codes[:].bitcast(FP8X4) if is_hot else b_words_sb[:, c, :].bitcast(FP4X4),
-                    rhs_scale=b_hot_scales[:] if is_hot else b_scales_sb[:, c, :],
+                    lhsT=dy_codes[m, call][:, P * at : P * (at + 1)].bitcast(FP8X4),
+                    lhsT_scale=dy_scales[m, call][:, P * at : P * (at + 1)],
+                    rhs=b_hot_codes[:].bitcast(FP8X4) if c == HOT else b_words_sb[:, c, :].bitcast(FP4X4),
+                    rhs_scale=b_hot_scales[:] if c == HOT else b_scales_sb[:, c, :],
                     start=(c == 0),
-                    stop=is_hot,
+                    stop=(c == HOT),
                 )
 
         def weigh_tokens(s):
-            g, t = divmod(s, PHASES)
+            g, t = divmod(s, PACK)
             if t == 0:
-                sums[g] = work.tile([P, PHASES, R], F32, name="sums", align_bytes=64, bufs=2)
+                sums[g] = work.tile([P, PACK, R], F32, name="sums", align_bytes=64, bufs=2)
             nc.scalar.activation(out=sums[g][:, t, :], in_=acc[s][:], func=COPY, scale=token_weight[:, s : s + 1])
             release(("acc", s))
 
         def weigh_ranks(g, h, dst):
             ranks = slice(HALF * h, HALF * (h + 1))
+            factors = lam_all[:, ranks].rearrange("p (c i) -> p c i", i=4).unsqueeze(2)
             nc.gpsimd.tensor_tensor(
-                out=dst.rearrange("p (c i t) -> p c t i", i=4, t=PHASES),
+                out=dst.rearrange("p (c i t) -> p c t i", i=4, t=PACK),
                 in0=sums[g][:, :, ranks].rearrange("p t (c i) -> p c t i", i=4),
-                in1=lam_all[:, ranks].rearrange("p (c i) -> p c i", i=4).unsqueeze(2).to_broadcast([P, HALF // 4, PHASES, 4]),
+                in1=factors.to_broadcast([P, HALF // 4, PACK, 4]),
                 op=MULT,
+            )
+
+        def weigh_both(s):
+            nc.vector.scalar_tensor_tensor(
+                out=last_tiles[:, s % PACK, :],
+                in0=acc[s][:],
+                scalar=token_weight[:, s : s + 1],
+                in1=lam_all[:],
+                op0=MULT,
+                op1=MULT,
+            )
+            release(("acc", s))
+
+        def interleave_last(copy, r0, r1):
+            copy(
+                out=interleaved[:, PACK * r0 : PACK * r1].rearrange("p (c i t) -> p c t i", i=4, t=PACK),
+                in_=last_tiles[:, :, r0:r1].rearrange("p t (c i) -> p c t i", i=4),
             )
 
         def quantise_g(g, h, src):
             ranks = slice(HALF * h, HALF * (h + 1))
             nc.vector.quantize_mx(out=g_codes[g][:, ranks].bitcast(FP8X4), scales=g_scales[g][:, ranks], in_=src)
 
-        def weigh_last(s):
-            nc.vector.scalar_tensor_tensor(
-                out=last_planes[:, s % PHASES, :], in0=acc[s][:], scalar=token_weight[:, s : s + 1], in1=lam_all[:], op0=MULT, op1=MULT
-            )
-            release(("acc", s))
+        held = {}
+        added = {}
+        parked = {}
+        result = {}
+        pending = []
 
-        def interleave_last(copy, r0, r1):
-            copy(
-                out=b_grouped[:, PHASES * r0 : PHASES * r1].rearrange("p (c i t) -> p c t i", i=4, t=PHASES),
-                in_=last_planes[:, :, r0:r1].rearrange("p t (c i) -> p c t i", i=4),
-            )
-
-        def just_read(m, i):
-            return grouped[m][:, PASSES + 2 * i : PASSES + 2 * (i + 1), :].rearrange("p c k -> p (c k)")
-
-        def stage2(bank, d, g0, g1, first, final):
-            for g in range(g0, g1):
+        def stage2(bank, d, groups, first, final):
+            for g in groups:
                 nc.tensor.matmul_mx(
                     out=bank[:],
                     lhsT=x_words_sb[g][:, 2 * P * d : 2 * P * (d + 1)].bitcast(FP4X4),
@@ -319,24 +310,18 @@ def tile_lora_down_gradient_s3_kernel(
                     stop=(g == final),
                 )
 
-        held = {}
-        added = {}
-        parked = {}
-        result = {}
-        pending = []
-
         def hold(d, upto):
             if d not in held:
                 held[d] = take(("held", d), [P, R])
                 added[d] = 0
-            stage2(held[d], d, added[d], upto, 0, GROUPS - 1)
+            stage2(held[d], d, range(added[d], upto), 0, LAST)
             added[d] = upto
 
-        def park(count):
+        def park(upto):
             d = OUT_TILES - 1 - len(parked)
             bank = take(("early", d), [P, R])
-            stage2(bank, d, 0, count, 0, count - 1)
-            parked[d] = count
+            stage2(bank, d, range(upto), 0, upto - 1)
+            parked[d] = upto
             pending.append((d, bank))
 
         def empty_parked():
@@ -346,15 +331,16 @@ def tile_lora_down_gradient_s3_kernel(
                 nc.scalar.copy(out=result[d][:], in_=bank[:])
                 release(("early", d))
 
-        widened[0] = work.tile([P, 2 * C], BF16, name="widened", align_bytes=64, bufs=3)
+        nc.vector.tensor_copy(out=channel_scale[:, REST, :], in_=channel_scale[:, 0, :])
+        widened[0] = work.tile([P, 2 * C], BF16, name="widened", align_bytes=64)
         nc.scalar.copy(out=widened[0][:, 0:K_PASS], in_=first_bytes[:].bitcast(FP8))
         nc.scalar.copy(out=widened[0][:, K_PASS:BANK], in_=other_bytes[:, 0:K_PASS].bitcast(FP8))
         nc.scalar.copy(out=widened[0][:, BANK:C], in_=other_bytes[:, K_PASS:].bitcast(FP8))
-        nc.scalar.copy(out=widened[0][:, C : 2 * BANK], in_=second_tile[:, 0:K_PASS].bitcast(FP8))
-        nc.scalar.copy(out=widened[0][:, 2 * BANK :], in_=second_tile[:, K_PASS:].bitcast(FP8))
+        nc.scalar.copy(out=widened[0][:, C : 2 * BANK], in_=second_bytes[:, 0:K_PASS].bitcast(FP8))
+        nc.scalar.copy(out=widened[0][:, 2 * BANK :], in_=second_bytes[:, K_PASS:].bitcast(FP8))
         nc.gpsimd.tensor_scalar(
-            out=b_grouped[:, 0 : PACK * B_CUT].rearrange("p (n t) -> p n t", t=PACK),
-            in0=b_raw[:, :, 0:B_CUT].rearrange("p t n -> p n t"),
+            out=interleaved[:].rearrange("p (n t) -> p n t", t=PACK),
+            in0=b_raw[:].rearrange("p t n -> p n t"),
             scalar1=1.0,
             scalar2=0.0,
             op0=MULT,
@@ -362,18 +348,15 @@ def tile_lora_down_gradient_s3_kernel(
         )
         turn(0, 0)
         turn(0, 1)
-        lam_bank = take(("lam", 0), [P, R])
+        lam_bank = take(("lam",), [P, R])
         nc.tensor.matmul(lam_bank[:], lhsT=ones[:], rhs=lam_row[:], start=True, stop=True)
         turn(0, 2)
+        spreading = [take(("spreading", c), [P, PACK, P]) for c in range(2)]
         for c in range(2):
-            spread_scales(c)
+            for t in range(PACK):
+                nc.tensor.transpose(spreading[c][:, t, :], channel_scale[:, c, t : t + 1].to_broadcast([P, P]), ident[:])
         nc.scalar.copy(out=lam_all[:], in_=lam_bank[:])
-        release(("lam", 0))
-        if B_CUT < R:
-            nc.scalar.copy(
-                out=b_grouped[:, PACK * B_CUT :].rearrange("p (c i t) -> p c t i", i=4, t=PACK),
-                in_=b_raw[:, :, B_CUT:].rearrange("p t (c i) -> p c t i", i=4),
-            )
+        release(("lam",))
         for j in range(REST):
             widen(1, j, j + 1)
         turn(0, HOT)
@@ -385,150 +368,112 @@ def tile_lora_down_gradient_s3_kernel(
         for j in range(REST):
             turn(1, j)
         for c in range(2):
-            empty_spread(c)
-        quantise_dy(0)
-        nc.vector.quantize_mx(out=b_hot_codes[:].bitcast(FP8X4), scales=b_hot_scales[:], in_=b_grouped[:])
-        quantise_dy(1)
+            nc.scalar.copy(out=spread[:, :, c, :, :], in_=spreading[c][:].rearrange("p (u e) n -> p u n e", u=2))
+            release(("spreading", c))
+        quantise_dy(0, 0)
+        nc.vector.quantize_mx(out=b_hot_codes[:].bitcast(FP8X4), scales=b_hot_scales[:], in_=interleaved[:])
+        quantise_dy(0, 1)
         widen(2, 0, 1)
 
-        last = GROUPS - 1
-        ready = 0
-        jobs = []
-        for n in range(3, PAIRS):
-            jobs.extend(("widen", n, j) for j in range(REST))
-            jobs.extend(("sort", n, j) for j in SORTS.get(n, ()))
+        jobs = [lambda m=m, j=j: widen(m, j, j + 1) for m in range(3, PAIRS) for j in range(REST)]
+        jobs.extend(lambda j=j: sort_words(PAIRS - 1, j, nc.scalar.copy) for j in (HOT, 0, 1, 2))
 
         def spare(count):
-            for i in range(min(count, len(jobs))):
-                kind, n, j = jobs.pop(0)
-                if kind == "widen":
-                    widen(n, j, j + 1)
-                else:
-                    assert (n, j) not in banks
-                    sort_words(n, j, nc.scalar.copy)
+            for i in range(count):
+                jobs.pop(0)()
 
+        ready = 0
         for m in range(1, PAIRS):
-            mine = [j for j in range(REST) if not (j == 0 and m in ON_GPSIMD)]
-            ahead = [j for j in range(REST) if not (j == 0 and m + 1 in ON_GPSIMD)] if m + 1 < PAIRS else []
-            g, h = divmod(m - 3, 2)
-            before, after = PARKS.get(m, (0, 0))
-            if m in VSORT:
-                sort_words(*VSORT[m], nc.vector.tensor_copy)
+            final_step = m + 1 == PAIRS
+            mine = range(1 if m in ON_GPSIMD else 0, REST)
+            g, h = divmod(m - FIRST_LAM_STEP, 2)
+            if m in ON_GPSIMD:
+                sort_words(m + 1, HOT, nc.vector.tensor_copy)
             if m + 1 in ON_GPSIMD:
-                scale_first(m + 1, just_read(m - 1, 0))
-            if m >= 3:
-                weigh_ranks(g, h, just_read(m - 1, 0))
-            for i, (pair, j) in enumerate(GSORTS.get(m, ())):
-                if m < 3 and i == 0 and m + 1 not in ON_GPSIMD:
-                    sort_into(pair, j, just_read(m - 1, 0))
-                else:
-                    sort_words(pair, j, nc.gpsimd.tensor_copy)
+                scale_before_turning(m + 1, just_read(m - 1))
+            if m >= FIRST_LAM_STEP:
+                weigh_ranks(g, h, just_read(m - 1))
             if m == 1:
                 widen(2, 1, REST)
                 nc.scalar.copy(out=token_weight[:], in_=token_weight_bf[:])
-                stage1(0, range(REST))
-                stage1(1, range(REST))
-                stage1(0, (HOT,))
-                stage1(1, (HOT,))
+                for passes in (range(REST), (HOT,)):
+                    stage1(0, passes)
+                    stage1(1, passes)
             else:
                 stage1(2 * m - 2, range(PASSES))
                 stage1(2 * m - 1, range(PASSES))
             product(m, mine[0])
-            if ready > 0:
-                for d in range(HELD):
-                    hold(d, ready)
-                for i in range(before):
-                    park(ready)
-            for j in mine[1:]:
+            if m >= FIRST_PARK_STEP:
+                park(ready)
+            product(m, mine[1])
+            if not final_step:
+                if m > 1:
+                    spare(1)
+                weigh_tokens(2 * m - 2)
+                weigh_tokens(2 * m - 1)
+            for j in mine[2:]:
                 product(m, j)
-            if m + 1 < PAIRS:
-                for i in range(2):
-                    spare(SLOTS[m][i])
-                    weigh_tokens(2 * m - 2 + i)
             empty_parked()
-            if m + 1 < PAIRS:
+            if not final_step:
                 turn(m + 1, HOT)
-                for j in ahead[:2]:
+                for j in range(1 if m + 1 in ON_GPSIMD else 0, REST):
                     turn(m + 1, j)
                 move(m + 1, HOT)
-            for j in ahead[2:]:
-                turn(m + 1, j)
-            if m + 1 < PAIRS:
-                spare(SLOTS[m][2])
-            if m + 1 in ON_GPSIMD:
-                turn(m + 1, 0)
-                move(m + 1, 0)
-            if m + 1 < PAIRS:
-                spare(SLOTS[m][3])
-            if m >= 3 and h == 1:
-                quantise_g(g, h, just_read(m - 1, 0))
+                behind = min(SPARE_JOBS, len(jobs) - (PAIRS - 2 - m > 0))
+                if m + 2 in ON_GPSIMD:
+                    spare(1)
+                    behind -= 1
+                if m + 1 in ON_GPSIMD:
+                    turn(m + 1, 0)
+                    move(m + 1, 0)
+                spare(behind)
+            if m >= FIRST_LAM_STEP and h == 1:
+                quantise_g(g, h, just_read(m - 1))
                 ready += 1
                 for d in range(HELD):
                     hold(d, ready)
-            for i in range(after):
-                park(ready)
-                empty_parked()
-            if m + 1 == PAIRS:
-                for d in range(HELD, HELD + LAST_HOLD):
-                    hold(d, ready)
-            quantise_dy(2 * m)
-            quantise_dy(2 * m + 1)
-            if m >= 3 and h == 0:
-                quantise_g(g, h, just_read(m - 1, 0))
+            if m >= FIRST_PARK_STEP:
+                for i in range(1 if final_step else 2):
+                    park(ready)
+                    empty_parked()
+            if final_step:
+                hold(HELD, ready)
+            quantise_dy(m, 0)
+            quantise_dy(m, 1)
+            if m >= FIRST_LAM_STEP and h == 0:
+                quantise_g(g, h, just_read(m - 1))
 
-        assert not jobs
-        weigh_ranks(last - 1, 1, just_read(PAIRS - 1, 0))
-        for s in (TILES - 2, TILES - 1):
-            stage1(s, range(PASSES))
-        weigh_last(TILES - 4)
-        weigh_last(TILES - 3)
+        weigh_ranks(LAST - 1, 1, just_read(PAIRS - 1))
+        stage1(TILES - 2, range(PASSES))
+        stage1(TILES - 1, range(PASSES))
+        weigh_both(TILES - 4)
+        weigh_both(TILES - 3)
         while free:
-            hold(len(held), last - 1)
-        weigh_last(TILES - 2)
-        weigh_last(TILES - 1)
-        quantise_g(last - 1, 1, just_read(PAIRS - 1, 0))
-        for d in range(EARLY):
-            hold(d, last)
+            hold(len(held), ready)
+        weigh_both(TILES - 2)
+        weigh_both(TILES - 1)
+        quantise_g(LAST - 1, 1, just_read(PAIRS - 1))
         interleave_last(nc.scalar.copy, R - SCALAR_RANKS, R)
         interleave_last(nc.vector.tensor_copy, 0, HALF)
         interleave_last(nc.vector.tensor_copy, HALF, R - SCALAR_RANKS)
+        for d in range(AHEAD_OF_LAST):
+            hold(d, LAST)
         for h in range(2):
-            quantise_g(last, h, b_grouped[:, PHASES * HALF * h : PHASES * HALF * (h + 1)])
+            quantise_g(LAST, h, interleaved[:, PACK * HALF * h : PACK * HALF * (h + 1)])
 
-        plain = [d for d in range(len(held), OUT_TILES) if d not in parked]
-        order = list(parked) + plain
-        if TURNS:
-            order = [d for both in zip(parked, plain) for d in both] + list(parked)[len(plain) :] + plain[len(parked) :]
-        for d in list(held) + order:
-            if SPLIT and d == order[-1]:
-                for h, copy in enumerate((nc.scalar.copy, nc.vector.tensor_copy)):
-                    ranks = slice(HALF * h, HALF * (h + 1))
-                    bank = take(("end", h), [P, HALF])
-                    for g in range(GROUPS):
-                        nc.tensor.matmul_mx(
-                            out=bank[:],
-                            lhsT=x_words_sb[g][:, 2 * P * d : 2 * P * (d + 1)].bitcast(FP4X4),
-                            lhsT_scale=x_scales_sb[:, g, P * d : P * (d + 1)],
-                            rhs=g_codes[g][:, ranks].bitcast(FP8X4),
-                            rhs_scale=g_scales[g][:, ranks],
-                            start=(g == 0),
-                            stop=(g == last),
-                        )
-                    part = work.tile([P, HALF], F32, name="end", align_bytes=64, bufs=2)
-                    copy(out=part[:], in_=bank[:])
-                    nc.sync.dma_start(out=out[P * d : P * (d + 1), ranks], in_=part[:])
-                continue
+        for d in list(held) + list(range(OUT_TILES - 1, len(held) - 1, -1)):
             if d in held:
                 hold(d, GROUPS)
                 bank, key = held[d], ("held", d)
             else:
                 key = ("late", d)
                 bank = take(key, [P, R])
-                stage2(bank, d, parked.get(d, 0), GROUPS, parked.get(d, 0), last)
+                stage2(bank, d, range(parked.get(d, 0), GROUPS), parked.get(d, 0), LAST)
             if d in parked:
                 nc.vector.tensor_tensor(out=result[d][:], in0=bank[:], in1=result[d][:], op=ADD)
             else:
                 result[d] = work.tile([P, R], F32, name="result", align_bytes=64, bufs=8)
-                (nc.scalar.copy, nc.vector.tensor_copy)[d % 2 if d in held else 0](out=result[d][:], in_=bank[:])
+                copy = nc.vector.tensor_copy if d in held and d % 2 else nc.scalar.copy
+                copy(out=result[d][:], in_=bank[:])
             release(key)
             nc.sync.dma_start(out=out[P * d : P * (d + 1), :], in_=result[d][:])

@@ -38,7 +38,7 @@ HELD = 2
 SPARE_JOBS = 3
 FIRST_PARK_STEP = 5
 AHEAD_OF_LAST = 5
-SCALAR_RANKS = 128
+SCALAR_RANKS = 160
 
 
 def tile_lora_down_gradient_s3_kernel(
@@ -110,11 +110,11 @@ def tile_lora_down_gradient_s3_kernel(
         second_bytes = keep.tile([P, C], U8, name="second_bytes", align_bytes=64)
         nc.sync.dma_start(out=first_bytes[:], in_=bytes_hbm[0][:, 0:K_PASS])
         nc.sync.dma_start(out=other_bytes[:], in_=bytes_hbm[0][:, K_PASS:C])
-        nc.sync.dma_start(out=lam_row[0:1, :], in_=lam.rearrange("(o r) -> o r", o=1))
         nc.sync.dma_start(out=second_bytes[:], in_=bytes_hbm[0][:, C : 2 * C])
         nc.sync.dma_start(
             out=channel_scale[:, 0:REST, :], in_=dy_rest_scale.rearrange("o (c p t) -> p (o c) t", p=P, t=PACK)
         )
+        nc.sync.dma_start(out=lam_row[0:1, :], in_=lam.rearrange("(o r) -> o r", o=1))
         nc.sync.dma_start(out=b_raw[:], in_=b_hot.rearrange("(p t) n -> p t n", t=PACK))
         load_bytes(1)
         load_hot(0, 1)

from contextlib import ExitStack

import concourse.mybir as mybir
from concourse.masks import make_identity

T, H, C, R, D = 2048, 512, 1536, 512, 2560
FLOPS = 2 * T * (H + C) * R + 2 * D * T * R

F32 = mybir.dt.float32
BF16 = mybir.dt.bfloat16
I32 = mybir.dt.int32
U32 = mybir.dt.uint32
U8 = mybir.dt.uint8
FP8 = mybir.dt.float8_e4m3fn
FP8X4 = mybir.dt.float8_e4m3fn_x4
FP4X4 = mybir.dt.float4_e2m1fn_x4
MULT = mybir.AluOpType.mult
ADD = mybir.AluOpType.add
COPY = mybir.ActivationFunctionType.Copy

P = 128
PACK = 4
K_PASS = P * PACK
GROUPS = T // K_PASS
TILES = GROUPS * PACK
PAIRS = TILES // 2
REST = C // K_PASS
PASSES = REST + 1
HOT = REST
BANK = 2 * K_PASS
OUT_TILES = D // P
HALF = R // 2
LAST = GROUPS - 1

FIRST_LAM_STEP = 3
ON_GPSIMD = range(2, FIRST_LAM_STEP + 1)
HELD = 2
SPARE_JOBS = 3
FIRST_PARK_STEP = 5
AHEAD_OF_LAST = 5
SCALAR_RANKS = 160


def tile_lora_down_gradient_s3_kernel(
    tc, dy_hot, b_hot, dy_rest_bytes, dy_rest_scale, b_rest_words, b_rest_scales, lam, token_w, x_words, x_scales, out
):
    nc = tc.nc

    with ExitStack() as ctx:
        keep = ctx.enter_context(tc.tile_pool(name="keep", bufs=1))
        work = ctx.enter_context(tc.tile_pool(name="work", bufs=3))
        psum = ctx.enter_context(tc.psum_pool(name="psum", bufs=1))
        ctx.enter_context(tc.manual_schedule())

        ident = keep.tile([P, P], F32, name="ident")
        token_weight_bf = keep.tile([P, TILES], BF16, name="token_weight_bf", align_bytes=64)
        token_weight = keep.tile([P, TILES], F32, name="token_weight", align_bytes=64)
        lam_all = keep.tile([P, R], BF16, name="lam_all", align_bytes=64)
        channel_scale = keep.tile([P, REST + 1, PACK], F32, name="channel_scale", align_bytes=64)
        b_raw = keep.tile([P, PACK, R], BF16, name="b_raw", align_bytes=64)
        interleaved = keep.tile([P, R * PACK], BF16, name="interleaved", align_bytes=64)
        b_hot_codes = keep.tile([P, R], U32, name="b_hot_codes", align_bytes=64)
        b_hot_scales = keep.tile([P, R], U8, name="b_hot_scales", align_bytes=64)
        b_words_sb = keep.tile([P, REST, 2 * R], U8, name="b_words_sb", align_bytes=64)
        b_scales_sb = keep.tile([P, REST, R], U8, name="b_scales_sb", align_bytes=64)
        x_words_sb = [keep.tile([P, 2 * D], U8, name="x_words_%d" % g, align_bytes=64) for g in range(GROUPS)]
        x_scales_sb = keep.tile([P, GROUPS, D], U8, name="x_scales_sb", align_bytes=64)
        g_codes = [keep.tile([P, R], U32, name="g_codes_%d" % g, align_bytes=64) for g in range(GROUPS)]
        g_scales = [keep.tile([P, R], U8, name="g_scales_%d" % g, align_bytes=64) for g in range(GROUPS)]
        last_tiles = keep.tile([P, PACK, R], BF16, name="last_tiles", align_bytes=64)
        spread = keep.tile([P, 2, 2, P, 2], F32, name="spread", align_bytes=64)
        lam_row = keep.tile([P, R], BF16, name="lam_row", align_bytes=64)
        ones = keep.tile([P, P], BF16, name="ones", align_bytes=64)

        nc.vector.memset(lam_row[:], 0.0)
        nc.vector.memset(ones[:], 1.0)
        nc.vector.memset(b_scales_sb[:].rearrange("p c n -> p (c n)").bitcast(I32), 0)
        nc.vector.memset(x_scales_sb[:].rearrange("p g n -> p (g n)").bitcast(I32), 0)
        make_identity(nc, ident[:])

        bytes_hbm = dy_rest_bytes.rearrange("(g m t) k -> g m (t k)", m=P, t=PACK)
        hot_hbm = dy_hot.rearrange("(g m t) k -> g m (t k)", m=P, t=PACK)
        pair_bytes = {}
        hot = {}

        def load_bytes(m):
            g, t = divmod(2 * m, PACK)
            pair_bytes[m] = keep.tile([P, 2 * C], U8, name="rest_bytes_%d" % m, align_bytes=64)
            nc.sync.dma_start(out=pair_bytes[m][:], in_=bytes_hbm[g][:, t * C : (t + 2) * C])

        def load_hot(m, count):
            g, t = divmod(2 * m, PACK)
            tile = keep.tile([P, count * BANK], BF16, name="hot_%d" % m, align_bytes=64)
            nc.sync.dma_start(out=tile[:], in_=hot_hbm[g][:, t * H : (t + 2 * count) * H])
            for i in range(count):
                hot[m + i] = tile[:, BANK * i : BANK * (i + 1)]

        def load_scale_rows(tile, hbm):
            for q in range(4):
                nc.sync.dma_start(
                    out=tile[32 * q : 32 * q + 4, :, :].bitcast(I32),
                    in_=hbm[:, 4 * q : 4 * q + 4, :].rearrange("g q n -> q g n").bitcast(I32),
                )

        def load_x(g):
            nc.sync.dma_start(out=x_words_sb[g][:].bitcast(I32), in_=x_words[g].bitcast(I32))

        first_bytes = keep.tile([P, K_PASS], U8, name="first_bytes", align_bytes=64)
        other_bytes = keep.tile([P, C - K_PASS], U8, name="other_bytes", align_bytes=64)
        second_bytes = keep.tile([P, C], U8, name="second_bytes", align_bytes=64)
        nc.sync.dma_start(out=first_bytes[:], in_=bytes_hbm[0][:, 0:K_PASS])
        nc.sync.dma_start(out=other_bytes[:], in_=bytes_hbm[0][:, K_PASS:C])
        nc.sync.dma_start(out=second_bytes[:], in_=bytes_hbm[0][:, C : 2 * C])
        nc.sync.dma_start(
            out=channel_scale[:, 0:REST, :], in_=dy_rest_scale.rearrange("o (c p t) -> p (o c) t", p=P, t=PACK)
        )
        nc.sync.dma_start(out=lam_row[0:1, :], in_=lam.rearrange("(o r) -> o r", o=1))
        nc.sync.dma_start(out=b_raw[:], in_=b_hot.rearrange("(p t) n -> p t n", t=PACK))
        load_bytes(1)
        load_hot(0, 1)
        load_hot(1, 1)
        nc.sync.dma_start(out=b_words_sb[:].bitcast(I32), in_=b_rest_words.rearrange("c p b -> p c b").bitcast(I32))
        load_scale_rows(b_scales_sb, b_rest_scales)
        load_bytes(2)
        nc.sync.dma_start(
            out=token_weight_bf[:].rearrange("m (g t) -> m g t", t=PACK),
            in_=token_w.rearrange("(g m t) -> m g t", m=P, t=PACK),
        )
        load_hot(2, 1)
        load_bytes(3)
        load_hot(3, 1)
        load_bytes(4)
        load_hot(4, 2)
        load_bytes(5)
        load_bytes(6)
        load_scale_rows(x_scales_sb, x_scales)
        load_x(0)
        load_bytes(7)
        load_hot(6, 2)
        for g in range(1, GROUPS):
            load_x(g)

        free = ["bank_%d" % i for i in range(8)]
        tag_of = {}

        def take(key, shape):
            tag_of[key] = free.pop(0)
            return psum.tile(shape, F32, name=key[0], tag=tag_of[key])

        def release(key):
            free.append(tag_of[key])

        widened = {}
        sorted_words = {}
        turned = {}
        grouped = {}
        dy_codes = {}
        dy_scales = {}

        def widen(m, j0, j1):
            if j0 == 0:
                widened[m] = work.tile([P, 2 * C], BF16, name="widened", align_bytes=64)
            cols = slice(BANK * j0, BANK * j1)
            nc.scalar.copy(out=widened[m][:, cols], in_=pair_bytes[m][:, cols].bitcast(FP8))

        def values(m, j):
            return hot[m] if j == HOT else widened[m][:, BANK * j : BANK * (j + 1)]

        def sort_words(m, j, copy):
            tile = work.tile([P, K_PASS], F32, name="sorted_words", align_bytes=64, bufs=6)
            copy(
                out=tile[:].rearrange("p (u n) -> p u n", u=2),
                in_=values(m, j).bitcast(F32).rearrange("p (n u) -> p u n", u=2),
            )
            sorted_words[m, j] = tile[:]

        def scale_before_turning(m, dst):
            nc.gpsimd.tensor_tensor(
                out=dst.rearrange("p (u n e) -> p u n e", u=2, e=2),
                in0=values(m, 0).rearrange("p (n u e) -> p u n e", u=2, e=2),
                in1=spread[:].rearrange("p u c n e -> p u (c n) e"),
                op=MULT,
            )
            sorted_words[m, 0] = dst.bitcast(F32)

        def turn(m, j):
            turned[m, j] = take(("turned", m, j), [P, 2, 2, P])
            for c in range(2):
                for u in range(2):
                    if (m, j) in sorted_words:
                        words = sorted_words[m, j][:, P * (2 * u + c) : P * (2 * u + c + 1)]
                    else:
                        words = values(m, j).bitcast(F32)[:, 2 * P * c + u : 2 * P * (c + 1) : 2]
                    nc.tensor.transpose(turned[m, j][:, u, c, :], words, ident[:])

        def place(m, i, c):
            if m == 0:
                return 2 * REST + i if c == HOT else REST * i + c
            return (2 * PASSES - 1) * i if c == HOT else REST * i + c + 1

        def places(m, j):
            if m not in grouped:
                grouped[m] = work.tile([P, 2 * PASSES, K_PASS], BF16, name="grouped", align_bytes=64, bufs=4)
            a, b = (place(m, 0, HOT), place(m, 1, HOT)) if j == HOT else (place(m, 0, 0) + 2 * j, place(m, 0, 0) + 2 * j + 1)
            return grouped[m][:, a : b + 1 : b - a, :]

        def move(m, j):
            nc.scalar.copy(
                out=places(m, j).bitcast(F32).rearrange("p c (n u) -> p c n u", u=2),
                in_=turned[m, j][:].rearrange("p u c n -> p c n u"),
            )
            release(("turned", m, j))

        def product(m, j):
            c0 = 2 * j % REST
            halves = turned[m, j][:].rearrange("p u c n -> p (u c n)").bitcast(BF16)
            scales = channel_scale[:, c0 : c0 + 2, :].unsqueeze(2).to_broadcast([P, 2, P, PACK])
            nc.vector.tensor_tensor(
                out=places(m, j).rearrange("p c (n u e) -> p c n u e", u=2, e=2),
                in0=halves.rearrange("p (u c n e) -> p c n u e", u=2, c=2, e=2),
                in1=scales.rearrange("p c n (u e) -> p c n u e", u=2),
                op=MULT,
            )
            release(("turned", m, j))

        def quantise_dy(m, i):
            dy_codes[m, i] = work.tile([P, PASSES * P], U32, name="dy_codes", align_bytes=64, bufs=4)
            dy_scales[m, i] = work.tile([P, PASSES * P], U8, name="dy_scales", align_bytes=64, bufs=4)
            nc.vector.quantize_mx(
                out=dy_codes[m, i][:].bitcast(FP8X4),
                scales=dy_scales[m, i][:],
                in_=grouped[m][:, PASSES * i : PASSES * (i + 1), :].rearrange("p c k -> p (c k)"),
            )

        def just_read(m):
            return grouped[m][:, PASSES : PASSES + 2, :].rearrange("p c k -> p (c k)")

        acc = {}
        sums = {}

        def stage1(s, passes):
            m, i = divmod(s, 2)
            if 0 in passes:
                acc[s] = take(("acc", s), [P, R])
            for c in passes:
                call, at = divmod(place(m, i, c), PASSES)
                nc.tensor.matmul_mx(
                    out=acc[s][:],
                    lhsT=dy_codes[m, call][:, P * at : P * (at + 1)].bitcast(FP8X4),
                    lhsT_scale=dy_scales[m, call][:, P * at : P * (at + 1)],
                    rhs=b_hot_codes[:].bitcast(FP8X4) if c == HOT else b_words_sb[:, c, :].bitcast(FP4X4),
                    rhs_scale=b_hot_scales[:] if c == HOT else b_scales_sb[:, c, :],
                    start=(c == 0),
                    stop=(c == HOT),
                )

        def weigh_tokens(s):
            g, t = divmod(s, PACK)
            if t == 0:
                sums[g] = work.tile([P, PACK, R], F32, name="sums", align_bytes=64, bufs=2)
            nc.scalar.activation(out=sums[g][:, t, :], in_=acc[s][:], func=COPY, scale=token_weight[:, s : s + 1])
            release(("acc", s))

        def weigh_ranks(g, h, dst):
            ranks = slice(HALF * h, HALF * (h + 1))
            factors = lam_all[:, ranks].rearrange("p (c i) -> p c i", i=4).unsqueeze(2)
            nc.gpsimd.tensor_tensor(
                out=dst.rearrange("p (c i t) -> p c t i", i=4, t=PACK),
                in0=sums[g][:, :, ranks].rearrange("p t (c i) -> p c t i", i=4),
                in1=factors.to_broadcast([P, HALF // 4, PACK, 4]),
                op=MULT,
            )

        def weigh_both(s):
            nc.vector.scalar_tensor_tensor(
                out=last_tiles[:, s % PACK, :],
                in0=acc[s][:],
                scalar=token_weight[:, s : s + 1],
                in1=lam_all[:],
                op0=MULT,
                op1=MULT,
            )
            release(("acc", s))

        def interleave_last(copy, r0, r1):
            copy(
                out=interleaved[:, PACK * r0 : PACK * r1].rearrange("p (c i t) -> p c t i", i=4, t=PACK),
                in_=last_tiles[:, :, r0:r1].rearrange("p t (c i) -> p c t i", i=4),
            )

        def quantise_g(g, h, src):
            ranks = slice(HALF * h, HALF * (h + 1))
            nc.vector.quantize_mx(out=g_codes[g][:, ranks].bitcast(FP8X4), scales=g_scales[g][:, ranks], in_=src)

        held = {}
        added = {}
        parked = {}
        result = {}
        pending = []

        def stage2(bank, d, groups, first, final):
            for g in groups:
                nc.tensor.matmul_mx(
                    out=bank[:],
                    lhsT=x_words_sb[g][:, 2 * P * d : 2 * P * (d + 1)].bitcast(FP4X4),
                    lhsT_scale=x_scales_sb[:, g, P * d : P * (d + 1)],
                    rhs=g_codes[g][:].bitcast(FP8X4),
                    rhs_scale=g_scales[g][:],
                    start=(g == first),
                    stop=(g == final),
                )

        def hold(d, upto):
            if d not in held:
                held[d] = take(("held", d), [P, R])
                added[d] = 0
            stage2(held[d], d, range(added[d], upto), 0, LAST)
            added[d] = upto

        def park(upto):
            d = OUT_TILES - 1 - len(parked)
            bank = take(("early", d), [P, R])
            stage2(bank, d, range(upto), 0, upto - 1)
            parked[d] = upto
            pending.append((d, bank))

        def empty_parked():
            while pending:
                d, bank = pending.pop(0)
                result[d] = keep.tile([P, R], F32, name="parked_%d" % d, align_bytes=64)
                nc.scalar.copy(out=result[d][:], in_=bank[:])
                release(("early", d))

        nc.vector.tensor_copy(out=channel_scale[:, REST, :], in_=channel_scale[:, 0, :])
        widened[0] = work.tile([P, 2 * C], BF16, name="widened", align_bytes=64)
        nc.scalar.copy(out=widened[0][:, 0:K_PASS], in_=first_bytes[:].bitcast(FP8))
        nc.scalar.copy(out=widened[0][:, K_PASS:BANK], in_=other_bytes[:, 0:K_PASS].bitcast(FP8))
        nc.scalar.copy(out=widened[0][:, BANK:C], in_=other_bytes[:, K_PASS:].bitcast(FP8))
        nc.scalar.copy(out=widened[0][:, C : 2 * BANK], in_=second_bytes[:, 0:K_PASS].bitcast(FP8))
        nc.scalar.copy(out=widened[0][:, 2 * BANK :], in_=second_bytes[:, K_PASS:].bitcast(FP8))
        nc.gpsimd.tensor_scalar(
            out=interleaved[:].rearrange("p (n t) -> p n t", t=PACK),
            in0=b_raw[:].rearrange("p t n -> p n t"),
            scalar1=1.0,
            scalar2=0.0,
            op0=MULT,
            op1=ADD,
        )
        turn(0, 0)
        turn(0, 1)
        lam_bank = take(("lam",), [P, R])
        nc.tensor.matmul(lam_bank[:], lhsT=ones[:], rhs=lam_row[:], start=True, stop=True)
        turn(0, 2)
        spreading = [take(("spreading", c), [P, PACK, P]) for c in range(2)]
        for c in range(2):
            for t in range(PACK):
                nc.tensor.transpose(spreading[c][:, t, :], channel_scale[:, c, t : t + 1].to_broadcast([P, P]), ident[:])
        nc.scalar.copy(out=lam_all[:], in_=lam_bank[:])
        release(("lam",))
        for j in range(REST):
            widen(1, j, j + 1)
        turn(0, HOT)
        turn(1, HOT)
        for j in range(REST):
            product(0, j)
        move(0, HOT)
        move(1, HOT)
        for j in range(REST):
            turn(1, j)
        for c in range(2):
            nc.scalar.copy(out=spread[:, :, c, :, :], in_=spreading[c][:].rearrange("p (u e) n -> p u n e", u=2))
            release(("spreading", c))
        quantise_dy(0, 0)
        nc.vector.quantize_mx(out=b_hot_codes[:].bitcast(FP8X4), scales=b_hot_scales[:], in_=interleaved[:])
        quantise_dy(0, 1)
        widen(2, 0, 1)

        jobs = [lambda m=m, j=j: widen(m, j, j + 1) for m in range(3, PAIRS) for j in range(REST)]
        jobs.extend(lambda j=j: sort_words(PAIRS - 1, j, nc.scalar.copy) for j in (HOT, 0, 1, 2))

        def spare(count):
            for i in range(count):
                jobs.pop(0)()

        ready = 0
        for m in range(1, PAIRS):
            final_step = m + 1 == PAIRS
            mine = range(1 if m in ON_GPSIMD else 0, REST)
            g, h = divmod(m - FIRST_LAM_STEP, 2)
            if m in ON_GPSIMD:
                sort_words(m + 1, HOT, nc.vector.tensor_copy)
            if m + 1 in ON_GPSIMD:
                scale_before_turning(m + 1, just_read(m - 1))
            if m >= FIRST_LAM_STEP:
                weigh_ranks(g, h, just_read(m - 1))
            if m == 1:
                widen(2, 1, REST)
                nc.scalar.copy(out=token_weight[:], in_=token_weight_bf[:])
                for passes in (range(REST), (HOT,)):
                    stage1(0, passes)
                    stage1(1, passes)
            else:
                stage1(2 * m - 2, range(PASSES))
                stage1(2 * m - 1, range(PASSES))
            product(m, mine[0])
            if m >= FIRST_PARK_STEP:
                park(ready)
            product(m, mine[1])
            if not final_step:
                if m > 1:
                    spare(1)
                weigh_tokens(2 * m - 2)
                weigh_tokens(2 * m - 1)
            for j in mine[2:]:
                product(m, j)
            empty_parked()
            if not final_step:
                turn(m + 1, HOT)
                for j in range(1 if m + 1 in ON_GPSIMD else 0, REST):
                    turn(m + 1, j)
                move(m + 1, HOT)
                behind = min(SPARE_JOBS, len(jobs) - (PAIRS - 2 - m > 0))
                if m + 2 in ON_GPSIMD:
                    spare(1)
                    behind -= 1
                if m + 1 in ON_GPSIMD:
                    turn(m + 1, 0)
                    move(m + 1, 0)
                spare(behind)
            if m >= FIRST_LAM_STEP and h == 1:
                quantise_g(g, h, just_read(m - 1))
                ready += 1
                for d in range(HELD):
                    hold(d, ready)
            if m >= FIRST_PARK_STEP:
                for i in range(1 if final_step else 2):
                    park(ready)
                    empty_parked()
            if final_step:
                hold(HELD, ready)
            quantise_dy(m, 0)
            quantise_dy(m, 1)
            if m >= FIRST_LAM_STEP and h == 0:
                quantise_g(g, h, just_read(m - 1))

        weigh_ranks(LAST - 1, 1, just_read(PAIRS - 1))
        stage1(TILES - 2, range(PASSES))
        stage1(TILES - 1, range(PASSES))
        weigh_both(TILES - 4)
        weigh_both(TILES - 3)
        while free:
            hold(len(held), ready)
        weigh_both(TILES - 2)
        weigh_both(TILES - 1)
        quantise_g(LAST - 1, 1, just_read(PAIRS - 1))
        interleave_last(nc.scalar.copy, R - SCALAR_RANKS, R)
        interleave_last(nc.vector.tensor_copy, 0, HALF)
        interleave_last(nc.vector.tensor_copy, HALF, R - SCALAR_RANKS)
        for d in range(AHEAD_OF_LAST):
            hold(d, LAST)
        for h in range(2):
            quantise_g(LAST, h, interleaved[:, PACK * HALF * h : PACK * HALF * (h + 1)])

        for d in list(held) + list(range(OUT_TILES - 1, len(held) - 1, -1)):
            if d in held:
                hold(d, GROUPS)
                bank, key = held[d], ("held", d)
            else:
                key = ("late", d)
                bank = take(key, [P, R])
                stage2(bank, d, range(parked.get(d, 0), GROUPS), parked.get(d, 0), LAST)
            if d in parked:
                nc.vector.tensor_tensor(out=result[d][:], in0=bank[:], in1=result[d][:], op=ADD)
            else:
                result[d] = work.tile([P, R], F32, name="result", align_bytes=64, bufs=8)
                copy = nc.vector.tensor_copy if d in held and d % 2 else nc.scalar.copy
                copy(out=result[d][:], in_=bank[:])
            release(key)
            nc.sync.dma_start(out=out[P * d : P * (d + 1), :], in_=result[d][:])
